import numpy as np, ml_dtypes
CORES = [9,25,41,57]
N = 4
BF = ml_dtypes.bfloat16
def gentries(a):
    return np.ascontiguousarray(a.reshape(8, 16, -1).transpose(0, 2, 1)).reshape(8, -1)
def gtable(e):
    e = np.asarray(e); return np.ascontiguousarray(e.reshape(8, -1, 16).transpose(0, 2, 1)).reshape(128, -1).astype(np.int32)
M, D, SD, Q, SQ, L, V = 256, 16, 8, 4, 10, 128, 6
W, P = M * D, M * Q
def unpack(x):
    x = np.ascontiguousarray(x.astype(np.int64).reshape(N, 8, 16, -1).transpose(0, 1, 3, 2)); return x >> 8, x & 255
def pick(x, i):
    return np.take_along_axis(x, i[..., None], 2)
def cut(lb, lm, pb, pm):
    o = np.argsort(np.concatenate([2 * lb, 2 * pb + 1], axis=-1), axis=-1, kind="stable")
    z = np.take_along_axis(np.concatenate([lb, pb], axis=-1), o, -1); lane = (o < 16).astype(np.int64)
    na = np.add.accumulate(lane, axis=-1) - 1; nb = np.maximum(np.add.accumulate(1 - lane, axis=-1) - 1, 0)
    ln = np.concatenate([z[..., 1:], np.full(z.shape[:-1] + (1,), 4096)], axis=-1) - z
    return z, ln, np.take_along_axis(lm, na, -1), np.take_along_axis(pm, nb, -1)
def weigh(tot, z, ln, a, b):
    ia = D * a + (z >> SD); ib = D * b + (z >> SD)
    sa = np.take_along_axis(tot, ia.reshape(N, 8, -1), 2).reshape(z.shape); sb = np.take_along_axis(tot, ib.reshape(N, 8, -1), 2).reshape(z.shape)
    w = ln * (sa + sb)
    return ia, ib, np.where(sb > sa, b, a), w, np.add.accumulate(w, axis=-1)
def remake(z, ln, den, vis, pb, pm):
    live = vis & (ln > 0)
    last = np.maximum.accumulate(np.where(live, np.arange(32), -1), axis=-1); e = last[..., -1:]
    zz = np.take_along_axis(z, e, -1); name = (Q * np.take_along_axis(den, e, -1) + (zz >> SQ))[..., 0]
    before = np.concatenate([np.full_like(e, -1), last[..., :-1]], axis=-1)
    new = live & ((before < 0) | (den != np.take_along_axis(den, np.maximum(before, 0), -1)))
    place = np.add.accumulate(new.astype(np.int64), axis=-1) - 1
    tb, tm = pick(pb, name), pick(pm, name); late = tb > zz
    tp = place[..., -1:] + np.add.accumulate(late.astype(np.int64), axis=-1)
    to = np.minimum(np.concatenate([np.where(new, place, 16), np.where(late, tp, 16)], axis=-1), 16)
    fb = np.full(z.shape[:-1] + (17,), 4095, np.int64); fm = np.zeros(fb.shape, np.int64)
    np.put_along_axis(fb, to, np.concatenate([z, tb], axis=-1), -1); np.put_along_axis(fm, to, np.concatenate([den, tm], axis=-1), -1)
    return fb[..., :16], fm[..., :16], name
def hand(fb, fm, name):
    return np.roll(fb, 1, axis=0), np.roll(fm, 1, axis=0), np.roll(name, (1, 1), axis=(0, 1))
def begins(rng, *shape):
    b = np.sort((4096 * rng.random(shape + (16,)) ** rng.choice(np.array([1, 1, 2, 3]), shape + (1,))).astype(np.int64), axis=-1); b[..., 0] = 0
    again = rng.random(b.shape) < 0.06; again[..., 0] = False
    b = np.where(again, np.concatenate([b[..., :1], b[..., :-1]], axis=-1), b)
    return np.where(rng.random(shape + (1,)) < 0.3, b & ~31, b)
def media(rng, *shape):
    m = rng.integers(0, M, shape + (16,)); same = rng.random(m.shape) < 0.15; same[..., 0] = False
    return np.where(same, np.concatenate([m[..., :1], m[..., :-1]], axis=-1), m)
def level(rng, t):
    return (t + (np.arange(16)[:, None] + rng.integers(0, 16, (N, 8, 1, W))) % 16) // 16
def paint(rng, share, own):
    return np.exp2(2 * (share * rng.random(own) + (1 - share) * rng.random((N, 8, 16, W))) - 1)
def parts(rng):
    lb, lm, pb, pm = begins(rng, N, 8, L), media(rng, N, 8, L), begins(rng, N, 8, P), media(rng, N, 8, P)
    sg = (rng.random((N, 8, 16, W)) * (rng.integers(1, 16, (N, 8, 1, W)) + 1)).astype(np.int64)
    co = paint(rng, 0.5, (N, 8, 16, 1)).reshape(N, 128, W).astype(np.float32).astype(BF)
    u = rng.random((N, 8, V, L)); om = np.where(rng.random(u.shape) < 0.5, np.exp2(12 + 9 * u), 1 + 2 ** 20 * u).astype(np.int64)
    return lb, lm, pb, pm, rng.integers(0, P, (N, 8, L)), sg, co, np.minimum(om, 2 ** 21)
def pack(lb, lm, pb, pm, fp, sg, co, om):
    ls, px = [np.ascontiguousarray((256 * b + m).transpose(0, 1, 3, 2).reshape(N, 128, -1)).astype(np.int32) for b, m in ((lb, lm), (pb, pm))]
    return {"sg": np.ascontiguousarray(sg.reshape(N, 128, W)).astype(np.float32).astype(BF), "co": co, "px": px, "ls": ls,
            "fp": np.stack([gtable(a) for a in fp]), "om": np.stack([gtable(a.reshape(8, -1)) for a in om])}
def plant(lb, lm, pb, pm, pn, sg, choose):
    tot = np.add.reduce(sg, axis=2); om = []
    for v in range(V):
        z, ln, a, b = cut(lb, lm, pick(pb, pn), pick(pm, pn)); ia, ib, den, w, cum = weigh(tot, z, ln, a, b)
        t = np.clip(choose(ln, w, cum), 1, 2 ** 21); om.append(t)
        lb, lm, pn = hand(*remake(z, ln, den, cum - w < t[..., None], pb, pm))
    return np.stack(om, axis=2)
def setup_inputs(rng):
    return pack(*parts(rng))
def setup_inputs_spread(rng):
    lb, lm, pb, pm, fp, sg, co, om = parts(rng)
    hi = np.minimum(np.exp2(2.1 + 2.1 * rng.random((N, 8, 1, W))).astype(np.int64) - 1, 15)
    sg = (rng.random((N, 8, 16, W)) * (hi + 1)).astype(np.int64) * (rng.random((N, 8, 1, W)) > 0.0625)
    co = paint(rng, 0.8, (N, 8, 1, W)).reshape(N, 128, W).astype(np.float32).astype(BF)
    u = rng.random((N, 8, V, L)); om = np.minimum(np.where(rng.random(u.shape) < 0.5, np.exp2(21 * u), 1 + 2 ** 21 * u).astype(np.int64), 2 ** 21)
    return pack(lb, lm, pb, pm, fp, sg, co, om)
def setup_inputs_ends(rng):
    lb, lm, pb, pm, fp, sg, co, om = parts(rng); i = np.arange(16)
    t = ((N - 1 - np.arange(N)[:, None] + 7 - np.arange(8)[None, :]) % 4)[:, :, None, None]
    sg = 15 * np.where(t == 0, 1, np.where(t == 1, rng.integers(0, 2, (N, 8, 1, W)), np.where(t == 2, rng.integers(0, 2, (N, 8, 16, W)), 0)))
    def some(n):
        first = i < rng.integers(1, 16, (N, 8, n, 1)); u = rng.random((N, 8, n, 1))
        b = np.where(u < 0.83, np.where(first, 0, 4095), begins(rng, N, 8, n))
        m = np.where(u < 0.66, np.where(first, 0, M - 1), np.where(u < 0.83, np.where(first, M - 1, 0), (M - 1) * rng.integers(0, 2, (N, 8, n, 16))))
        return b, m
    lb, lm = some(L); pb, pm = some(P); b0 = np.where(i < 15, 0, 4095); m0 = np.where(i < 15, 0, M - 1)
    lb[:, :, [0, 1, L - 2, L - 1]] = b0; lm[:, :, [0, 1, L - 2, L - 1]] = m0; pb[:, :, [0, P - 1]] = b0; pm[:, :, [0, P - 1]] = m0
    pb[:, :, [1, 2, P - 3, P - 2]] = begins(rng, N, 8, 4); pm[:, :, [1, 2, P - 3, P - 2]] = (M - 1) * rng.integers(0, 2, (N, 8, 4, 16))
    fp = (P - 1) * rng.integers(0, 2, (N, 8, L))
    whole = [2, 3, L - 4, L - 3]; pb[:, :, P - 1] = 0
    lb[:, :, whole] = 0; lm[:, :, whole] = m0; fp[:, :, whole] = P - 1
    om = np.where(rng.random(om.shape) < 0.7, np.where(rng.random(om.shape) < 0.4, 1, 2 ** 21), rng.choice(np.array([479, 480, 481, 480 * 4095, 480 * 4095 + 1, 480 * 4096 - 1, 480 * 4096, 480 * 4096 + 1]), om.shape))
    om[..., [0, L - 1]] = 480 * 4095 + 1; om[..., [1, L - 2]] = 480 * 4095
    om[:, :, 0, 2] = 480 * 4096; om[:, :, 0, L - 3] = 480 * 4096; om[:, :, 0, 3] = 2 ** 21; om[:, :, 0, L - 4] = 2 ** 21
    return pack(lb, lm, pb, pm, fp, sg, co, om)
def setup_inputs_corners(rng):
    lb, lm, pb, pm, fp, sg, co, om = parts(rng); i = np.arange(16)
    kind = (np.arange(N)[:, None] + np.arange(8)[None, :]) % 4; k4 = kind[:, :, None, None]
    sg = np.where(k4 == 0, level(rng, np.arange(W) // D * 240 // (M - 1)), np.where(k4 == 2, level(rng, rng.integers(1, 240, (N, 8, 1, 1))), sg))
    runs = rng.choice(np.array([1, 2, 3, 15, 16, 16, 17, 31]), (N, 8, L, 1)); own = rng.integers(np.maximum(1, runs - 15), np.minimum(16, runs) + 1)
    steps = 120 * i + rng.integers(0, 100, (N, 8, L, 16)); steps[..., 0] = 0
    lb = np.where(k4 == 0, steps, lb); lm = np.where(k4 == 0, rng.integers(2, M // 4, (N, 8, L, 1)) + 4 * (np.minimum(i, own - 1) % 2), lm)
    kk = np.arange(16)[:, None]; late = i >= 16 - kk
    pb[:, :, P - 16:] = np.where(k4 == 0, np.where(late, 2100 + 120 * (i - 16 + kk) + rng.integers(0, 100, (N, 8, 16, 16)), 0), pb[:, :, P - 16:])
    pm[:, :, P - 16:] = np.where(k4 == 0, np.where(late, M // 2 + 4 + 4 * (i % 2), 0), pm[:, :, P - 16:])
    one = np.repeat(fp[:, :, :1], L, axis=2); one[:, :, L - 1] = (one[:, :, L - 1] + 1) % P
    fp = np.where(kind[:, :, None] == 0, P - 16 + (runs - own)[..., 0], np.where(kind[:, :, None] == 1, one, fp))
    sel = rng.integers(0, 4, (N, 8, L, 1)); at = np.where(sel == 0, 0, np.where(sel == 1, 4095, rng.integers(1, 4096, (N, 8, L, 1))))
    lb = np.where((k4 == 1) & (sel < 3), np.where(i == 0, 0, at), lb)
    lb = np.where(k4 == 3, pick(pb, fp), lb)
    om = np.where((k4 == 1) & (rng.random(om.shape) < 0.5), 1, om)
    om[:, :, 0] = np.where((kind[:, :, None] == 0) & (rng.random((N, 8, L)) < 0.75), 2 ** 21, om[:, :, 0])
    return pack(lb, lm, pb, pm, fp, sg, co, om)
def setup_inputs_ties(rng):
    lb, lm, pb, pm, fp, sg, co, om = parts(rng); lb = lb & ~255; pb = np.where(rng.random((N, 8, P, 1)) < 0.8, pb & ~255, pb)
    sg = level(rng, rng.choice(np.array([40, 41, 120, 239, 240]), (N, 8, 1, W)))
    def choose(ln, w, cum):
        e = rng.integers(0, 32, (N, 8, L, 1)); return (np.take_along_axis(cum, e, -1) + rng.integers(0, 2, e.shape))[..., 0]
    return pack(lb, lm, pb, pm, fp, sg, co, plant(lb, lm, pb, pm, fp, sg, choose))
def setup_inputs_calm(rng):
    lb, lm, pb, pm, fp, sg, co, om = parts(rng); low = np.where(np.arange(8) % 2 == 0, 0, M - 2)[None, :, None, None]
    sg = rng.integers(4, 16, (N, 8, 16, W))
    def near(n):
        u = rng.integers(0, 3, (N, 8, n, 1)); x = np.sort(rng.integers(0, 26, (N, 8, n, 16)), axis=-1)
        b = np.where(u == 0, x, np.where(u == 1, 4070 + x, begins(rng, N, 8, n))); b[..., 0] = 0
        return b, low + rng.integers(0, 2, (N, 8, n, 16))
    lb, lm = near(L); pb, pm = near(P); fp = rng.choice(np.array([0, 1, 2, 3, P - 2, P - 1]), (N, 8, L))
    def choose(ln, w, cum):
        o = np.argsort(ln == 0, axis=-1, kind="stable"); n = np.add.reduce((ln > 0).astype(np.int64), axis=-1, keepdims=True)
        k = rng.integers(0, 6, n.shape); k = np.maximum(np.where(k < 4, np.minimum(k, n - 1), n - 1 - (k - 4)), 0)
        e = np.take_along_axis(o, k, -1); hit = np.take_along_axis(cum, e, -1)
        return np.where(rng.random(n.shape) < 0.5, hit, hit - np.take_along_axis(w, e, -1) + 1)[..., 0]
    return pack(lb, lm, pb, pm, fp, sg, co, plant(lb, lm, pb, pm, fp, sg, choose))
def check_ranges(d):
    bad = []; s = d["sg"].astype(np.float32); c = d["co"].astype(np.float32)
    if not np.all((s >= 0) & (s <= 15) & (s == np.floor(s))): bad.append("range of sg")
    if not np.all((c >= 0.5) & (c <= 2)): bad.append("range of co")
    for k, lo, hi in (("px", 0, 4095 * 256 + M - 1), ("ls", 0, 4095 * 256 + M - 1), ("fp", 0, P - 1), ("om", 1, 2 ** 21)):
        if np.min(d[k]) < lo or np.max(d[k]) > hi: bad.append("range of " + k)
    for k in ("px", "ls"):
        b, m = unpack(d[k])
        if np.max(m) >= M: bad.append("media of " + k)
        if np.any(b[..., 0] != 0) or np.any(b[..., 1:] < b[..., :-1]): bad.append("begins of " + k)
    return bad
def reference(sg, co, px, ls, fp, om):
    s = sg.astype(np.float64).reshape(N, 8, 16, W); c = co.astype(np.float64).reshape(N, 8, 16, W); tot = np.add.reduce(s, axis=2).astype(np.int64)
    pb, pm = unpack(px); lb, lm = unpack(ls); pn = np.stack([gentries(a) for a in fp]).astype(np.int64)
    bound = np.stack([gentries(a) for a in om]).astype(np.int64).reshape(N, 8, V, L)
    yc = np.zeros((N, 8, 16, V, L), np.float32); yt = np.zeros((N, 8, 16, V, L), np.float32)
    for v in range(V):
        z, ln, a, b = cut(lb, lm, pick(pb, pn), pick(pm, pn)); ia, ib, den, w, cum = weigh(tot, z, ln, a, b)
        vis = cum - w < bound[:, :, v, :, None]; seen = np.where(vis, ln, 0)
        for q in range(N):
            for g in range(8):
                ja, jb = ia[q, g].reshape(-1), ib[q, g].reshape(-1)
                tau = ((np.take(s[q, g], ja, 1) + np.take(s[q, g], jb, 1)) * seen[q, g].reshape(-1) * 2.0 ** -14).reshape(16, L, 32)
                al = tau * 0.125; tr = np.ones_like(al); tr[..., 1:] = np.multiply.accumulate(1.0 - al, axis=-1)[..., :-1]
                cc = (np.take(c[q, g], ja, 1) + np.take(c[q, g], jb, 1)).reshape(16, L, 32)
                yc[q, g, :, v] = np.add.reduce(tr * al * cc, axis=-1); yt[q, g, :, v] = np.add.reduce(tau, axis=-1)
        if v < V - 1: lb, lm, pn = hand(*remake(z, ln, den, vis, pb, pm))
    return {"yc": yc.reshape(N, 128, V * L), "yt": yt.reshape(N, 128, V * L)}

def check_inputs(d):
    bad = list(check_ranges(d))
    if not bad:
        for name, y in reference(**d).items():
            for q in range(N):
                v = np.abs(np.asarray(y[q], np.float64)); s = np.sqrt(np.mean(v * v))
                if v.max() > 7 * s or s < 2.0 ** -3: bad.append('%s of rank %d is uneven or too small' % (name, q))
    return bad

@@ -1,0 +1,617 @@
+from concourse.bass import DstId, RemoteDMATransfer
+from concourse.mybir import dt, AluOpType, AxisListType, ActivationFunctionType
+
+V = 6
+MM = 0x8421
+S21 = 2.0 ** -21
+HOLE = 1.0 - 2.0 ** -13
+YTP = 10
+COV = ()
+PEC, OVH, GK, LAT = 0.7, 30, 1.5, 3000
+YTH = (1,)
+YTX = ()
+NIT = 4
+GCH = [(0, 16), (16, 64), (64, 128)]
+F32, BF, I32, U16 = "float32", "bfloat16", "int32", "uint16"
+
+SCRATCH = {}
+for _n, _c, _d in [
+    ("SG", 4112, BF), ("CO", 4112, BF), ("pxr", 1024, I32), ("pxu", 1024, I32), ("lsr", 128, I32), ("fpr", 8, I32),
+    ("omi", 48, I32), ("omf", 48, F32), ("omo", 48, I32), ("omu", 48, U16), ("OMB", 768, F32), ("OMX", 768, F32),
+    ("KT", 1024, F32), ("PY", 1024, F32), ("ti", 512, I32),
+    ("ones", 1024, BF), ("onef", 256, F32), ("Ib", 128, BF), ("nI", 128, BF), ("I25", 128, BF), ("nI17", 128, BF),
+    ("If", 128, F32), ("I21", 128, F32), ("PR", 128, F32), ("PL", 128, F32), ("cm", 128, BF),
+    ("blk", 8, F32), ("nblk", 8, F32), ("RS", 16, BF), ("RA", 16, BF), ("Sel", 1024, BF), ("E16", 512, BF),
+    ("rst", 256, BF), ("r16", 128, BF), ("d0c", 256, F32), ("cG", 256, F32), ("cGy", 128, F32), ("ck", 128, F32),
+    ("mk2", 256, F32), ("sio", 256, F32), ("pj", 8, I32), ("col", 8, F32),
+    ("NO", 48, U16), ("NL", 48, U16), ("LS", 640, F32), ("LL", 768, F32),
+    ("g0", 128, I32), ("k0i", 128, I32), ("k0f", 128, F32), ("LG", 128, F32),
+    ("PG", 128, F32), ("Lo0", 128, F32), ("Lo1", 128, F32), ("Ks", 256, I32), ("fi", 256, I32),
+    ("dA", 256, BF), ("qq", 256, BF), ("fB", 256, BF), ("A", 256, BF), ("B", 256, BF), ("sl", 256, BF),
+    ("ZI", 264, I32), ("ln", 256, F32), ("zs", 264, F32), ("hI", 128, BF), ("nh", 128, BF), ("OF0", 512, U16), ("OF1", 512, U16),
+    ("w", 256, F32), ("lm", 256, F32), ("gt", 256, F32), ("mm", 256, F32), ("lk", 256, F32), ("dF", 256, F32),
+    ("e", 256, I32), ("e2", 256, I32), ("nn", 256, F32), ("G", 256, F32),
+    ("li", 24, I32), ("E2", 2048, F32), ("a3", 8, F32), ("NI", 256, F32), ("AN", 256, F32),
+    ("YG", 128, F32), ("LI", 128, F32), ("LB", 128, F32), ("nl", 128, F32), ("lt", 128, F32),
+    ("Gy", 128, F32), ("y2", 384, I32), ("y3", 384, I32), ("y4", 384, I32), ("E0", 192, F32), ("E1", 192, F32),
+    ("Z", 384, F32), ("XF", 128, F32), ("xi", 128, I32), ("xh", 128, I32), ("xl", 128, I32),
+    ("xt", 128, F32), ("HL", 512, BF), ("HR", 512, F32), ("LT0", 512, BF), ("LT1", 512, BF),
+    ("xA", 4096, BF), ("S0", 4096, BF), ("S1", 4096, BF), ("cA0", 4112, BF), ("cA1", 4112, BF),
+    ("cB0", 4112, BF), ("cB1", 4112, BF), ("tr0", 4104, F32), ("tr1", 4104, F32), ("Eo", 4104, F32),
+    ("YC", 768, F32), ("YT", 768, F32), ("rs4", 512, BF),
+]:
+    SCRATCH[_n] = ("sbuf", [128, _c], _d)
+SCRATCH["DM"] = ("sbuf", [128, 8, 48], I32)
+SCRATCH["PN"] = ("sbuf", [128, 8, 48], F32)
+for _k in range(8):
+    SCRATCH["b%d" % _k] = ("psum", [128, 512], F32)
+
+SEMAPHORES = (["sV", "sA", "sP", "sG", "sent"] + ["d%d" % _k for _k in range(24)]
+              + ["nm%d" % _k for _k in range(1, V)] + ["li%d" % _k for _k in range(1, V)])
+
+ALU = AluOpType
+ACT = ActivationFunctionType
+CYC = 0.83
+GAP1, GAP2, SLACK = 120.0, 200.0, 300.0
+
+
+def R(name, a=0, b=None, s=1, p=None):
+    if b is None:
+        b = SCRATCH[name][1][1]
+    cols = range(a, b, s)
+    exact = 0
+    if abs(s) == 1:
+        exact = ((1 << len(cols)) - 1) << min(cols)
+    else:
+        for c in cols:
+            exact |= 1 << c
+    lo, hi = min(cols), max(cols)
+    return {"n": name, "a": a, "b": b, "s": s, "p": p, "len": len(cols), "x": exact,
+            "box": ((1 << (hi - lo + 1)) - 1) << lo, "ps": SCRATCH[name][0] == "psum", "dt": SCRATCH[name][2]}
+
+
+def R3(name, a, b):
+    x = 0
+    for k in range(8):
+        x |= ((1 << (b - a)) - 1) << (48 * k + a)
+    return {"n": name, "in": (a, b), "p": None, "len": 8 * (b - a), "x": x, "box": (1 << 384) - 1, "ps": False,
+            "dt": SCRATCH[name][2]}
+
+
+def IND(win, off):
+    return {"win": win, "off": off, "len": 16 * off["len"], "ps": False, "dt": win["dt"]}
+
+
+def build(T, rank, core, topo):
+    ops = []
+    hist = {}
+    turns = {}
+
+    def ap(r):
+        if not isinstance(r, dict):
+            return r
+        if "win" in r:
+            return ap(r["win"]).indirect(ap(r["off"]))
+        t = T[r["n"]]
+        if "in" in r:
+            return t[:, :, r["in"][0]:r["in"][1]]
+        b = None if r["b"] < 0 else r["b"]
+        cs = slice(r["a"], b) if r["s"] == 1 else slice(r["a"], b, r["s"])
+        ps = slice(None) if r["p"] is None else slice(r["p"][0], r["p"][1])
+        return t[ps, cs]
+
+    def add(eng, fn, outs, ins, cost, lat=0.0, after=(), sem=None, ext=None):
+        me = len(ops)
+        reads = []
+        for r in ins:
+            if isinstance(r, dict):
+                reads += [r["win"], r["off"]] if "win" in r else [r]
+        deps = set(after)
+        for r, wr in [(r, False) for r in reads] + [(r, True) for r in outs]:
+            h = hist.setdefault(r["n"], [])
+            if r["ps"]:
+                turn = turns.setdefault(r["n"], [eng, [], []])
+                if turn[0] != eng:
+                    turn[:] = [eng, turn[2], []]
+                    h[:] = []
+                deps.update(turn[1])
+                if eng == "P":
+                    deps.update(turn[2][-2:])
+                if me not in turn[2]:
+                    turn[2].append(me)
+            for (o, oe, ox, obox, ow) in h:
+                if oe == eng and sem is None and (o == me or ops[o]["sem"] is None):
+                    if (wr or ow) and (ox & r["x"]):
+                        deps.add(o)
+                elif (wr or ow) and (obox & r["box"]):
+                    deps.add(o)
+            if wr and r["p"] is None:
+                h[:] = [z for z in h if z[2] & ~r["x"]]
+            h.append((me, eng, r["x"], r["box"], wr))
+        deps.discard(me)
+        ops.append({"e": eng, "fn": fn, "deps": deps, "cost": cost, "lat": lat, "sem": sem, "ext": ext, "ord": set(),
+                    "nm": outs[0]["n"] if outs else "-"})
+        return me
+
+    def chain(lst):
+        for a, b in zip(lst, lst[1:]):
+            ops[b]["ord"].add(a)
+
+    def vcost(n, k=1.0):
+        return CYC * 1.2 * (OVH + max(n * k, 64 - OVH))
+
+    def half(*rs):
+        return 0.5 if all(r["dt"] in (BF, U16) for r in rs if isinstance(r, dict)) else 1.0
+
+    def gk(r, k):
+        return GK if "win" in r else k
+
+    def ts(out, in0, s1, op0, s2=None, op1=None):
+        if op1 is None:
+            f = lambda g: g.vector.tensor_scalar(ap(out), ap(in0), ap(s1), None, op0)
+        else:
+            f = lambda g: g.vector.tensor_scalar(ap(out), ap(in0), ap(s1), ap(s2), op0, op1)
+        return add("V", f, [out], [in0, s1, s2], vcost(out["len"], gk(in0, half(out, in0))))
+
+    def tt(out, a, b, op):
+        k = gk(a, 1.0 if (a["ps"] or b["ps"]) else 2.0)
+        return add("V", lambda g: g.vector.tensor_tensor(ap(out), ap(a), ap(b), op), [out], [a, b], vcost(out["len"], k))
+
+    def cp(out, a):
+        return add("V", lambda g: g.vector.tensor_copy(ap(out), ap(a)), [out], [a], vcost(out["len"], gk(a, half(out, a))))
+
+    def ms(out, c):
+        return add("V", lambda g: g.vector.memset(ap(out), c), [out], [], vcost(out["len"], half(out)))
+
+    def scan(out, d0, d1, init, op0, op1):
+        return add("V", lambda g: g.vector.tensor_tensor_scan(ap(out), ap(d0), ap(d1), init, op0, op1),
+                   [out], [d0, d1], vcost(out["len"], half(out, d0, d1)))
+
+    def act(out, a, func=None, bias=None, scale=None):
+        kw = {}
+        if bias is not None:
+            kw["bias"] = bias
+        if scale is not None:
+            kw["scale"] = scale
+        fu = ACT.Identity if func is None else func
+        return add("A", lambda g: g.scalar.activation(ap(out), ap(a), fu, **kw), [out], [a], vcost(out["len"] + 20, gk(a, 1.0)))
+
+    def mm(lst):
+        def f(g):
+            r = None
+            for (o, l, h, st, sp) in lst:
+                r = g.tensor.matmul(ap(o), ap(l), ap(h), st, sp)
+            return r
+        c = sum(max(min(64, l["len"]), h["len"]) * (4 if l["dt"] == F32 else 1) for (o, l, h, st, sp) in lst)
+        return add("P", f, [x[0] for x in lst], [x[1] for x in lst] + [x[2] for x in lst], 30 + PEC * c)
+
+    def iota(out, pat, base, ch):
+        if out["dt"] == I32:
+            f = lambda g: g.iota(ap(out), pat, base, ch)
+        else:
+            f = lambda g: g.iota(ap(out), pat, base, ch, allow_small_or_imprecise_dtypes=True)
+        return add("G", f, [out], [], 150 + 2 * out["len"])
+
+    def sel(out, a, pat, op, base, ch):
+        return add("G", lambda g: g.affine_select(ap(out), ap(a), pat, op, 0.0, base, ch), [out], [a], 200 + 2 * out["len"])
+
+    nd = [0]
+
+    def dma(eng, out, src, nbytes, outs, ins):
+        s = "d%d" % nd[0]
+        nd[0] += 1
+        if eng == "S":
+            f = lambda g: g.sync.dma_start(ap(out), ap(src))
+        else:
+            f = lambda g: g.scalar.dma_start(ap(out), ap(src))
+        return add(eng, f, outs, ins, 60, lat=2000 + nbytes / 200.0, sem=(s, 16))
+
+    dma("S", R("lsr"), T.ls[:], 65536, [R("lsr")], [])
+    dma("S", R("fpr", p=(0, 112)), T.fp[16:128, :], 4096, [R("fpr", p=(0, 112))], [])
+    dma("S", R("fpr", p=(112, 128)), T.fp[0:16, :], 4096, [], [])
+    fp2 = len(ops) - 1
+    dma("S", R("pxr", p=(0, 112)), T.px[16:128, :], 500000, [R("pxr", p=(0, 112))], [])
+    dma("S", R("pxr", p=(112, 128)), T.px[0:16, :], 500000, [], [])
+    px2 = len(ops) - 1
+    dma("S", R("omi"), T.om[:], 500000, [R("omi")], [])
+    dma("S", R("SG", 0, 4096), T.sg[:], 1600000, [R("SG", 0, 4096)], [])
+    dma("S", R("pxu"), T.px[:], 2100000, [R("pxu")], [])
+    dma("S", R("CO", 0, 4096), T.co[:], 3100000, [R("CO", 0, 4096)], [])
+    chain(list(range(len(ops))))
+    hist["fpr"].append((fp2, "S", R("fpr")["x"], R("fpr")["box"], True))
+    hist["pxr"].append((px2, "S", R("pxr")["x"], R("pxr")["box"], True))
+
+    iota(R("pj", 0, 1), [[0, 1]], 0, 1)
+    iota(R("onef"), [[0, 256]], 1, 0)
+    sel(R("PL"), R("onef", 0, 128), [[-1, 16], [-16, 8]], ALU.is_equal, 0, 1)
+    sel(R("PR"), R("onef", 0, 128), [[1, 16], [-16, 8]], ALU.is_equal, 1, 1)
+    sel(R("PR", 0, 128, 8), R("onef", 0, 16), [[1, 16]], ALU.is_equal, -127, 1)
+    sel(R("If"), R("onef", 0, 128), [[-1, 128]], ALU.is_equal, 0, 1)
+    sel(R("blk"), R("onef", 0, 8), [[-16, 8]], ALU.is_ge, 0, 1)
+    sel(R("blk"), R("blk"), [[16, 8]], ALU.is_ge, 15, -1)
+    ms(R("ones"), 1.0)
+    iota(R("omo"), [[1, 48]], 0, 0)
+    sel(R("E16", p=(0, 16)), R("ones", 0, 512, p=(0, 16)), [[0, 32], [-1, 16]], ALU.is_equal, 0, 1)
+    sel(R("rst"), R("ones", 0, 256), [[0, 8], [1, 32]], ALU.is_gt, 0, 0)
+    iota(R("sio"), [[0, 8], [1, 32]], 0, 0)
+    sel(R("r16"), R("ones", 0, 128), [[0, 8], [1, 16]], ALU.is_gt, 0, 0)
+    iota(R("cGy"), [[0, 8], [-1, 16]], 16, 0)
+    iota(R("ck"), [[512, 16], [0, 8]], 512 - 2 ** 24, 0)
+    sel(R("Sel", p=(0, 64)), R("ones", p=(0, 64)), [[-1, 8], [-8, 8], [0, 16]], ALU.is_equal, 0, 1)
+    sel(R("Sel", p=(64, 128)), R("ones", p=(64, 128)), [[-1, 8], [-8, 8], [0, 16]], ALU.is_equal, 0, 1)
+    ts(R("pj", 1, 2), R("pj", 0, 1), 15, ALU.bitwise_and)
+    jj = R("pj", 1, 2)
+    ts(R("col", 0, 1), jj, 512.0, ALU.mult, -2.0 ** 24, ALU.add)
+    ts(R("col", 1, 2), jj, 512.0, ALU.mult, 256.0 - 2.0 ** 24, ALU.add)
+    ts(R("col", 2, 3), jj, 0.5, ALU.is_gt)
+    ts(R("col", 3, 4), R("col", 2, 3), -4224.0, ALU.mult, 4096.0, ALU.add)
+    ts(R("col", 4, 5), jj, 2.0, ALU.mult)
+    act(R("Ib"), R("If"))
+    act(R("I25"), R("If"), scale=2.0 ** 25)
+    act(R("nI"), R("If"), scale=-1.0)
+    act(R("nblk"), R("blk"), scale=-1.0)
+    act(R("RS", 0, 8), R("blk"), scale=-4096.0)
+    act(R("RS", 8, 16), R("blk"))
+    act(R("RA", 0, 8), R("blk"), scale=0.0)
+    act(R("RA", 8, 16), R("blk"), scale=-2.0)
+    act(R("I21"), R("If"), scale=S21)
+    act(R("nI17"), R("If"), scale=-2.0 ** -17)
+    act(R("cm"), R("onef", 0, 128), scale=-1.0 / 128)
+    act(R("d0c"), R("rst"), scale=2.0 ** 30, bias=-float(MM))
+    act(R("cG"), R("sio"), scale=-MM / HOLE, bias=32.0 * MM / HOLE)
+    act(R("b3", 128, 256), R("cGy"), scale=float(MM))
+    act(R("b3", 384, 512), R("ck"))
+    act(R("hI"), R("If"), scale=0.5)
+    act(R("nh"), R("If"), scale=-0.5)
+    act(R("cGy"), R("If"), scale=-2.0 ** -17)
+    ms(R("HR", 0, 256), 0.0)
+    ms(R("SG", 4096, 4112), 0.5)
+    ms(R("CO", 4096, 4112), 0.0)
+    for n in ("cA0", "cA1", "cB0", "cB1", "tr0", "tr1"):
+        ms(R(n, 4096, 4104), 0.0)
+    ms(R("lm", 0, 1), -1.0)
+    ms(R("dF", 0, 1), -1.0)
+    ms(R("NI"), 0.0)
+    ms(R("LI"), 0.0)
+    ts(R("mk2"), R("sio"), R("col", 4, 5), ALU.is_le)
+    sel(R("mk2"), R("mk2"), [[0, 8], [1, 32]], ALU.is_gt, 0, 0)
+    sel(R("rs4"), R("ones", 0, 512), [[0, 16], [1, 32]], ALU.is_gt, 0, 0)
+    cp(R("omu"), R("omo"))
+    cp(R("omf"), R("omi"))
+    act(R("OMB"), IND(R("omf"), R("omu")))
+    mm([(R("b5"), R("E16", 0, 128, p=(0, 16)), R("E16", p=(0, 16)), True, True)])
+    tt(R("OMX", 0, 256), R("b5", 0, 256), R("OMB", 0, 256), ALU.mult)
+    tt(R("OMX", 256, 768), R("b5"), R("OMB", 256, 768), ALU.mult)
+
+    def keys(out, src, n, ti, tf, c):
+        ts(R(ti, 0, n), src, 0xFFF00, ALU.bitwise_and)
+        ts(R(tf, 0, n), R(ti, 0, n), 31.0, ALU.mult, c, ALU.add)
+        tt(out, R(tf, 0, n), src, ALU.add)
+
+    keys(R("LG"), R("lsr"), 128, "xi", "xt", R("col", 1, 2))
+    mm([(R("b4", 0, 128), R("LG"), R("PL"), True, True)])
+    cp(R("LL", 0, 128), R("b4", 0, 128))
+    cp(R("NL", 0, 8), R("fpr"))
+    cp(R("g0"), IND(R("pxr"), R("NL", 0, 8)))
+    keys(R("PG"), R("g0"), 128, "k0i", "k0f", R("col", 0, 1))
+    for a in range(0, 1024, 512):
+        ts(R("ti"), R("pxu", a, a + 512), 0xFFF00, ALU.bitwise_and)
+        ts(R("b6"), R("ti"), 3.0, ALU.mult, 256.0, ALU.add)
+        tt(R("PY", a, a + 512), R("b6"), R("pxu", a, a + 512), ALU.subtract)
+    for a in range(0, 1024, 512):
+        ts(R("ti"), R("pxr", a, a + 512), 0xFFF00, ALU.bitwise_and)
+        ts(R("b6"), R("ti"), 31.0, ALU.mult, R("col", 0, 1), ALU.add)
+        tt(R("KT", a, a + 512), R("b6"), R("pxr", a, a + 512), ALU.add)
+
+    nxt = T.cores[(rank + 1) % len(T.cores)]
+    rid, pid = topo.addr(nxt)[0], topo.addr(nxt)[1]
+    msk = topo.mask(core, nxt)
+    neng = len(topo.engines(core, nxt))
+    nsent = [0]
+
+    def send(dst, src, sem):
+        f = lambda g: g.remote_dma(ap(dst), ap(src), T.sem[sem], T.sem.sent, pid, rid, msk)
+        nsent[0] += neng
+        o = add("G", f, [], [src], 600, sem=("", 0))
+        return add("X", None, [dst], [], 0, lat=LAT + (1200 if src["dt"] == F32 else 0), after=[o], ext=(sem, neng), sem=("", 0))
+
+    mn, mx = ALU.min, ALU.max
+    P0, P1, P2, P3 = R("b0", 0, 256), R("b0", 256, 512), R("b1", 0, 256), R("b1", 256, 512)
+    fb = [0]
+
+    def fbank():
+        fb[0] += 1
+        return "b%d" % (4 + fb[0] % 3)
+
+    for v in range(V):
+        OF, S, cA, cB, tr = ["%s%d" % (n, v % 2) for n in ("OF", "S", "cA", "cB", "tr")]
+        if v > 0:
+            act(R("PG"), IND(R("KT"), R("NL", 8 * v, 8 * v + 8)))
+        mm([(R("b3", 0, 128), R("PG"), R("PR"), True, True)])
+        lo, hi = ("LL", 128 * v), ("b3", 0)
+        for st in range(4):
+            nlo, nhi = ("Lo%d" % (st % 2), 0), ("b0", 128 * (st % 2))
+            for (h0, dst) in ((0, nlo), (64, nhi)):
+                for (k, op) in ((0, mn), (1, mx)):
+                    tt(R(dst[0], dst[1] + k, dst[1] + 128, 2), R(lo[0], lo[1] + h0, lo[1] + h0 + 64),
+                       R(hi[0], hi[1] + h0, hi[1] + h0 + 64), op)
+            lo, hi = nlo, nhi
+        for (k, op) in ((0, mn), (1, mx)):
+            tt(R("Ks", k, 256, 2), R(lo[0], lo[1], lo[1] + 128), R(hi[0], hi[1], hi[1] + 128), op)
+        ts(R("fi"), R("Ks"), 511, ALU.bitwise_and)
+        ts(R("ZI", 0, 256), R("Ks"), 13, ALU.arith_shift_right)
+        ts(R("dA"), R("fi"), 256.0, ALU.subtract, S21, ALU.mult)
+        ms(R("ZI", 0, 257, 32), 2048)
+        ts(R("zs", 0, 257), R("ZI", 0, 257), 2048.5, ALU.add, 2.0 ** -12, ALU.mult)
+        act(R("fB"), R("dA"), bias=2.0 ** -13)
+        act(R("sl"), R("zs", 0, 256), scale=16.0, bias=127.5)
+        act(R("b1", 0, 257), R("zs", 0, 257), scale=4096.0, bias=-2048.5)
+        ts(R("qq"), R("dA"), 0.0, ALU.is_lt)
+        scan(R("A"), R("qq"), R("dA"), 0.0, mn, mx)
+        scan(R("B"), R("qq"), R("fB"), 0.0, ALU.add, mn)
+        for h in range(2):
+            lst = []
+            for k, n in enumerate("AB"):
+                o = R("b2", 256 * h + 128 * k, 256 * h + 128 * k + 128)
+                lst += [(o, R("sl", h, 256, 2), R("Ib"), True, False), (o, R(n, h, 256, 2), R("I25"), False, True)]
+            mm(lst)
+        ts(R(OF, 0, 256), R("b2", 0, 256), R("col", 2, 3), ALU.mult, R("col", 3, 4), ALU.add)
+        ts(R(OF, 256, 512), R("b2", 256, 512), -128.0, ALU.add)
+        tt(R("ln"), R("b1", 1, 257), R("ZI", 0, 256), ALU.subtract)
+        if v < V - 1:
+            mm([(P2, R("If"), R("zs", 0, 256), True, False)])
+            mm([(P2, R("nh"), R("A"), False, False), (P2, R("nh"), R("B"), False, True),
+                (P3, R("hI"), R("A"), True, False), (P3, R("nh"), R("B"), False, True)])
+        mm([(R("b2", 0, 256, 32), R("OMX", 128 * v, 128 * v + 128), R("nblk"), True, False)])
+        ga, gb = [], []
+        for h in range(2):
+            for (l0, l1) in (GCH if h == 0 else [(0, 64), (64, 128)]):
+                c0, c1 = 2048 * h + 16 * l0, 2048 * h + 16 * l1
+                ga.append(act(R("xA", c0, c1), IND(R("SG"), R(OF, 256 * h + l0, 256 * h + l1))))
+                src = IND(R("SG"), R(OF, 256 * h + 128 + l0, 256 * h + 128 + l1))
+                gb.append(tt(R(S, c0, c1), src, R("xA", c0, c1), ALU.add))
+            chain(ga)
+            chain(gb)
+            ss = [s for s in range(h, 32, 2) if s > 0]
+            if v < V - 1:
+                mm([(R("b2", s, 512, 32), R("xA", 2048 * h + s // 2, 2048 * h + 2048, 16), R("RA"), False, False) for s in ss])
+            mm([(R("b2", s, 512 if v < V - 1 else 256, 32), R(S, 2048 * h + s // 2, 2048 * h + 2048, 16),
+                 R("RS", 0, 16 if v < V - 1 else 8), False, s == 31) for s in ss])
+        tt(R("w"), R("b2", 0, 256), R("ln"), ALU.mult)
+        if v < V - 1:
+            act(R("gt"), R("b2", 256, 512), ACT.Sign, bias=-0.5)
+        scan(P0, R("rst"), R("w"), 0.0, ALU.mult, ALU.add)
+        tt(R("lm", 1, 256), R("b0", 0, 255), R("ln", 1, 256), mn)
+        if v < V - 1:
+            tt(R("mm"), P3, R("gt"), ALU.mult)
+            tt(P1, P2, R("mm"), ALU.add)
+            tt(R("lk"), P1, R("lm"), mn)
+            scan(P0, R("rst"), R("lk"), 0.0, ALU.mult, mx)
+            last = R("b0", 31, 256, 32)
+            li, a1, a2 = R("li", 0, 8), R("li", 8, 16), R("li", 16, 24)
+            ts(li, last, 2.0 ** 21, ALU.mult)
+            ts(a1, li, 511, ALU.bitwise_and)
+            ts(a2, li, 19, ALU.arith_shift_right)
+            ts(R("a3"), a1, -4.0, ALU.mult, 1024.0, ALU.add)
+            tt(R("NI", 0, 256, 32), R("a3"), a2, ALU.add)
+            scan(R("AN"), R("mk2"), R("NI"), 0.0, ALU.mult, ALU.add)
+            mm([(R("b3", 0, 8), R("AN", 0, 256, 2), R("blk"), True, False),
+                (R("b3", 0, 8), R("AN", 1, 256, 2), R("nblk"), False, True)])
+            no = R("NO", 8 * v, 8 * v + 8)
+            cp(no, R("b3", 0, 8))
+            send(R("NL", 8 * v + 8, 8 * v + 16), no, "nm%d" % (v + 1))
+            act(R("YG"), IND(R("PY"), no))
+            yps = R("b3", 256, 384)
+            mm([(yps, R("YG"), R("I21"), True, True)])
+            tt(R("dF", 1, 256), R("lk", 1, 256), R("b0", 0, 255), ALU.subtract)
+            ts(R("LI", 0, 128, 16), last, 256.5 * S21, ALU.add)
+            ts(R("e"), R("dF"), 0.0, mx, 2.0 ** 21, ALU.mult)
+            ts(R("e2"), R("e"), 511, ALU.bitwise_and)
+            ts(R("nn"), R("e2"), 1.0, mn, float(MM), ALU.mult)
+            act(P2, R("nn"), ACT.Relu, scale=-2.0 / MM, bias=HOLE)
+            scan(P1, R("d0c"), R("nn"), -float(MM), mn, ALU.add)
+            tt(R("G"), P2, R("cG"), ALU.mult)
+            tt(R3("PN", 0, 32), P2, R("lk"), mx)
+            tt(R3("DM", 0, 32), P1, R("G"), ALU.add)
+            scan(R("LB"), R("r16"), R("LI"), 0.0, ALU.mult, ALU.add)
+            tt(R("nl"), yps, R("LB"), ALU.is_le)
+            ts(R("lt"), R("nl"), -float(MM), ALU.mult, float(MM), ALU.add)
+            ts(R("lt", 0, 128, 16), R("b0", 256 + 31, 512, 32), 15.0 * MM, mn)
+            scan(R("b1", 256, 384), R("r16"), R("lt"), 0.0, ALU.mult, ALU.add)
+            tt(R("Gy"), R("b3", 128, 256), R("nl"), ALU.mult)
+            tt(R3("PN", 32, 48), yps, R("nl"), mx)
+            tt(R3("DM", 32, 48), R("b1", 256, 384), R("Gy"), ALU.add)
+            act(R("b1", 0, 384), R3("PN", 0, 48), bias=-8.0)
+            ts(R("y2"), R3("DM", 0, 48), 0x8888, ALU.bitwise_and)
+            ts(R("y3"), R("y2"), float(0x249), ALU.mult)
+            ts(R("y4"), R("y3"), 12, ALU.arith_shift_right, 15, ALU.bitwise_and)
+            tt(R("E0"), R("b1", 0, 384, 2), R("y4", 0, 384, 2), ALU.add)
+            tt(R("b0", 0, 192), R("b1", 1, 384, 2), R("y4", 1, 384, 2), ALU.add)
+            for st in range(3):
+                e0, e1, o0, o1 = "E%d" % (st % 2), "E%d" % (1 - st % 2), 256 * (st % 2), 256 * (1 - st % 2)
+                for (k, dn, d0) in ((0, e1, 0), (1, "b0", o1)):
+                    for (u, op) in ((0, mn), (96, mx)):
+                        tt(R(dn, d0 + u, d0 + u + 96), R(e0, k, 192, 2), R("b0", o0 + k, o0 + 192, 2), op)
+            tt(R("Z", 0, 192), R("E1"), R("b0", 256, 448), mn)
+            tt(R("Z", 192, 384), R("E1"), R("b0", 256, 448), mx)
+            tt(R("b0", 0, 128), R("Z", 0, 384, 3), R("Z", 1, 384, 3), mn)
+            tt(R("XF"), R("b0", 0, 128), R("Z", 2, 384, 3), mn)
+            ts(R("xi"), R("XF"), 2.0 ** 25, ALU.mult)
+            ts(R("xl"), R("xi"), 4, ALU.arith_shift_right, 511, ALU.bitwise_and)
+            ts(R("xh"), R("xi"), 0x1FFE000, ALU.bitwise_and)
+            tt(R("b0", 128, 256), R("b3", 384, 512), R("xl"), ALU.subtract)
+            tt(R("LS", 128 * v, 128 * v + 128), R("b0", 128, 256), R("xh"), ALU.add)
+            send(R("LL", 128 * v + 128, 128 * v + 256), R("LS", 128 * v, 128 * v + 128), "li%d" % (v + 1))
+        act(R("HL", 0, 256), R("lm"), ACT.Relu)
+        act(R("HR", 256, 512), R("lm"), ACT.Relu)
+        act(R("HL", 256, 512), R("HL", 0, 256), scale=-1.0)
+        for u in range(4):
+            o = R("b2", 128 * u, 128 * u + 128)
+            mm([(o, R("HR", u, 512, 4), R("cGy"), True, False), (o, R("HL", u, 512, 4), R("nI17"), False, True)])
+        LT = "LT%d" % (v % 2)
+        act(R(LT), R("b2"))
+        for hf in (1, 0):
+            for h in range(2):
+                for (n, k) in ((cA, 0), (cB, 128)):
+                    (cp if (v == V - 1 and n == cB and hf in COV) else act)(
+                        R(n, 2048 * hf + h, 2048 * hf + 2048, 2),
+                        IND(R("CO"), R(OF, 256 * h + k + 64 * hf, 256 * h + k + 64 * hf + 64)))
+            for q in range(4):
+                bk = fbank()
+                lst = []
+                for t in range(8):
+                    if q == 0 and t == 0:
+                        lst.append((R(bk, 0, 512, 8), R("cm"), R("ones", 0, 64), True, True))
+                    else:
+                        lst.append((R(bk, t, 512, 8), R("Sel", 128 * t, 128 * t + 128),
+                                    R(LT, 128 * q + 64 * hf, 128 * q + 64 * hf + 64), True, True))
+                mm(lst)
+                c0 = 2048 * (q % 2) + 1024 * hf
+                tt(R(tr, 2048 * hf + q, 2048 * hf + 2048, 4), R(bk), R(S, c0 + q // 2, c0 + 1024, 2), ALU.mult)
+            for a in (2048 * hf + 1024, 2048 * hf):
+                act(R(tr, a, a + 1024), R(tr, a, a + 1024), bias=1.0)
+            for c in range(4 * hf + 3, 4 * hf - 1, -1):
+                bk = fbank()
+                a = 512 * c
+                mm([(R(bk), R("Ib"), R(cA, a + 1, a + 513), True, False)])
+                mm([(R(bk), R("Ib"), R(cB, a + 1, a + 513), False, False)])
+                mm([(R(bk), R("nI"), R(cA, a, a + 512), False, False)])
+                mm([(R(bk), R("nI"), R(cB, a, a + 512), False, True)])
+                scan(R("Eo", a + 512, a, -1), R(tr, a + 512, a, -1), R(bk, 511, -1, -1), 0.0, ALU.mult, ALU.add)
+            o = 128 * v + 64 * hf
+            act(R("YC", o, o + 64), R("Eo", 2048 * hf + 1, 2048 * hf + 2048, 32))
+            if (2 * v + 1 - hf < YTP and hf in YTH) or (v, hf) in YTX:
+                for s0 in range(1, 32, 2):
+                    mm([(R("b7", 256 + 64 * hf, 320 + 64 * hf), R("If"), R(tr, 2048 * hf + s, 2048 * hf + 2048, 32),
+                         s == 1, s == 31) for s in range(s0, min(s0 + 2, 32))])
+                act(R("YT", o, o + 64), R("b7", 256 + 64 * hf, 320 + 64 * hf), scale=-8.0, bias=248.0)
+            else:
+                for a in range(2048 * hf, 2048 * hf + 2048, 512):
+                    scan(R("E2", a % 2048, a % 2048 + 512), R("rs4"), R(tr, a, a + 512), 0.0, ALU.mult, ALU.add)
+                act(R("YT", o, o + 64), R("E2", 31, 2048, 32), scale=-8.0, bias=248.0)
+        o = 128 * v
+        dma("S", T.yc[:, o:o + 128], R("YC", o, o + 128), 65536, [], [R("YC", o, o + 128)])
+        dma("S", T.yt[:, o:o + 128], R("YT", o, o + 128), 65536, [], [R("YT", o, o + 128)])
+    return ops, nsent[0]
+
+
+def schedule(ops):
+    n = len(ops)
+    kids = [[] for _ in range(n)]
+    for i, o in enumerate(ops):
+        for d in o["deps"] | o["ord"]:
+            kids[d].append(i)
+
+    def gap(a, b):
+        if a not in ops[b]["deps"] or (ops[a]["e"] == "P" and ops[b]["e"] == "P"):
+            return 0.0
+        return (GAP1 if ops[a]["e"] == ops[b]["e"] else GAP2) + ops[a]["lat"]
+    tail = [0.0] * n
+    for i in range(n - 1, -1, -1):
+        tail[i] = ops[i]["cost"] + max([gap(i, k) + tail[k] for k in kids[i]] + [ops[i]["lat"]])
+    par = [sorted(o["deps"] | o["ord"]) for o in ops]
+    key = [-x for x in tail]
+    best = None
+    for it in range(NIT):
+        order, st, end = one_pass(ops, par, kids, gap, key)
+        if best is None or end < best[1]:
+            best = (order, end, st)
+        back = one_pass(ops, kids, par, lambda a, b: gap(b, a), [-(st[i] + ops[i]["cost"]) for i in range(n)])[1]
+        key = [-(back[i] + ops[i]["cost"]) for i in range(n)]
+    for i in range(n):
+        ops[i]["st"] = best[2][i]
+    return best[0], best[1]
+
+
+def one_pass(ops, par, kids, gap, key):
+    n = len(ops)
+    left = [len(b) for b in par]
+    rdy = [0.0] * n
+    start = [0.0] * n
+    pool = {}
+    free = {}
+    order = {}
+    for e in "VAPGSX":
+        pool[e], free[e], order[e] = [], 0.0, []
+    for i in range(n):
+        if left[i] == 0:
+            pool[ops[i]["e"]].append(i)
+    done = 0
+    end = 0.0
+    while done < n:
+        t, e = min((max(free[e], min(rdy[i] for i in pool[e])), e) for e in pool if pool[e])
+        i = None
+        soon = 1e18
+        for k in sorted(pool[e], key=lambda k: (key[k], k)):
+            if rdy[k] <= t + 1.0 and t + ops[k]["cost"] <= soon + SLACK:
+                i = k
+                break
+            if rdy[k] > t + 1.0:
+                soon = min(soon, rdy[k])
+        if i is None:
+            free[e] = soon
+            continue
+        pool[e].remove(i)
+        st = max(t, rdy[i])
+        start[i] = st
+        fin = st + ops[i]["cost"]
+        free[e] = fin if e != "X" else 0.0
+        order[e].append(i)
+        end = max(end, fin + ops[i]["lat"])
+        done += 1
+        for k in kids[i]:
+            rdy[k] = max(rdy[k], fin + gap(i, k))
+            left[k] -= 1
+            if left[k] == 0:
+                pool[ops[k]["e"]].append(k)
+    return order, start, end
+
+
+ORDER = []
+
+
+def rank_program(g, core, T, topo):
+    rank = T.rank_of(core)
+    if rank is None:
+        return
+    ops, nsent = build(T, rank, core, topo)
+    if not ORDER:
+        ORDER.append(schedule(ops)[0])
+    order = ORDER[0]
+    queue = {"V": g.vector, "A": g.scalar, "P": g.tensor, "G": g, "S": g.sync}
+    mark = {}
+    total = {}
+    for e in "VAPG":
+        c = 0
+        for i in order[e]:
+            if ops[i]["sem"] is None:
+                c += 1
+                mark[i] = ("s" + e, c)
+        total["s" + e] = c
+    for i, o in enumerate(ops):
+        if o["ext"] is not None:
+            mark[i] = o["ext"]
+            total[o["ext"][0]] = o["ext"][1]
+        elif o["sem"] is not None and o["sem"][0]:
+            mark[i] = o["sem"]
+            total[o["sem"][0]] = o["sem"][1]
+    for e in "SAGPV":
+        seen = {}
+        for i in order[e]:
+            need = {}
+            for d in ops[i]["deps"]:
+                if d in mark and not (e == "P" and ops[d]["e"] == "P"):
+                    s, c = mark[d]
+                    need[s] = max(need.get(s, 0), c)
+            if e == "G" and i in mark and mark[i][1] > 1:
+                need["sG"] = mark[i][1] - 1
+            for s in sorted(need):
+                if seen.get(s, 0) < need[s]:
+                    queue[e].wait_ge(T.sem[s], need[s])
+                    seen[s] = need[s]
+            r = ops[i]["fn"](g)
+            if i in mark:
+                r.then_inc(T.sem[mark[i][0]], 16 if ops[i]["sem"] is not None else 1)
+    total["sent"] = nsent
+    for s in sorted(total):
+        g.wait_ge(T.sem[s], total[s])

@@ -5,54 +5,63 @@ V = 6
 MM = 0x8421
 S21 = 2.0 ** -21
 HOLE = 1.0 - 2.0 ** -13
-YTP = 10
-COV = ()
-PEC, OVH, GK, LAT = 0.7, 30, 1.5, 3000
-YTH = (1,)
-YTX = ()
-NIT = 4
-GCH = [(0, 16), (16, 64), (64, 128)]
-F32, BF, I32, U16 = "float32", "bfloat16", "int32", "uint16"
+PEC, OVH, GK, LAT, FF, MINC = 0.6, 62, 1.75, 3000, 1.0, 16
+GDC, GBW, SDC, WLAT, ADDK = 1000, 300.0, 100, 1200, 1.4
+STAG, WOFF, FOFF = 31000.0, 30000.0, 0.0
+NIT, LAG, AHEAD, JIT, SEED = 3, 4000.0, 0.0, 0.0, 0
+SGV = [48] + [8] * 4 + [48]
+COV = [0] * 5 + [16]
+QUICK = (5,)
+SUM = "DDDDDD"
+ONE = "DDADDADDADAB"
+TAU = "PPPVPPPVPVVV"
+FKP, LTA, QQF, GTV, HOV, P1P = True, True, False, False, 0, True
+GCH, CCH, FCH, PCH, YCA = 64, 32, 512, 512, False
+ZC = 1.5 * 2.0 ** 36
+F32, BF, I32, U16, F16 = "float32", "bfloat16", "int32", "uint16", "float16"
 
 SCRATCH = {}
 for _n, _c, _d in [
-    ("SG", 4112, BF), ("CO", 4112, BF), ("pxr", 1024, I32), ("pxu", 1024, I32), ("lsr", 128, I32), ("fpr", 8, I32),
-    ("omi", 48, I32), ("omf", 48, F32), ("omo", 48, I32), ("omu", 48, U16), ("OMB", 768, F32), ("OMX", 768, F32),
-    ("KT", 1024, F32), ("PY", 1024, F32), ("ti", 512, I32),
-    ("ones", 1024, BF), ("onef", 256, F32), ("Ib", 128, BF), ("nI", 128, BF), ("I25", 128, BF), ("nI17", 128, BF),
-    ("If", 128, F32), ("I21", 128, F32), ("PR", 128, F32), ("PL", 128, F32), ("cm", 128, BF),
-    ("blk", 8, F32), ("nblk", 8, F32), ("RS", 16, BF), ("RA", 16, BF), ("Sel", 1024, BF), ("E16", 512, BF),
-    ("rst", 256, BF), ("r16", 128, BF), ("d0c", 256, F32), ("cG", 256, F32), ("cGy", 128, F32), ("ck", 128, F32),
-    ("mk2", 256, F32), ("sio", 256, F32), ("pj", 8, I32), ("col", 8, F32),
-    ("NO", 48, U16), ("NL", 48, U16), ("LS", 640, F32), ("LL", 768, F32),
+    ("SG", 8208, BF), ("CO", 8208, BF), ("pxi", 1152, I32), ("lsr", 128, I32), ("fpr", 8, I32),
+    ("omi", 48, I32), ("omf", 48, F32), ("omu", 48, U16),
+    ("OMS", 1536, F32), ("KT", 1024, F32), ("PY", 1024, F32),
+    ("ones", 1024, BF), ("onef", 128, F32), ("Ib", 128, BF), ("nI", 128, BF), ("I25", 128, BF),
+    ("If", 128, F32), ("I21", 128, F32), ("PRa", 128, F32), ("PRb", 128, F32), ("PL", 128, F32),
+    ("c14", 256, BF), ("Mm", 512, BF), ("Cst", 512, BF),
+    ("blk", 8, F32), ("blkK", 8, F32), ("blk4", 8, F32), ("RS", 16, BF),
+    ("E16", 512, BF), ("rst", 256, BF), ("r16", 128, BF), ("d0c", 256, F32), ("cG", 256, F32), ("cGy", 128, F32),
+    ("ck", 128, F32), ("mk2", 256, BF), ("sio", 256, F32), ("pj", 8, I32), ("col", 8, F32), ("hI", 128, BF),
+    ("nh", 128, BF), ("rs4", 512, BF),
+    ("NO", 96, U16), ("NL", 96, U16), ("LS", 640, F32), ("LL", 768, F32),
     ("g0", 128, I32), ("k0i", 128, I32), ("k0f", 128, F32), ("LG", 128, F32),
-    ("PG", 128, F32), ("Lo0", 128, F32), ("Lo1", 128, F32), ("Ks", 256, I32), ("fi", 256, I32),
-    ("dA", 256, BF), ("qq", 256, BF), ("fB", 256, BF), ("A", 256, BF), ("B", 256, BF), ("sl", 256, BF),
-    ("ZI", 264, I32), ("ln", 256, F32), ("zs", 264, F32), ("hI", 128, BF), ("nh", 128, BF), ("OF0", 512, U16), ("OF1", 512, U16),
-    ("w", 256, F32), ("lm", 256, F32), ("gt", 256, F32), ("mm", 256, F32), ("lk", 256, F32), ("dF", 256, F32),
-    ("e", 256, I32), ("e2", 256, I32), ("nn", 256, F32), ("G", 256, F32),
-    ("li", 24, I32), ("E2", 2048, F32), ("a3", 8, F32), ("NI", 256, F32), ("AN", 256, F32),
-    ("YG", 128, F32), ("LI", 128, F32), ("LB", 128, F32), ("nl", 128, F32), ("lt", 128, F32),
-    ("Gy", 128, F32), ("y2", 384, I32), ("y3", 384, I32), ("y4", 384, I32), ("E0", 192, F32), ("E1", 192, F32),
-    ("Z", 384, F32), ("XF", 128, F32), ("xi", 128, I32), ("xh", 128, I32), ("xl", 128, I32),
-    ("xt", 128, F32), ("HL", 512, BF), ("HR", 512, F32), ("LT0", 512, BF), ("LT1", 512, BF),
-    ("xA", 4096, BF), ("S0", 4096, BF), ("S1", 4096, BF), ("cA0", 4112, BF), ("cA1", 4112, BF),
-    ("cB0", 4112, BF), ("cB1", 4112, BF), ("tr0", 4104, F32), ("tr1", 4104, F32), ("Eo", 4104, F32),
-    ("YC", 768, F32), ("YT", 768, F32), ("rs4", 512, BF),
+    ("OF", 1024, U16), ("lm", 512, F32), ("X", 8192, BF), ("S", 4096, BF), ("L", 6144, F32),
+    ("C0", 8208, BF), ("C1", 8208, BF),
+    ("tr0", 2056, F32), ("tr1", 2056, F32), ("tr2", 2056, F32), ("tr3", 2056, F32), ("Eo", 2056, F32),
+    ("YC", 256, F32), ("YT", 256, F32), ("c3k", 256, BF), ("I25f", 128, F32),
+    ("bk16", 16, BF), ("ckp", 128, F32), ("c3m", 128, BF), ("III", 384, F32),
+    ("PG", 256, F32), ("Lo0", 128, F32), ("Lo1", 128, F32), ("Ks", 256, I32), ("fi", 256, I32), ("dA", 256, BF),
+    ("qq", 256, BF), ("AB", 512, BF), ("SL", 256, BF), ("zs", 272, F32), ("ln", 256, F32), ("w", 256, F32),
+    ("gt", 256, F32), ("mm", 256, BF), ("lk", 256, F32), ("dF", 256, F32), ("e", 256, I32), ("e2", 256, I32),
+    ("nn", 256, F32), ("G", 256, F32), ("li", 32, I32), ("NI", 256, F16), ("AN", 256, F16), ("YG0", 128, F32),
+    ("YG1", 128, F32), ("M0", 256, F32),
+    ("LI", 128, F32), ("LB", 128, F32), ("nl", 128, F32), ("lt", 128, F32), ("Gy", 128, F32), ("PN", 384, F32),
+    ("DM", 384, I32), ("E0", 192, F32), ("E1", 192, F32),
+    ("XF", 128, F32), ("xr", 128, F32), ("Sel", 1024, BF), ("HL", 512, BF), ("LT", 512, BF), ("cm", 128, BF),
 ]:
     SCRATCH[_n] = ("sbuf", [128, _c], _d)
-SCRATCH["DM"] = ("sbuf", [128, 8, 48], I32)
-SCRATCH["PN"] = ("sbuf", [128, 8, 48], F32)
+TWO = True
+SCRATCH["Z2" if TWO else "Z"] = ("sbuf", [128, 32, 12] if TWO else [128, 16, 24], F32)
+SCRATCH["Ld"] = ("dram", [2, 8, 128, 32], F32)
 for _k in range(8):
     SCRATCH["b%d" % _k] = ("psum", [128, 512], F32)
 
-SEMAPHORES = (["sV", "sA", "sP", "sG", "sent"] + ["d%d" % _k for _k in range(24)]
-              + ["nm%d" % _k for _k in range(1, V)] + ["li%d" % _k for _k in range(1, V)])
+SEMAPHORES = (["sV", "sA", "sP", "sG", "sent"] + ["d%d" % _k for _k in range(90)]
+              + [_n % _k for _n in ("nm%d", "li%d") for _k in (range(2, 2 * V) if TWO else range(1, V))])
 
 ALU = AluOpType
 ACT = ActivationFunctionType
 CYC = 0.83
-GAP1, GAP2, SLACK = 120.0, 200.0, 300.0
+GAP1, GAP2, SLACK = 100.0, 200.0, 300.0
 
 
 def R(name, a=0, b=None, s=1, p=None):
@@ -70,12 +79,14 @@ def R(name, a=0, b=None, s=1, p=None):
             "box": ((1 << (hi - lo + 1)) - 1) << lo, "ps": SCRATCH[name][0] == "psum", "dt": SCRATCH[name][2]}
 
 
-def R3(name, a, b):
+def R3(name, o0, o1, a, b, s=1):
+    w = SCRATCH[name][1][2]
     x = 0
-    for k in range(8):
-        x |= ((1 << (b - a)) - 1) << (48 * k + a)
-    return {"n": name, "in": (a, b), "p": None, "len": 8 * (b - a), "x": x, "box": (1 << 384) - 1, "ps": False,
-            "dt": SCRATCH[name][2]}
+    for k in range(o0, o1):
+        for c in range(a, b, s):
+            x |= 1 << (w * k + c)
+    return {"n": name, "in": (o0, o1, a, b, s), "p": None, "len": (o1 - o0) * len(range(a, b, s)), "x": x,
+            "box": ((1 << (w * (o1 - o0))) - 1) << (w * o0), "ps": False, "dt": SCRATCH[name][2]}
 
 
 def IND(win, off):
@@ -86,6 +97,7 @@ def build(T, rank, core, topo):
     ops = []
     hist = {}
     turns = {}
+    tag = [None]
 
     def ap(r):
         if not isinstance(r, dict):
@@ -94,13 +106,14 @@ def build(T, rank, core, topo):
             return ap(r["win"]).indirect(ap(r["off"]))
         t = T[r["n"]]
         if "in" in r:
-            return t[:, :, r["in"][0]:r["in"][1]]
+            o0, o1, a, b, s = r["in"]
+            return t[:, o0:o1, a:b] if s == 1 else t[:, o0:o1, a:b:s]
         b = None if r["b"] < 0 else r["b"]
         cs = slice(r["a"], b) if r["s"] == 1 else slice(r["a"], b, r["s"])
-        ps = slice(None) if r["p"] is None else slice(r["p"][0], r["p"][1])
+        ps = slice(None) if r["p"] is None else slice(*r["p"])
         return t[ps, cs]
 
-    def add(eng, fn, outs, ins, cost, lat=0.0, after=(), sem=None, ext=None):
+    def add(eng, fn, outs, ins, cost, lat=0.0, after=(), sem=None, ext=None, dm=0.0):
         me = len(ops)
         reads = []
         for r in ins:
@@ -130,7 +143,7 @@ def build(T, rank, core, topo):
             h.append((me, eng, r["x"], r["box"], wr))
         deps.discard(me)
         ops.append({"e": eng, "fn": fn, "deps": deps, "cost": cost, "lat": lat, "sem": sem, "ext": ext, "ord": set(),
-                    "nm": outs[0]["n"] if outs else "-"})
+                    "nm": outs[0]["n"] if outs else "-", "tag": tag[0], "dm": dm})
         return me
 
     def chain(lst):
@@ -138,10 +151,10 @@ def build(T, rank, core, topo):
             ops[b]["ord"].add(a)
 
     def vcost(n, k=1.0):
-        return CYC * 1.2 * (OVH + max(n * k, 64 - OVH))
+        return CYC * FF * (OVH + max(n * k, MINC))
 
     def half(*rs):
-        return 0.5 if all(r["dt"] in (BF, U16) for r in rs if isinstance(r, dict)) else 1.0
+        return 0.5 if all(r["dt"] in (BF, U16, F16) for r in rs if isinstance(r, dict)) else 1.0
 
     def gk(r, k):
         return GK if "win" in r else k
@@ -174,7 +187,8 @@ def build(T, rank, core, topo):
         if scale is not None:
             kw["scale"] = scale
         fu = ACT.Identity if func is None else func
-        return add("A", lambda g: g.scalar.activation(ap(out), ap(a), fu, **kw), [out], [a], vcost(out["len"] + 20, gk(a, 1.0)))
+        return add("A", lambda g: g.scalar.activation(ap(out), ap(a), fu, **{u: ap(kw[u]) for u in kw}), [out], [a, bias],
+                   vcost(out["len"] + 20, gk(a, 1.0)))
 
     def mm(lst):
         def f(g):
@@ -197,111 +211,170 @@ def build(T, rank, core, topo):
 
     nd = [0]
 
-    def dma(eng, out, src, nbytes, outs, ins):
+    def dmas(lst, busy, outs, ins, after=()):
         s = "d%d" % nd[0]
         nd[0] += 1
-        if eng == "S":
-            f = lambda g: g.sync.dma_start(ap(out), ap(src))
-        else:
-            f = lambda g: g.scalar.dma_start(ap(out), ap(src))
-        return add(eng, f, outs, ins, 60, lat=2000 + nbytes / 200.0, sem=(s, 16))
 
-    dma("S", R("lsr"), T.ls[:], 65536, [R("lsr")], [])
-    dma("S", R("fpr", p=(0, 112)), T.fp[16:128, :], 4096, [R("fpr", p=(0, 112))], [])
-    dma("S", R("fpr", p=(112, 128)), T.fp[0:16, :], 4096, [], [])
-    fp2 = len(ops) - 1
-    dma("S", R("pxr", p=(0, 112)), T.px[16:128, :], 500000, [R("pxr", p=(0, 112))], [])
-    dma("S", R("pxr", p=(112, 128)), T.px[0:16, :], 500000, [], [])
-    px2 = len(ops) - 1
-    dma("S", R("omi"), T.om[:], 500000, [R("omi")], [])
-    dma("S", R("SG", 0, 4096), T.sg[:], 1600000, [R("SG", 0, 4096)], [])
-    dma("S", R("pxu"), T.px[:], 2100000, [R("pxu")], [])
-    dma("S", R("CO", 0, 4096), T.co[:], 3100000, [R("CO", 0, 4096)], [])
+        def f(g):
+            r = None
+            for (u, (o, a)) in enumerate(lst):
+                r = g.sync.dma_start(ap(o), ap(a))
+                if u < len(lst) - 1 and r is not None:
+                    r.then_inc(T.sem[s], 16)
+            return r
+        return add("S", f, outs, ins, SDC * len(lst), lat=2000 + busy, sem=(s, 16 * len(lst)), after=after, dm=busy)
+
+    def dma(out, src, nbytes, outs, ins):
+        return dmas([(out, src)], nbytes / GBW, outs, ins)
+
+    def gadd(out, src, nbytes):
+        s = "d%d" % nd[0]
+        nd[0] += 1
+        f = lambda g: g.dma_start(ap(out), ap(src), accum_op=ALU.add, max_dma_last_dim=4096)
+        return add("G", f, [out], [src, out], GDC, lat=2000 + ADDK * nbytes / GBW, sem=(s, 16), dm=ADDK * nbytes / GBW)
+
+    HALF = ((0, 64), (64, 128))
+
+    def load4(name, src):
+        for gh in range(2):
+            r = R(name, 4096 * gh, 4096 * gh + 4096)
+            dmas([(R(name, 4096 * gh, 4096 * gh + 4096, p=HALF[x]), src[64 * gh:64 * gh + 64, :]) for x in range(2)],
+                 1048576 / GBW, [r], [])
+
+    dma(R("lsr"), T.ls[:], 65536, [R("lsr")], [])
+    dma(R("fpr"), T.fp[:], 20000, [R("fpr")], [])
+    dma(R("pxi", 0, 1024), T.px[:], 524288, [R("pxi", 0, 1024)], [])
+    load4("SG", T.sg)
+    dma(R("omi"), T.om[:], 30000, [R("omi")], [])
+    load4("CO", T.co)
     chain(list(range(len(ops))))
-    hist["fpr"].append((fp2, "S", R("fpr")["x"], R("fpr")["box"], True))
-    hist["pxr"].append((px2, "S", R("pxr")["x"], R("pxr")["box"], True))
 
+    eq = ALU.is_equal
     iota(R("pj", 0, 1), [[0, 1]], 0, 1)
-    iota(R("onef"), [[0, 256]], 1, 0)
-    sel(R("PL"), R("onef", 0, 128), [[-1, 16], [-16, 8]], ALU.is_equal, 0, 1)
-    sel(R("PR"), R("onef", 0, 128), [[1, 16], [-16, 8]], ALU.is_equal, 1, 1)
-    sel(R("PR", 0, 128, 8), R("onef", 0, 16), [[1, 16]], ALU.is_equal, -127, 1)
-    sel(R("If"), R("onef", 0, 128), [[-1, 128]], ALU.is_equal, 0, 1)
+    iota(R("onef"), [[0, 128]], 1, 0)
+    NG = 4 if TWO else 8
+    gp = lambda j: [[-64, 2], [j, 16], [-16, 4]] if TWO else [[j, 16], [-16, 8]]
+    sel(R("PL"), R("onef"), gp(-1), eq, 0, 1)
+    sel(R("PRb"), R("onef"), gp(1), eq, -15, 1)
+    sel(R("If"), R("onef"), [[-1, 128]], eq, 0, 1)
     sel(R("blk"), R("onef", 0, 8), [[-16, 8]], ALU.is_ge, 0, 1)
     sel(R("blk"), R("blk"), [[16, 8]], ALU.is_ge, 15, -1)
     ms(R("ones"), 1.0)
-    iota(R("omo"), [[1, 48]], 0, 0)
-    sel(R("E16", p=(0, 16)), R("ones", 0, 512, p=(0, 16)), [[0, 32], [-1, 16]], ALU.is_equal, 0, 1)
+    for q in range(2):
+        iota(R("Cst", 256 * q, 256 * q + 256), [[4096, 2], [4096, 2], [0, 64]], -128, 0)
+    iota(R("Cst", 0, 256, 16), [[4096, 2], [4096, 2], [0, 4]], 16384 - 128, 0)
+    iota(R("e2", 0, 48), [[1, 48]], 0, 0)
+    sel(R("E16", p=(0, 16)), R("ones", 0, 512, p=(0, 16)), [[0, 32], [-1, 16]], eq, 0, 1)
     sel(R("rst"), R("ones", 0, 256), [[0, 8], [1, 32]], ALU.is_gt, 0, 0)
     iota(R("sio"), [[0, 8], [1, 32]], 0, 0)
     sel(R("r16"), R("ones", 0, 128), [[0, 8], [1, 16]], ALU.is_gt, 0, 0)
     iota(R("cGy"), [[0, 8], [-1, 16]], 16, 0)
-    iota(R("ck"), [[512, 16], [0, 8]], 512 - 2 ** 24, 0)
-    sel(R("Sel", p=(0, 64)), R("ones", p=(0, 64)), [[-1, 8], [-8, 8], [0, 16]], ALU.is_equal, 0, 1)
-    sel(R("Sel", p=(64, 128)), R("ones", p=(64, 128)), [[-1, 8], [-8, 8], [0, 16]], ALU.is_equal, 0, 1)
+    iota(R("ck", 0, 16 * NG), [[512, 16], [0, NG]], 512 - 2 ** 24, 0)
+    sel(R("PRa"), R("onef"), gp(1), eq, 1, 1)
+    sel(R("PRa", 0, 16 * NG, NG), R("onef", 0, 16), [[1, 16]], eq, -127, 1)
+    if TWO:
+        sel(R("Lo1"), R("PRa"), [[0, 128]], ALU.is_ge, -64, 1)
+        sel(R("PRa"), R("PRa"), [[0, 128]], ALU.is_ge, 63, -1)
+    for x in range(2):
+        sel(R("Mm", 0, 256, p=HALF[x]), R("ones", 0, 256, p=HALF[x]), [[64, 2], [-1, 128]], eq, 0, 1)
+    if QUICK:
+        for x in range(2):
+            for u in range(0, 1024, 512):
+                sel(R("Sel", u, u + 512, p=HALF[x]), R("ones", 0, 512, p=HALF[x]), [[-1, 4], [-8, 8], [0, 16]], eq, -u // 128, 1)
+        act(R("cm"), R("onef"), scale=2.0 ** 18)
+    act(R("tr1", 0, 512), R("ones", 0, 512), scale=2.0 ** 25)
+    held = [[dma(T.Ld[:], R("tr1", 0, 512), 262144, [], [R("tr1", 0, 512)])]] * 2
     ts(R("pj", 1, 2), R("pj", 0, 1), 15, ALU.bitwise_and)
     jj = R("pj", 1, 2)
     ts(R("col", 0, 1), jj, 512.0, ALU.mult, -2.0 ** 24, ALU.add)
     ts(R("col", 1, 2), jj, 512.0, ALU.mult, 256.0 - 2.0 ** 24, ALU.add)
-    ts(R("col", 2, 3), jj, 0.5, ALU.is_gt)
-    ts(R("col", 3, 4), R("col", 2, 3), -4224.0, ALU.mult, 4096.0, ALU.add)
     ts(R("col", 4, 5), jj, 2.0, ALU.mult)
     act(R("Ib"), R("If"))
     act(R("I25"), R("If"), scale=2.0 ** 25)
-    act(R("nI"), R("If"), scale=-1.0)
-    act(R("nblk"), R("blk"), scale=-1.0)
-    act(R("RS", 0, 8), R("blk"), scale=-4096.0)
-    act(R("RS", 8, 16), R("blk"))
-    act(R("RA", 0, 8), R("blk"), scale=0.0)
-    act(R("RA", 8, 16), R("blk"), scale=-2.0)
-    act(R("I21"), R("If"), scale=S21)
-    act(R("nI17"), R("If"), scale=-2.0 ** -17)
-    act(R("cm"), R("onef", 0, 128), scale=-1.0 / 128)
-    act(R("d0c"), R("rst"), scale=2.0 ** 30, bias=-float(MM))
-    act(R("cG"), R("sio"), scale=-MM / HOLE, bias=32.0 * MM / HOLE)
-    act(R("b3", 128, 256), R("cGy"), scale=float(MM))
-    act(R("b3", 384, 512), R("ck"))
     act(R("hI"), R("If"), scale=0.5)
     act(R("nh"), R("If"), scale=-0.5)
-    act(R("cGy"), R("If"), scale=-2.0 ** -17)
-    ms(R("HR", 0, 256), 0.0)
-    ms(R("SG", 4096, 4112), 0.5)
-    ms(R("CO", 4096, 4112), 0.0)
-    for n in ("cA0", "cA1", "cB0", "cB1", "tr0", "tr1"):
-        ms(R(n, 4096, 4104), 0.0)
-    ms(R("lm", 0, 1), -1.0)
-    ms(R("dF", 0, 1), -1.0)
+    act(R("c14"), R("ones", 0, 256), scale=-128 * S21)
+    act(R("nI"), R("If"), scale=-1.0)
+    act(R("bk16", 0, 8), R("blk"))
+    act(R("bk16", 8, 16), R("blk"), scale=-1.0)
+    act(R("blkK"), R("blk"), scale=2.0 ** 25)
+    act(R("c3k"), R("ones", 0, 256), scale=ZC * 2.0 ** -25)
+    act(R("I25f"), R("If"), scale=2.0 ** -25)
+    if FKP:
+        for (u, c) in enumerate((2.0 ** 25, 2.0 ** 21, -2.0 ** 21)):
+            act(R("III", 128 * u, 128 * u + 128), R("If"), scale=c)
+        act(R("c3m"), R("onef"), scale=3072.0 * 2 ** 21)
+        x0, x1 = R("DM", 0, 16 * NG), R("DM", 128, 128 + 16 * NG)
+        iota(x0, [[1, 16], [0, NG]], 0, 0)
+        ts(x1, x0, float(MM), ALU.mult)
+        ts(x0, x1, 0x8888, ALU.bitwise_and)
+        ts(x1, x0, float(0x249), ALU.mult)
+        ts(x0, x1, 12, ALU.arith_shift_right, 15, ALU.bitwise_and)
+        ts(R("ckp", 0, 16 * NG), x0, 3064.0, ALU.add, -2.0 ** 25, ALU.mult)
+    tt(R("blk4", 0, 4), R("blk", 0, 4), R("blk", 4, 8), ALU.add)
+    tt(R("blk4", 4, 8), R("blk", 4, 8), R("blk", 0, 4), ALU.subtract)
+    act(R("RS", 4, 8), R("blk4", 4, 8), scale=-2.0 ** 30)
+    act(R("RS", 0, 4), R("blk4", 0, 4), scale=2.0 ** 42)
+    act(R("RS", 8, 12), R("blk4", 0, 4), scale=-2.0 ** 45)
+    act(R("RS", 12, 16), R("blk4", 0, 4), scale=0.0)
+    act(R("I21"), R("If"), scale=S21)
+    act(R("d0c"), R("rst"), scale=2.0 ** 30, bias=-float(MM))
+    act(R("cG"), R("sio"), scale=-MM / HOLE, bias=32.0 * MM / HOLE)
+    if TWO:
+        act(R("b0", 384, 448), R("cGy", 0, 64), scale=float(MM))
+        act(R("b0", 448, 512), R("ck", 0, 64))
+        ms(R("NO"), 0)
+    else:
+        act(R("b3", 128, 256), R("cGy"), scale=float(MM))
+        act(R("b2", 384, 512), R("ck"))
+    act(R("Mm", 256, 512), R("Mm", 0, 256), scale=-1.0)
+    ms(R("SG", 8192, 8208), 16.0)
+    ms(R("CO", 8192, 8208), 0.0)
+    for n in ("C0", "C1"):
+        ms(R(n, 8192, 8200), 0.0)
+    for n in ("tr0", "tr1", "tr2", "tr3"):
+        ms(R(n, 2048, 2056), 0.0)
+    ms(R("lm", 0, 512, 128), -2.0 ** 25)
     ms(R("NI"), 0.0)
     ms(R("LI"), 0.0)
     ts(R("mk2"), R("sio"), R("col", 4, 5), ALU.is_le)
     sel(R("mk2"), R("mk2"), [[0, 8], [1, 32]], ALU.is_gt, 0, 0)
-    sel(R("rs4"), R("ones", 0, 512), [[0, 16], [1, 32]], ALU.is_gt, 0, 0)
-    cp(R("omu"), R("omo"))
+    if "V" in TAU:
+        sel(R("rs4"), R("ones", 0, 512), [[0, 16], [1, 32]], ALU.is_gt, 0, 0)
+    iota(R("OMS", 0, 256), [[0, 256]], 0, 0)
+    iota(R("OMS", 256, 1536), [[0, 1280]], 0, 0)
+    cp(R("omu"), R("e2", 0, 48))
     cp(R("omf"), R("omi"))
-    act(R("OMB"), IND(R("omf"), R("omu")))
+    act(R("Eo", 1024, 1792), IND(R("omf"), R("omu")))
     mm([(R("b5"), R("E16", 0, 128, p=(0, 16)), R("E16", p=(0, 16)), True, True)])
-    tt(R("OMX", 0, 256), R("b5", 0, 256), R("OMB", 0, 256), ALU.mult)
-    tt(R("OMX", 256, 768), R("b5"), R("OMB", 256, 768), ALU.mult)
+    tt(R("Eo", 0, 256), R("b5", 0, 256), R("Eo", 1024, 1280), ALU.mult)
+    tt(R("Eo", 256, 768), R("b5"), R("Eo", 1280, 1792), ALU.mult)
+    for (k0, k1, bk) in ((0, 1, "b6"), (1, V, "b7")):
+        mm([(R(bk, 8 * k, 8 * k + 8), R("Eo", 128 * k, 128 * k + 128), R("blkK"), True, True) for k in range(k0, k1)])
+        act(R("OMS", 256 * k0, 256 * k1, 32), R(bk, 8 * k0, 8 * k1))
 
     def keys(out, src, n, ti, tf, c):
         ts(R(ti, 0, n), src, 0xFFF00, ALU.bitwise_and)
         ts(R(tf, 0, n), R(ti, 0, n), 31.0, ALU.mult, c, ALU.add)
         tt(out, R(tf, 0, n), src, ALU.add)
 
-    keys(R("LG"), R("lsr"), 128, "xi", "xt", R("col", 1, 2))
+    keys(R("LG"), R("lsr"), 128, "e", "dF", R("col", 1, 2))
+    ms(R("dF", 0, 256, 128), -1.0)
     mm([(R("b4", 0, 128), R("LG"), R("PL"), True, True)])
     cp(R("LL", 0, 128), R("b4", 0, 128))
     cp(R("NL", 0, 8), R("fpr"))
-    cp(R("g0"), IND(R("pxr"), R("NL", 0, 8)))
-    keys(R("PG"), R("g0"), 128, "k0i", "k0f", R("col", 0, 1))
+    cp(R("g0"), IND(R("pxi", 0, 1024), R("NL", 0, 8)))
+    keys(R("PG", 0, 128), R("g0"), 128, "k0i", "k0f", R("col", 0, 1))
     for a in range(0, 1024, 512):
-        ts(R("ti"), R("pxu", a, a + 512), 0xFFF00, ALU.bitwise_and)
-        ts(R("b6"), R("ti"), 3.0, ALU.mult, 256.0, ALU.add)
-        tt(R("PY", a, a + 512), R("b6"), R("pxu", a, a + 512), ALU.subtract)
-    for a in range(0, 1024, 512):
-        ts(R("ti"), R("pxr", a, a + 512), 0xFFF00, ALU.bitwise_and)
-        ts(R("b6"), R("ti"), 31.0, ALU.mult, R("col", 0, 1), ALU.add)
-        tt(R("KT", a, a + 512), R("b6"), R("pxr", a, a + 512), ALU.add)
+        px, hi = R("pxi", a, a + 512), R("tr3", 1024 + a, 1536 + a)
+        ts(hi, px, 127.5, ALU.subtract, 1.5 * 2.0 ** 31, ALU.add)
+        act(hi, hi, bias=-1.5 * 2.0 ** 31)
+        act(R("b5"), hi, scale=3.0, bias=256.0)
+        tt(R("PY", a, a + 512), R("b5"), px, ALU.subtract)
+        act(R("b6"), hi, scale=31.0, bias=R("col", 0, 1))
+        tt(R("tr3", a, a + 512), R("b6"), px, ALU.add)
+    dmas([(R("KT", p=(0, 112)), R("tr3", 0, 1024, p=(16, 128))), (R("KT", p=(112, 128)), R("tr3", 0, 1024, p=(0, 16)))],
+         524288 / GBW, [R("KT")], [R("tr3", 0, 1024)])
 
     nxt = T.cores[(rank + 1) % len(T.cores)]
     rid, pid = topo.addr(nxt)[0], topo.addr(nxt)[1]
@@ -313,186 +386,460 @@ def build(T, rank, core, topo):
         f = lambda g: g.remote_dma(ap(dst), ap(src), T.sem[sem], T.sem.sent, pid, rid, msk)
         nsent[0] += neng
         o = add("G", f, [], [src], 600, sem=("", 0))
-        return add("X", None, [dst], [], 0, lat=LAT + (1200 if src["dt"] == F32 else 0), after=[o], ext=(sem, neng), sem=("", 0))
+        return add("X", None, [dst], [], 0, lat=LAT + (8 * src["len"] + 200 if src["dt"] == F32 else 0), after=[o], ext=(sem, neng), sem=("", 0))
 
     mn, mx = ALU.min, ALU.max
-    P0, P1, P2, P3 = R("b0", 0, 256), R("b0", 256, 512), R("b1", 0, 256), R("b1", 256, 512)
-    fb = [0]
+    rot = {"s": [0, ("b4", "b4")], "d": [0, ("b5", "b6")]}
 
-    def fbank():
-        fb[0] += 1
-        return "b%d" % (4 + fb[0] % 3)
+    def bank(k):
+        rot[k][0] += 1
+        return rot[k][1][rot[k][0] % 2]
 
-    for v in range(V):
-        OF, S, cA, cB, tr = ["%s%d" % (n, v % 2) for n in ("OF", "S", "cA", "cB", "tr")]
+    def gathers(dst, win, o0, gh, l0, l1, nv, step, last):
+        for (e, p0, p1) in (("A", l0, l1 - nv), ("V", l1 - nv, l1)):
+            n = -(-(p1 - p0) // step)
+            cuts = [p0 + (p1 - p0) * k // max(n, 1) for k in range(n + 1)]
+            cuts = [128 * gh + a + a % 2 for a in cuts]
+            for (a, b) in zip(cuts, cuts[1:]):
+                for q in range(2):
+                    out = R(dst, 32 * a + q, 32 * b, 2)
+                    c = o0 + 128 * (gh + q)
+                    src = IND(R(win), R("OF", c + a, c + b))
+                    if dst != "X":
+                        o = (act if e == "A" else cp)(out, src)
+                    elif e == "A":
+                        o = act(out, src, scale=-2.0 ** -30)
+                    else:
+                        o = ts(out, src, -2.0 ** -30, ALU.mult)
+                    chain(last.get(e, []) + [o])
+                    last[e] = [o]
+
+    def whole(v):
+        tag[0] = ("w", v, 0)
+        o0, l0 = 512 * (v % 2), 256 * (v % 2)
+        lm = lambda a, b: R("lm", l0 + a, l0 + b)
         if v > 0:
-            act(R("PG"), IND(R("KT"), R("NL", 8 * v, 8 * v + 8)))
-        mm([(R("b3", 0, 128), R("PG"), R("PR"), True, True)])
+            act(R("PG", 0, 128), IND(R("KT"), R("NL", 8 * v, 8 * v + 8)))
+        mm([(R("b3", 0, 128), R("PG", 0, 128), R("PRa" if v > 0 else "PRb"), True, True)])
         lo, hi = ("LL", 128 * v), ("b3", 0)
         for st in range(4):
             nlo, nhi = ("Lo%d" % (st % 2), 0), ("b0", 128 * (st % 2))
             for (h0, dst) in ((0, nlo), (64, nhi)):
-                for (k, op) in ((0, mn), (1, mx)):
-                    tt(R(dst[0], dst[1] + k, dst[1] + 128, 2), R(lo[0], lo[1] + h0, lo[1] + h0 + 64),
+                for (u, op) in ((0, mn), (1, mx)):
+                    tt(R(dst[0], dst[1] + u, dst[1] + 128, 2), R(lo[0], lo[1] + h0, lo[1] + h0 + 64),
                        R(hi[0], hi[1] + h0, hi[1] + h0 + 64), op)
             lo, hi = nlo, nhi
-        for (k, op) in ((0, mn), (1, mx)):
-            tt(R("Ks", k, 256, 2), R(lo[0], lo[1], lo[1] + 128), R(hi[0], hi[1], hi[1] + 128), op)
+        for (u, op) in ((0, mn), (1, mx)):
+            tt(R("Ks", u, 256, 2), R(lo[0], lo[1], lo[1] + 128), R(hi[0], hi[1], hi[1] + 128), op)
         ts(R("fi"), R("Ks"), 511, ALU.bitwise_and)
-        ts(R("ZI", 0, 256), R("Ks"), 13, ALU.arith_shift_right)
+        ts(R("SL"), R("Ks"), S21, ALU.mult, 135.5 - 2.0 ** -14, ALU.add)
         ts(R("dA"), R("fi"), 256.0, ALU.subtract, S21, ALU.mult)
-        ms(R("ZI", 0, 257, 32), 2048)
-        ts(R("zs", 0, 257), R("ZI", 0, 257), 2048.5, ALU.add, 2.0 ** -12, ALU.mult)
-        act(R("fB"), R("dA"), bias=2.0 ** -13)
-        act(R("sl"), R("zs", 0, 256), scale=16.0, bias=127.5)
-        act(R("b1", 0, 257), R("zs", 0, 257), scale=4096.0, bias=-2048.5)
-        ts(R("qq"), R("dA"), 0.0, ALU.is_lt)
-        scan(R("A"), R("qq"), R("dA"), 0.0, mn, mx)
-        scan(R("B"), R("qq"), R("fB"), 0.0, ALU.add, mn)
-        for h in range(2):
-            lst = []
-            for k, n in enumerate("AB"):
-                o = R("b2", 256 * h + 128 * k, 256 * h + 128 * k + 128)
-                lst += [(o, R("sl", h, 256, 2), R("Ib"), True, False), (o, R(n, h, 256, 2), R("I25"), False, True)]
-            mm(lst)
-        ts(R(OF, 0, 256), R("b2", 0, 256), R("col", 2, 3), ALU.mult, R("col", 3, 4), ALU.add)
-        ts(R(OF, 256, 512), R("b2", 256, 512), -128.0, ALU.add)
-        tt(R("ln"), R("b1", 1, 257), R("ZI", 0, 256), ALU.subtract)
+        if QQF:
+            ts(R("qq"), R("fi"), 256.0, ALU.is_lt)
+        else:
+            ts(R("qq"), R("dA"), 0.0, ALU.is_lt)
+        ts(R("zs", 0, 256), R("Ks"), 4096.0, ALU.subtract, ZC + 2.0 ** 24, ALU.add)
+        act(R("zs", 0, 257, 32), R("onef", 0, 9), scale=ZC + 2.0 ** 25)
+        A = [R("AB", 256 * gh, 256 * gh + 128) for gh in range(2)]
+        Bm = [R("AB", 256 * gh + 128, 256 * gh + 256) for gh in range(2)]
+        for gh in range(2):
+            c = 128 * gh
+            scan(A[gh], R("qq", c, c + 128), R("dA", c, c + 128), 0.0, mn, mx)
+            scan(Bm[gh], R("qq", c, c + 128), R("dA", c, c + 128), 0.0, ALU.add, mn)
+        qg = [(q, gh, 256 * q + 128 * gh) for gh in range(2) for q in range(2)]
+        mm([(R("b1", c, c + 128), R("Cst", c, c + 128), R("Ib"), c == 0, False) for (q, gh, c) in qg])
+        mm([(R("b1", c, c + 128, p=HALF[x]), R("SL", 128 * gh + q, 128 * gh + 128, 2), R("Ib"), False, False)
+            for (q, gh, c) in qg for x in range(2)])
+        mm([(R("b1", c, c + 128), R("AB", 256 * gh + q, 256 * gh + 256, 2), R("I25"), False, c == 384) for (q, gh, c) in qg])
+        for (q, gh, c) in qg:
+            d = o0 + 256 * gh + 128 * q
+            ts(R("OF", d, d + 128), R("b1", c, c + 128), 8192.0, mn)
+        scan(R("ln"), R("zs", 1, 257), R("zs", 0, 256), 0.0, mx, ALU.subtract)
+        P2, P3 = R("b2", 0, 256), R("b3", 256, 512)
         if v < V - 1:
-            mm([(P2, R("If"), R("zs", 0, 256), True, False)])
-            mm([(P2, R("nh"), R("A"), False, False), (P2, R("nh"), R("B"), False, True),
-                (P3, R("hI"), R("A"), True, False), (P3, R("nh"), R("B"), False, True)])
-        mm([(R("b2", 0, 256, 32), R("OMX", 128 * v, 128 * v + 128), R("nblk"), True, False)])
-        ga, gb = [], []
-        for h in range(2):
-            for (l0, l1) in (GCH if h == 0 else [(0, 64), (64, 128)]):
-                c0, c1 = 2048 * h + 16 * l0, 2048 * h + 16 * l1
-                ga.append(act(R("xA", c0, c1), IND(R("SG"), R(OF, 256 * h + l0, 256 * h + l1))))
-                src = IND(R("SG"), R(OF, 256 * h + 128 + l0, 256 * h + 128 + l1))
-                gb.append(tt(R(S, c0, c1), src, R("xA", c0, c1), ALU.add))
-            chain(ga)
-            chain(gb)
-            ss = [s for s in range(h, 32, 2) if s > 0]
+            hv = [(gh, 128 * gh) for gh in range(2)]
+            mm([(P2, R("nI"), R("c3k"), True, False), (P2, R("I25f"), R("zs", 0, 256), False, False)])
+            mm([(P2, R("nI"), R("c14"), False, False)]
+               + [(R("b2", c, c + 128), R("nh"), z[gh], False, z is Bm and gh == 1 and not P1P) for z in (A, Bm) for (gh, c) in hv])
+            mm([(P3, R("Ib"), R("c14"), u == 0, False) for u in range(2 if GTV else 1)]
+               + [(R("b3", 256 + c, 384 + c), R("Ib" if GTV else "hI"), A[gh], False, False) for (gh, c) in hv]
+               + [(R("b3", 256 + c, 384 + c), R("nI" if GTV else "nh"), Bm[gh], False, gh == 1) for (gh, c) in hv])
+        n = 8 if v < V - 1 else 4
+        last = {}
+        for gh in range(2):
+            gathers("X", "SG", o0, gh, 0, 128, SGV[v], GCH, last)
+            c, d = 256 * gh, 128 * gh
+            mm([(R("b1", c + s, c + 32 * n, 32), R("X", 4096 * gh + s, 4096 * gh + 4096, 32),
+                 R("RS", 8 * (s == 0), 8 * (s == 0) + n), s == 0, s == 31) for s in range(32)])
+            tt(R("w", d, d + 128), R("b1", c, c + 128), R("ln", d, d + 128), ALU.mult)
             if v < V - 1:
-                mm([(R("b2", s, 512, 32), R("xA", 2048 * h + s // 2, 2048 * h + 2048, 16), R("RA"), False, False) for s in ss])
-            mm([(R("b2", s, 512 if v < V - 1 else 256, 32), R(S, 2048 * h + s // 2, 2048 * h + 2048, 16),
-                 R("RS", 0, 16 if v < V - 1 else 8), False, s == 31) for s in ss])
-        tt(R("w"), R("b2", 0, 256), R("ln"), ALU.mult)
-        if v < V - 1:
-            act(R("gt"), R("b2", 256, 512), ACT.Sign, bias=-0.5)
-        scan(P0, R("rst"), R("w"), 0.0, ALU.mult, ALU.add)
-        tt(R("lm", 1, 256), R("b0", 0, 255), R("ln", 1, 256), mn)
-        if v < V - 1:
-            tt(R("mm"), P3, R("gt"), ALU.mult)
-            tt(P1, P2, R("mm"), ALU.add)
-            tt(R("lk"), P1, R("lm"), mn)
-            scan(P0, R("rst"), R("lk"), 0.0, ALU.mult, mx)
-            last = R("b0", 31, 256, 32)
-            li, a1, a2 = R("li", 0, 8), R("li", 8, 16), R("li", 16, 24)
-            ts(li, last, 2.0 ** 21, ALU.mult)
-            ts(a1, li, 511, ALU.bitwise_and)
-            ts(a2, li, 19, ALU.arith_shift_right)
-            ts(R("a3"), a1, -4.0, ALU.mult, 1024.0, ALU.add)
-            tt(R("NI", 0, 256, 32), R("a3"), a2, ALU.add)
-            scan(R("AN"), R("mk2"), R("NI"), 0.0, ALU.mult, ALU.add)
-            mm([(R("b3", 0, 8), R("AN", 0, 256, 2), R("blk"), True, False),
-                (R("b3", 0, 8), R("AN", 1, 256, 2), R("nblk"), False, True)])
-            no = R("NO", 8 * v, 8 * v + 8)
-            cp(no, R("b3", 0, 8))
-            send(R("NL", 8 * v + 8, 8 * v + 16), no, "nm%d" % (v + 1))
-            act(R("YG"), IND(R("PY"), no))
-            yps = R("b3", 256, 384)
-            mm([(yps, R("YG"), R("I21"), True, True)])
-            tt(R("dF", 1, 256), R("lk", 1, 256), R("b0", 0, 255), ALU.subtract)
-            ts(R("LI", 0, 128, 16), last, 256.5 * S21, ALU.add)
-            ts(R("e"), R("dF"), 0.0, mx, 2.0 ** 21, ALU.mult)
-            ts(R("e2"), R("e"), 511, ALU.bitwise_and)
-            ts(R("nn"), R("e2"), 1.0, mn, float(MM), ALU.mult)
-            act(P2, R("nn"), ACT.Relu, scale=-2.0 / MM, bias=HOLE)
-            scan(P1, R("d0c"), R("nn"), -float(MM), mn, ALU.add)
-            tt(R("G"), P2, R("cG"), ALU.mult)
-            tt(R3("PN", 0, 32), P2, R("lk"), mx)
-            tt(R3("DM", 0, 32), P1, R("G"), ALU.add)
-            scan(R("LB"), R("r16"), R("LI"), 0.0, ALU.mult, ALU.add)
-            tt(R("nl"), yps, R("LB"), ALU.is_le)
+                if GTV:
+                    ts(R("gt", d, d + 128), R("b1", c + 128, c + 256), 0.5, ALU.is_gt, 0.5, ALU.subtract)
+                else:
+                    act(R("gt", d, d + 128), R("b1", c + 128, c + 256), ACT.Sign, bias=-0.5)
+        scan(R("b0", 0, 256), R("w"), R("OMS", 256 * v, 256 * v + 256), 0.0, ALU.add, mx)
+        tt(lm(1, 256), R("b0", 0, 255), R("ln", 1, 256), mn)
+        if v == V - 1:
+            return
+        tt(R("mm"), P3, R("gt"), ALU.mult)
+        if P1P:
+            mm([(P2, R("Ib"), R("mm"), False, True)])
+        else:
+            tt(P2, P2, R("mm"), ALU.add)
+        tt(R("lk"), P2, lm(0, 256), mn)
+        scan(R("b0", 256, 512), R("rst"), R("lk"), 0.0, ALU.mult, mx)
+        last = R("b0", 256 + 31, 512, 32)
+        li, a1, a2 = R("li", 0, 8), R("li", 8, 16), R("li", 16, 24)
+        ts(li, last, 2.0 ** 23, ALU.mult)
+        ts(a1, li, 0x7FC, ALU.bitwise_and)
+        ts(a2, li, 21, ALU.arith_shift_right)
+        tt(R("NI", 0, 256, 32), a2, a1, ALU.subtract)
+        scan(R("AN"), R("mk2"), R("NI"), 0.0, ALU.mult, ALU.add)
+        mm([(R("b3", 0, 8), R("AN", 0, 256, 2), R("bk16", 0, 8), True, False),
+            (R("b3", 0, 8), R("AN", 1, 256, 2), R("bk16", 8, 16), False, True)])
+        no = R("NO", 8 * v, 8 * v + 8)
+        ts(no, R("b3", 0, 8), 1024.0, ALU.add)
+        send(R("NL", 8 * v + 8, 8 * v + 16), no, "nm%d" % (v + 1))
+        act(R("YG0"), IND(R("PY"), no))
+        yps = R("b3", 256, 384)
+        mm([(yps, R("YG0"), R("I21"), True, True)])
+        tt(R("dF", 1, 256), R("lk", 1, 256), R("b0", 256, 511), ALU.subtract)
+        ts(R("LI", 0, 128, 16), last, 256.5 * S21, ALU.add)
+        ts(R("e"), R("dF"), 0.0, mx, 2.0 ** 21, ALU.mult)
+        ts(R("e2"), R("e"), 511, ALU.bitwise_and)
+        ts(R("nn"), R("e2"), 1.0, mn, float(MM), ALU.mult)
+        hole = R("b2", 0, 256)
+        if HOV:
+            ts(hole, R("e2"), 0.0, eq, HOLE, ALU.mult)
+        else:
+            act(hole, R("nn"), ACT.Relu, scale=-2.0 / MM, bias=HOLE)
+        scan(R("b0", 0, 256), R("d0c"), R("nn"), -float(MM), mn, ALU.add)
+        tt(R("G"), hole, R("cG"), ALU.mult)
+        tt(R("PN", 0, 256), hole, R("lk"), mx)
+        tt(R("DM", 0, 256), R("b0", 0, 256), R("G"), ALU.add)
+        scan(R("LB"), R("r16"), R("LI"), 0.0, ALU.mult, ALU.add)
+        tt(R("nl"), yps, R("LB"), ALU.is_le)
+        if LTA:
+            act(R("lt"), R("nl"), scale=-float(MM), bias=float(MM))
+        else:
             ts(R("lt"), R("nl"), -float(MM), ALU.mult, float(MM), ALU.add)
-            ts(R("lt", 0, 128, 16), R("b0", 256 + 31, 512, 32), 15.0 * MM, mn)
-            scan(R("b1", 256, 384), R("r16"), R("lt"), 0.0, ALU.mult, ALU.add)
-            tt(R("Gy"), R("b3", 128, 256), R("nl"), ALU.mult)
-            tt(R3("PN", 32, 48), yps, R("nl"), mx)
-            tt(R3("DM", 32, 48), R("b1", 256, 384), R("Gy"), ALU.add)
-            act(R("b1", 0, 384), R3("PN", 0, 48), bias=-8.0)
-            ts(R("y2"), R3("DM", 0, 48), 0x8888, ALU.bitwise_and)
-            ts(R("y3"), R("y2"), float(0x249), ALU.mult)
-            ts(R("y4"), R("y3"), 12, ALU.arith_shift_right, 15, ALU.bitwise_and)
-            tt(R("E0"), R("b1", 0, 384, 2), R("y4", 0, 384, 2), ALU.add)
-            tt(R("b0", 0, 192), R("b1", 1, 384, 2), R("y4", 1, 384, 2), ALU.add)
-            for st in range(3):
-                e0, e1, o0, o1 = "E%d" % (st % 2), "E%d" % (1 - st % 2), 256 * (st % 2), 256 * (1 - st % 2)
-                for (k, dn, d0) in ((0, e1, 0), (1, "b0", o1)):
-                    for (u, op) in ((0, mn), (96, mx)):
-                        tt(R(dn, d0 + u, d0 + u + 96), R(e0, k, 192, 2), R("b0", o0 + k, o0 + 192, 2), op)
-            tt(R("Z", 0, 192), R("E1"), R("b0", 256, 448), mn)
-            tt(R("Z", 192, 384), R("E1"), R("b0", 256, 448), mx)
-            tt(R("b0", 0, 128), R("Z", 0, 384, 3), R("Z", 1, 384, 3), mn)
-            tt(R("XF"), R("b0", 0, 128), R("Z", 2, 384, 3), mn)
-            ts(R("xi"), R("XF"), 2.0 ** 25, ALU.mult)
-            ts(R("xl"), R("xi"), 4, ALU.arith_shift_right, 511, ALU.bitwise_and)
-            ts(R("xh"), R("xi"), 0x1FFE000, ALU.bitwise_and)
-            tt(R("b0", 128, 256), R("b3", 384, 512), R("xl"), ALU.subtract)
-            tt(R("LS", 128 * v, 128 * v + 128), R("b0", 128, 256), R("xh"), ALU.add)
-            send(R("LL", 128 * v + 128, 128 * v + 256), R("LS", 128 * v, 128 * v + 128), "li%d" % (v + 1))
-        act(R("HL", 0, 256), R("lm"), ACT.Relu)
-        act(R("HR", 256, 512), R("lm"), ACT.Relu)
-        act(R("HL", 256, 512), R("HL", 0, 256), scale=-1.0)
-        for u in range(4):
-            o = R("b2", 128 * u, 128 * u + 128)
-            mm([(o, R("HR", u, 512, 4), R("cGy"), True, False), (o, R("HL", u, 512, 4), R("nI17"), False, True)])
-        LT = "LT%d" % (v % 2)
-        act(R(LT), R("b2"))
-        for hf in (1, 0):
-            for h in range(2):
-                for (n, k) in ((cA, 0), (cB, 128)):
-                    (cp if (v == V - 1 and n == cB and hf in COV) else act)(
-                        R(n, 2048 * hf + h, 2048 * hf + 2048, 2),
-                        IND(R("CO"), R(OF, 256 * h + k + 64 * hf, 256 * h + k + 64 * hf + 64)))
-            for q in range(4):
-                bk = fbank()
-                lst = []
-                for t in range(8):
-                    if q == 0 and t == 0:
-                        lst.append((R(bk, 0, 512, 8), R("cm"), R("ones", 0, 64), True, True))
-                    else:
-                        lst.append((R(bk, t, 512, 8), R("Sel", 128 * t, 128 * t + 128),
-                                    R(LT, 128 * q + 64 * hf, 128 * q + 64 * hf + 64), True, True))
-                mm(lst)
-                c0 = 2048 * (q % 2) + 1024 * hf
-                tt(R(tr, 2048 * hf + q, 2048 * hf + 2048, 4), R(bk), R(S, c0 + q // 2, c0 + 1024, 2), ALU.mult)
-            for a in (2048 * hf + 1024, 2048 * hf):
-                act(R(tr, a, a + 1024), R(tr, a, a + 1024), bias=1.0)
-            for c in range(4 * hf + 3, 4 * hf - 1, -1):
-                bk = fbank()
-                a = 512 * c
-                mm([(R(bk), R("Ib"), R(cA, a + 1, a + 513), True, False)])
-                mm([(R(bk), R("Ib"), R(cB, a + 1, a + 513), False, False)])
-                mm([(R(bk), R("nI"), R(cA, a, a + 512), False, False)])
-                mm([(R(bk), R("nI"), R(cB, a, a + 512), False, True)])
-                scan(R("Eo", a + 512, a, -1), R(tr, a + 512, a, -1), R(bk, 511, -1, -1), 0.0, ALU.mult, ALU.add)
-            o = 128 * v + 64 * hf
-            act(R("YC", o, o + 64), R("Eo", 2048 * hf + 1, 2048 * hf + 2048, 32))
-            if (2 * v + 1 - hf < YTP and hf in YTH) or (v, hf) in YTX:
-                for s0 in range(1, 32, 2):
-                    mm([(R("b7", 256 + 64 * hf, 320 + 64 * hf), R("If"), R(tr, 2048 * hf + s, 2048 * hf + 2048, 32),
-                         s == 1, s == 31) for s in range(s0, min(s0 + 2, 32))])
-                act(R("YT", o, o + 64), R("b7", 256 + 64 * hf, 320 + 64 * hf), scale=-8.0, bias=248.0)
+        ts(R("lt", 0, 128, 16), R("b0", 31, 256, 32), 15.0 * MM, mn)
+        scan(R("b0", 256, 384), R("r16"), R("lt"), 0.0, ALU.mult, ALU.add)
+        tt(R("Gy"), R("b3", 128, 256), R("nl"), ALU.mult)
+        tt(R("PN", 256, 384), yps, R("nl"), mx)
+        tt(R("DM", 256, 384), R("b0", 256, 384), R("Gy"), ALU.add)
+        act(R("b2", 0, 384), R("PN"), bias=-8.0)
+        for (a, b) in YSP:
+            ts(R("y2", a, b), R("DM", a, b), 0x8888, ALU.bitwise_and)
+            ts(R("y3", a, b), R("y2", a, b), float(0x249), ALU.mult)
+            ts(R("y4", a, b), R("y3", a, b), 12, ALU.arith_shift_right, 15, ALU.bitwise_and)
+        tt(R("E0"), R("b2", 0, 384, 2), R("y4", 0, 384, 2), ALU.add)
+        tt(R("b0", 0, 192), R("b2", 1, 384, 2), R("y4", 1, 384, 2), ALU.add)
+        for st in range(3):
+            e0, e1, q0, q1 = "E%d" % (st % 2), "E%d" % (1 - st % 2), 256 * (st % 2), 256 * (1 - st % 2)
+            for (u, dn, d0) in ((0, e1, 0), (1, "b0", q1)):
+                for (d, op) in ((0, mn), (96, mx)):
+                    tt(R(dn, d0 + d, d0 + d + 96), R(e0, u, 192, 2), R("b0", q0 + u, q0 + 192, 2), op)
+        tt(R3("Z", 0, 8, 0, 24), R("E1"), R("b0", 256, 448), mn)
+        tt(R3("Z", 8, 16, 0, 24), R("E1"), R("b0", 256, 448), mx)
+        tt(R("b0", 0, 128), R3("Z", 0, 16, 0, 16, 2), R3("Z", 0, 16, 1, 16, 2), mn)
+        tt(R("XF"), R("b0", 0, 128), R3("Z", 0, 16, 16, 24), mn)
+        ls = R("LS", 128 * v, 128 * v + 128)
+        if FKP:
+            ts(R("xr"), R("XF"), 128 * S21, ALU.subtract, 3072.0, ALU.add)
+            o = R("b1", 0, 128)
+            mm([(o, R("If"), R("ckp"), True, False)])
+            mm([(o, R("III", 0, 128), R("xr"), False, False),
+                (o, R("If"), R("ck"), False, False), (o, R("III", 128, 256), R("xr"), False, False),
+                (o, R("nI"), R("c3m"), False, False), (o, R("III", 256, 384), R("XF"), False, True)])
+            act(ls, o)
+        else:
+            xi, xl, xh = R("y2", 0, 128), R("y2", 128, 256), R("y2", 256, 384)
+            ts(xi, R("XF"), 2.0 ** 25, ALU.mult)
+            ts(xl, xi, 4, ALU.arith_shift_right, 511, ALU.bitwise_and)
+            ts(xh, xi, 0x1FFE000, ALU.bitwise_and)
+            tt(R("b0", 128, 256), R("b2", 384, 512), xl, ALU.subtract)
+            tt(ls, R("b0", 128, 256), xh, ALU.add)
+        send(R("LL", 128 * v + 128, 128 * v + 256), ls, "li%d" % (v + 1))
+
+    def whole2(v, h):
+        k = 2 * v + h
+        tag[0] = ("w", v, h)
+
+        def W(name, a=0, b=None, s=1):
+            n = SCRATCH[name][1][1] // 2
+            return R(name, n * h + a, n * h + (n if b is None else b), s)
+
+        def Q(a, b, s=1):
+            return R("b0", 192 * h + a, 192 * h + b, s)
+
+        def B(a, b, s=1, p=None):
+            return R("b%d" % (1 + h), a, b, s, p)
+
+        def first(name, n):
+            return R(name, 0, n)
+
+        o0, l0 = 512 * (v % 2), 256 * (v % 2) + 128 * h
+        lm = lambda a, b: R("lm", l0 + a, l0 + b)
+        if v > 0 and h == 0:
+            for u in range(2):
+                act(R("PG", 128 * u, 128 * u + 128), IND(R("KT"), R("NL", 16 * v + 8 * u, 16 * v + 8 * u + 8)))
+        if v > 0:
+            mm([(B(0, 64), R("PG", 128 * u, 128 * u + 128), R(("PRa", "Lo1")[u], 64 * h, 64 * h + 64), u == 0, u == 1)
+                for u in range(2)])
+        else:
+            mm([(B(0, 64), R("PG", 0, 128), R("PRb", 64 * h, 64 * h + 64), True, True)])
+        lo, hi = R("LL", 64 * k, 64 * k + 64), B(0, 64)
+        for st in range(2):
+            for (u, op) in ((0, mn), (1, mx)):
+                tt(W("M0", u, 128, 2), lo, hi, op)
+            for (u, op) in ((0, mn), (1, mx)):
+                tt(W("Lo0", u, 64, 2), W("M0", 0, 32), W("M0", 64, 96), op)
+                tt(Q(u, 64, 2), W("M0", 32, 64), W("M0", 96, 128), op)
+            lo, hi = W("Lo0"), Q(0, 64)
+        for (u, op) in ((0, mn), (1, mx)):
+            tt(W("Ks", u, 128, 2), lo, hi, op)
+        ts(W("fi"), W("Ks"), 511, ALU.bitwise_and)
+        ts(W("dA"), W("fi"), 256.0, ALU.subtract, S21, ALU.mult)
+        ts(W("SL"), W("Ks"), S21, ALU.mult, 135.5 - 2.0 ** -14, ALU.add)
+        ts(W("zs", 0, 128), W("Ks"), 4096.0, ALU.subtract, ZC + 2.0 ** 24, ALU.add)
+        act(W("zs", 0, 129, 32), R("onef", 0, 5), scale=ZC + 2.0 ** 25)
+        if QQF:
+            ts(W("qq"), W("fi"), 256.0, ALU.is_lt)
+        else:
+            ts(W("qq"), W("dA"), 0.0, ALU.is_lt)
+        A, Bm = W("AB", 0, 128), W("AB", 128, 256)
+        scan(A, W("qq"), W("dA"), 0.0, mn, mx)
+        scan(Bm, W("qq"), W("dA"), 0.0, ALU.add, mn)
+        mm([(B(128 * q, 128 * q + 128), R("Cst", 256 * q + 128 * h, 256 * q + 128 * h + 128), R("Ib"), q == 0, False)
+            for q in range(2)])
+        mm([(B(128 * q, 128 * q + 128, p=HALF[x]), W("SL", q, 128, 2), R("Ib"), False, False)
+            for q in range(2) for x in range(2)])
+        mm([(B(128 * q, 128 * q + 128), W("AB", q, 256, 2), R("I25"), False, q == 1) for q in range(2)])
+        ts(R("OF", o0 + 256 * h, o0 + 256 * h + 256), B(0, 256), 8192.0, mn)
+        scan(W("ln"), W("zs", 1, 129), W("zs", 0, 128), 0.0, mx, ALU.subtract)
+        P2, P3 = R("b%d" % (3 + h), 0, 128), B(384, 512)
+        if v < V - 1:
+            mm([(P2, R("nI"), first("c3k", 128), True, False), (P2, R("I25f"), W("zs", 0, 128), False, False),
+                (P2, R("nI"), first("c14", 128), False, False), (P2, R("nh"), A, False, False),
+                (P2, R("nh"), Bm, False, not P1P)])
+            mm([(P3, R("Ib" if GTV else "hI"), A, True, False), (P3, R("nI" if GTV else "nh"), Bm, False, False)]
+               + [(P3, R("Ib"), first("c14", 128), False, u == 0) for u in range(1 if GTV else 0, -1, -1)])
+        gathers("X", "SG", o0, h, 0, 128, SGV[v], GCH, {})
+        n = 8 if v < V - 1 else 4
+        mm([(B(s, 32 * n, 32), R("X", 4096 * h + s, 4096 * h + 4096, 32), R("RS", 8 * (s == 0), 8 * (s == 0) + n),
+             s == 0, s == 31) for s in range(32)])
+        tt(W("w"), B(0, 128), W("ln"), ALU.mult)
+        if v < V - 1:
+            if GTV:
+                ts(W("gt"), B(128, 256), 0.5, ALU.is_gt, 0.5, ALU.subtract)
             else:
-                for a in range(2048 * hf, 2048 * hf + 2048, 512):
-                    scan(R("E2", a % 2048, a % 2048 + 512), R("rs4"), R(tr, a, a + 512), 0.0, ALU.mult, ALU.add)
-                act(R("YT", o, o + 64), R("E2", 31, 2048, 32), scale=-8.0, bias=248.0)
-        o = 128 * v
-        dma("S", T.yc[:, o:o + 128], R("YC", o, o + 128), 65536, [], [R("YC", o, o + 128)])
-        dma("S", T.yt[:, o:o + 128], R("YT", o, o + 128), 65536, [], [R("YT", o, o + 128)])
+                act(W("gt"), B(128, 256), ACT.Sign, bias=-0.5)
+        scan(Q(0, 128), W("w"), R("OMS", 128 * k, 128 * k + 128), 0.0, ALU.add, mx)
+        tt(lm(1, 128), Q(0, 127), W("ln", 1, 128), mn)
+        if v == V - 1:
+            return
+        tt(W("mm"), P3, W("gt"), ALU.mult)
+        if P1P:
+            mm([(P2, R("Ib"), W("mm"), False, True)])
+        else:
+            tt(P2, P2, W("mm"), ALU.add)
+        tt(W("lk"), P2, lm(0, 128), mn)
+        scan(Q(0, 128), first("rst", 128), W("lk"), 0.0, ALU.mult, mx)
+        last = Q(31, 128, 32)
+        li, a1, a2 = W("li", 0, 4), W("li", 4, 8), W("li", 8, 12)
+        ts(li, last, 2.0 ** 23, ALU.mult)
+        ts(a1, li, 0x7FC, ALU.bitwise_and)
+        ts(a2, li, 21, ALU.arith_shift_right)
+        tt(W("NI", 0, 128, 32), a2, a1, ALU.subtract)
+        scan(W("AN"), first("mk2", 128), W("NI"), 0.0, ALU.mult, ALU.add)
+        tt(W("dF", 1, 128), W("lk", 1, 128), Q(0, 127), ALU.subtract)
+        ts(W("LI", 0, 64, 16), last, 256.5 * S21, ALU.add)
+        ts(W("e"), W("dF"), 0.0, mx, 2.0 ** 21, ALU.mult)
+        ts(W("e2"), W("e"), 511, ALU.bitwise_and)
+        ts(W("nn"), W("e2"), 1.0, mn, float(MM), ALU.mult)
+        o = B(0, 8, p=HALF[h])
+        mm([(o, W("AN", 0, 128, 2), R("bk16", 0, 8), True, False), (o, W("AN", 1, 128, 2), R("bk16", 8, 16), False, True)])
+        no = R("NO", 8 * k, 8 * k + 8)
+        ts(R("NO", 8 * k, 8 * k + 8, p=HALF[h]), o, 1024.0, ALU.add)
+        send(R("NL", 8 * k + 16, 8 * k + 24), no, "nm%d" % (k + 2))
+        act(R("YG%d" % h), IND(R("PY"), no))
+        hole = R("b%d" % (3 + h), 128, 256)
+        if HOV:
+            ts(hole, W("e2"), 0.0, eq, HOLE, ALU.mult)
+        else:
+            act(hole, W("nn"), ACT.Relu, scale=-2.0 / MM, bias=HOLE)
+        scan(Q(0, 128), first("d0c", 128), W("nn"), -float(MM), mn, ALU.add)
+        tt(W("G"), hole, first("cG", 128), ALU.mult)
+        tt(W("PN", 0, 128), hole, W("lk"), mx)
+        tt(W("DM", 0, 128), Q(0, 128), W("G"), ALU.add)
+        yps = B(0, 64)
+        mm([(yps, R("YG%d" % h), R("I21", 64 * h, 64 * h + 64), True, True)])
+        scan(W("LB"), first("r16", 64), W("LI"), 0.0, ALU.mult, ALU.add)
+        tt(W("nl"), yps, W("LB"), ALU.is_le)
+        if LTA:
+            act(W("lt"), W("nl"), scale=-float(MM), bias=float(MM))
+        else:
+            ts(W("lt"), W("nl"), -float(MM), ALU.mult, float(MM), ALU.add)
+        ts(W("lt", 0, 64, 16), Q(31, 128, 32), 15.0 * MM, mn)
+        scan(Q(128, 192), first("r16", 64), W("lt"), 0.0, ALU.mult, ALU.add)
+        tt(W("Gy"), R("b0", 384, 448), W("nl"), ALU.mult)
+        tt(W("PN", 128, 192), yps, W("nl"), mx)
+        tt(W("DM", 128, 192), Q(128, 192), W("Gy"), ALU.add)
+        act(B(0, 192), W("PN"), bias=-8.0)
+        Y = lambda n, a=0, b=192, s=1: R("pxi", 384 * n + 192 * h + a, 384 * n + 192 * h + b, s)
+        ts(Y(0), W("DM"), 0x8888, ALU.bitwise_and)
+        ts(Y(1), Y(0), float(0x249), ALU.mult)
+        ts(Y(2), Y(1), 12, ALU.arith_shift_right, 15, ALU.bitwise_and)
+        tt(W("E0"), B(0, 192, 2), Y(2, 0, 192, 2), ALU.add)
+        tt(Q(0, 96), B(1, 192, 2), Y(2, 1, 192, 2), ALU.add)
+        for st in range(3):
+            e0, e1, q0, q1 = "E%d" % (st % 2), "E%d" % (1 - st % 2), 96 * (st % 2), 96 * (1 - st % 2)
+            for u in range(2):
+                for (d, op) in ((0, mn), (48, mx)):
+                    dst = W(e1, d, d + 48) if u == 0 else Q(q1 + d, q1 + d + 48)
+                    tt(dst, W(e0, u, 96, 2), Q(q0 + u, q0 + 96, 2), op)
+        z0 = 16 * h
+        tt(R3("Z2", z0, z0 + 8, 0, 12), W("E1"), Q(96, 192), mn)
+        tt(R3("Z2", z0 + 8, z0 + 16, 0, 12), W("E1"), Q(96, 192), mx)
+        tt(Q(0, 64), R3("Z2", z0, z0 + 16, 0, 8, 2), R3("Z2", z0, z0 + 16, 1, 8, 2), mn)
+        tt(W("XF"), Q(0, 64), R3("Z2", z0, z0 + 16, 8, 12), mn)
+        ls = R("LS", 64 * k, 64 * k + 64)
+        if FKP:
+            ts(W("xr"), W("XF"), 128 * S21, ALU.subtract, 3072.0, ALU.add)
+            o = B(256, 320)
+            mm([(o, R("If"), first("ckp", 64), True, False)])
+            mm([(o, R("III", 0, 128), W("xr"), False, False),
+                (o, R("If"), first("ck", 64), False, False), (o, R("III", 128, 256), W("xr"), False, False),
+                (o, R("nI"), first("c3m", 64), False, False), (o, R("III", 256, 384), W("XF"), False, True)])
+            act(ls, o)
+        else:
+            xi, xl, xh = Y(0, 0, 64), Y(0, 64, 128), Y(0, 128, 192)
+            ts(xi, W("XF"), 2.0 ** 25, ALU.mult)
+            ts(xl, xi, 4, ALU.arith_shift_right, 511, ALU.bitwise_and)
+            ts(xh, xi, 0x1FFE000, ALU.bitwise_and)
+            tt(Q(64, 128), R("b0", 448, 512), xl, ALU.subtract)
+            tt(ls, Q(64, 128), xh, ALU.add)
+        send(R("LL", 64 * k + 128, 64 * k + 192), ls, "li%d" % (k + 2))
+
+    def spread(v):
+        tag[0] = ("f", v, 0)
+        l0 = 256 * (v % 2)
+        if SUM[v] == "D":
+            old, new = list(hist.get("S", [])), []
+            for gh in range(2):
+                hist["S"] = list(old)
+                c, d = 4096 * gh, R("S", p=HALF[gh])
+                dma(d, R("X", c, c + 4096, p=HALF[0]), 524288, [d], [R("X", c, c + 4096)])
+                gadd(d, R("X", c, c + 4096, p=HALF[1]), 524288)
+                new += hist["S"][len(old):]
+            hist["S"] = new
+        if v in QUICK:
+            lm, hi, lo = R("lm", l0, l0 + 256), R("HL", 0, 256), R("HL", 256, 512)
+            act(hi, lm)
+            mm([(R("b2", 0, 256), R("If"), lm, True, False), (R("b2", 0, 256), R("nI"), hi, False, True)])
+            act(lo, R("b2", 0, 256))
+            mm([(R("b1", 128 * u, 128 * u + 128), R("HL", u, 512, 4), R("Ib"), True, True) for u in range(4)])
+            act(R("LT"), R("b1"))
+            return
+        w = [dmas([(T.Ld[v % 2, u, :, 1:32], R("lm", l0 + 32 * u + 1, l0 + 32 * u + 32)) for u in range(4 * gh, 4 * gh + 4)],
+                  WLAT / 2, [], [R("lm", l0 + 128 * gh, l0 + 128 * gh + 128)], after=held[v % 2]) for gh in range(2)]
+        held[v % 2] = []
+        for h in range(2):
+            a = 2048 * ((2 * v + h) % 3)
+            held[v % 2].append(dmas([(R("L", a, a + 2048, p=(i, 128, 16)), T.Ld[v % 2, :, 64 * h:64 * h + 64, :])
+                                     for i in range(16)], 1048576 / GBW, [R("L", a, a + 2048)], [], after=w))
+
+    def opacity(v, h):
+        k = 2 * v + h
+        tag[0] = ("f", v, h)
+        s0, l0, tr = 2048 * h, 2048 * (k % 3), "tr%d" % (k % 4)
+        last = {}
+        for gh in range(2):
+            gathers("C%d" % (v % 2), "CO", 512 * (v % 2), gh, 64 * h, 64 * h + 64, COV[v] // 2, CCH, last)
+        to = "tr%d" % ((k + 2) % 4) if ONE[k] == "B" else tr
+        if v in QUICK:
+            for q in range(4):
+                bk = ("b3", "b4")[q % 2]
+                mm([(R(bk, t, 512, 8), R("Sel", 128 * t, 128 * t + 128), R("LT", 128 * q + 64 * h, 128 * q + 64 * h + 64), True, True)
+                    if q + t else (R(bk, 0, 512, 8), R("cm"), R("ones", 0, 64), True, True) for t in range(8)])
+                tt(R(tr, q, 2048, 4), R(bk), R("S", s0 + q, s0 + 2048, 4), ALU.mult)
+        for a in range(1536, -1, -512):
+            if v in QUICK:
+                pass
+            elif SUM[v] == "D":
+                if a % PCH == 0:
+                    scan(R(tr, a, a + PCH), R("L", l0 + a, l0 + a + PCH), R("S", s0 + a, s0 + a + PCH), 0.0, mx, ALU.mult)
+            else:
+                bk = bank("s")
+                mm([(R(bk), R("Mm", 128 * gh, 128 * gh + 128), R("X", 4096 * gh + s0 + a, 4096 * gh + s0 + a + 512),
+                     gh == 0, gh == 1) for gh in range(2)])
+                tt(R(tr, a, a + 512), R(bk), R("L", l0 + a, l0 + a + 512), ALU.mult)
+            if ONE[k] == "D":
+                if a % 1024 == 0:
+                    gadd(R(tr, a, a + 1024), R("ones", 0, 1024), 524288)
+            elif ONE[k] in "AB":
+                n = 512 if v == V - 1 else PCH
+                if a % n == 0:
+                    act(R(to, a, a + n), R(tr, a, a + n), bias=1.0)
+            else:
+                ts(R(tr, a, a + 512), R(tr, a, a + 512), 1.0, ALU.add)
+
+    def colour(v, h):
+        k = 2 * v + h
+        tag[0] = ("f", v, h)
+        tr, C, c0 = "tr%d" % (k % 4), "C%d" % (v % 2), 2048 * h
+        t1 = "tr%d" % ((k + 2) % 4) if ONE[k] == "B" else tr
+        for a in range(1536, -1, -512):
+            bk = bank("d")
+            c = c0 + a
+            for (u, (m, d)) in enumerate(((0, c + 1), (128, 4096 + c + 1), (256, c), (384, 4096 + c))):
+                mm([(R(bk), R("Mm", m, m + 128), R(C, d, d + 512), u == 0, u == 3)])
+            for c in range(0, 512, FCH):
+                scan(R("Eo", a + c + FCH, a + c, -1), R(t1, a + c + FCH, a + c, -1), R(bk, c + FCH - 1, c - 1, -1),
+                     0.0, ALU.mult, ALU.add)
+        o = 64 * k
+        base = 248.0
+        if TAU[k] == "P":
+            for s0 in range(1, 32, 2):
+                mm([(R("b7", 0, 64), R("If"), R(tr, s, 2048, 32), s == 1, s == 31) for s in range(s0, min(s0 + 2, 32))])
+            if ONE[k] == "B":
+                base = 0.0
+            src = R("b7", 0, 64)
+        else:
+            e0 = 2048 * (k % 3)
+            for a in range(e0, e0 + 2048, 512):
+                scan(R("L", a, a + 512), R("rs4"), R(tr, a - e0, a - e0 + 512), 0.0, ALU.mult, ALU.add)
+            src = R("L", e0 + 31, e0 + 2048, 32)
+            if ONE[k] == "B":
+                base = -8.0
+        y = o % 256
+        act(R("YT", y, y + 64), src, scale=-8.0, bias=base)
+        (act if YCA else cp)(R("YC", y, y + 64), R("Eo", 1, 2048, 32))
+        if v == V - 1:
+            dma(T.yt[:, o:o + 64], R("YT", y, y + 64), 32768, [], [R("YT", y, y + 64)])
+            dma(T.yc[:, o:o + 64], R("YC", y, y + 64), 32768, [], [R("YC", y, y + 64)])
+        elif h == 1:
+            o, y = o - 64, y - 64
+            dmas([(T.yc[:, o:o + 128], R("YC", y, y + 128)), (T.yt[:, o:o + 128], R("YT", y, y + 128))], 131072 / GBW,
+                 [], [R("YC", y, y + 128), R("YT", y, y + 128)])
+
+    for v in range(V):
+        if TWO:
+            whole2(v, 0)
+            whole2(v, 1)
+        else:
+            whole(v)
+        spread(v)
+        for h in range(2):
+            opacity(v, h)
+        for h in range(2):
+            colour(v, h)
     return ops, nsent[0]
+
+
+YSP = [(0, 384)]
+LSP = [2] * 6
 
 
 def schedule(ops):
@@ -505,26 +852,33 @@ def schedule(ops):
     def gap(a, b):
         if a not in ops[b]["deps"] or (ops[a]["e"] == "P" and ops[b]["e"] == "P"):
             return 0.0
-        return (GAP1 if ops[a]["e"] == ops[b]["e"] else GAP2) + ops[a]["lat"]
+        if ops[a]["e"] == ops[b]["e"] and ops[a]["sem"] is None:
+            return GAP1
+        return GAP2 + ops[a]["lat"]
     tail = [0.0] * n
     for i in range(n - 1, -1, -1):
-        tail[i] = ops[i]["cost"] + max([gap(i, k) + tail[k] for k in kids[i]] + [ops[i]["lat"]])
+        due = 0.0
+        if ops[i]["tag"] is not None:
+            kind, v, h = ops[i]["tag"]
+            due = (V - 1 - v) * STAG + (WOFF - h * LAG if kind == "w" else FOFF - h * STAG / 4)
+        tail[i] = ops[i]["cost"] + max([gap(i, k) + tail[k] for k in kids[i]] + [ops[i]["lat"], due])
     par = [sorted(o["deps"] | o["ord"]) for o in ops]
-    key = [-x for x in tail]
+    key = [-tail[i] + JIT * (((i + SEED) * 2654435761 >> 7) % 1000) / 1000.0 for i in range(n)]
     best = None
     for it in range(NIT):
         order, st, end = one_pass(ops, par, kids, gap, key)
         if best is None or end < best[1]:
             best = (order, end, st)
-        back = one_pass(ops, kids, par, lambda a, b: gap(b, a), [-(st[i] + ops[i]["cost"]) for i in range(n)])[1]
+        back = one_pass(ops, kids, par, lambda a, b: gap(b, a), [-(st[i] + ops[i]["cost"]) for i in range(n)], False)[1]
         key = [-(back[i] + ops[i]["cost"]) for i in range(n)]
     for i in range(n):
         ops[i]["st"] = best[2][i]
     return best[0], best[1]
 
 
-def one_pass(ops, par, kids, gap, key):
+def one_pass(ops, par, kids, gap, key, fwd=True):
     n = len(ops)
+    pipe = 0.0
     left = [len(b) for b in par]
     rdy = [0.0] * n
     start = [0.0] * n
@@ -542,19 +896,31 @@ def one_pass(ops, par, kids, gap, key):
         t, e = min((max(free[e], min(rdy[i] for i in pool[e])), e) for e in pool if pool[e])
         i = None
         soon = 1e18
-        for k in sorted(pool[e], key=lambda k: (key[k], k)):
-            if rdy[k] <= t + 1.0 and t + ops[k]["cost"] <= soon + SLACK:
+        when = {k: rdy[k] for k in pool[e]}
+        for f in pool:
+            if f != e and AHEAD:
+                for p in pool[f]:
+                    s = max(free[f], rdy[p], t)
+                    if s < t + AHEAD:
+                        for k in kids[p]:
+                            if left[k] == 1 and ops[k]["e"] == e:
+                                when[k] = max(rdy[k], s + ops[p]["cost"] + gap(p, k), t + 2.0)
+        for k in sorted(when, key=lambda k: (key[k], k)):
+            if when[k] <= t + 1.0 and t + ops[k]["cost"] <= soon + SLACK:
                 i = k
                 break
-            if rdy[k] > t + 1.0:
-                soon = min(soon, rdy[k])
+            if when[k] > t + 1.0:
+                soon = min(soon, when[k])
         if i is None:
-            free[e] = soon
+            free[e] = min(soon, t + 100.0)
             continue
         pool[e].remove(i)
         st = max(t, rdy[i])
         start[i] = st
         fin = st + ops[i]["cost"]
+        if ops[i]["dm"] and fwd:
+            pipe = max(st + 1500, pipe) + ops[i]["dm"]
+            ops[i]["lat"] = max(pipe, fin + 1500) + 500 - fin
         free[e] = fin if e != "X" else 0.0
         order[e].append(i)
         end = max(end, fin + ops[i]["lat"])
@@ -603,7 +969,7 @@ def rank_program(g, core, T, topo):
                 if d in mark and not (e == "P" and ops[d]["e"] == "P"):
                     s, c = mark[d]
                     need[s] = max(need.get(s, 0), c)
-            if e == "G" and i in mark and mark[i][1] > 1:
+            if e == "G" and i in mark and ops[i]["sem"] is None and mark[i][1] > 1:
                 need["sG"] = mark[i][1] - 1
             for s in sorted(need):
                 if seen.get(s, 0) < need[s]:

@@ -5,77 +5,70 @@ V = 6
 MM = 0x8421
 S21 = 2.0 ** -21
 HOLE = 1.0 - 2.0 ** -13
-PEC, OVH, GK, LAT, FF, MINC = 0.6, 62, 1.75, 3000, 1.0, 16
-GDC, GBW, SDC, WLAT, ADDK = 1000, 300.0, 100, 1200, 1.4
-STAG, WOFF, FOFF = 31000.0, 30000.0, 0.0
-NIT, LAG, AHEAD, JIT, SEED = 3, 4000.0, 0.0, 0.0, 0
-SGV = [48] + [8] * 4 + [48]
-COV = [0] * 5 + [16]
-QUICK = (5,)
-SUM = "DDDDDD"
-ONE = "DDADDADDADAB"
-TAU = "PPPVPPPVPVVV"
-FKP, LTA, QQF, GTV, HOV, P1P = True, True, False, False, 0, True
-GCH, CCH, FCH, PCH, YCA = 64, 32, 512, 512, False
 ZC = 1.5 * 2.0 ** 36
+TW = 4112
+SGV = [(40, 72)] + [(0, 12)] * 4 + [(16, 48)]
+COV = [0] * 5 + [16]
+ONE = "DDDDDDDDAAAB"
+TAU = "PPHPPPPVHVVV"
+GCH, CCH = 64, 32
+LTA, QA, YCA, QQA, GTV, YSP = False, True, True, (0, 0), (0, 0), (0, 1)
+CYC, FF, OVH, MINC, GK, PEC = 0.83, 1.0, 62, 16, 1.75, 0.63
+GDC, SDC, GBW, WLAT, ADDK, LAT = 1000, 100, 300.0, 1000, 1.4, 3000
+SPEEDS, SWAPS = [(1.0, 1.1, 0.42), (1.0, 1.56, 0.42), (1.2, 2.05, 0.5), (1.35, 1.4, 0.58), (1.05, 1.5, 0.7)], 8000
+GAP1, GAP2, SLACK = 100.0, 200.0, 250.0
+STAG, WOFF, FOFF, LAG, NIT = 33000.0, 30000.0, 4000.0, 3000.0, 8
 F32, BF, I32, U16, F16 = "float32", "bfloat16", "int32", "uint16", "float16"
 
 SCRATCH = {}
 for _n, _c, _d in [
-    ("SG", 8208, BF), ("CO", 8208, BF), ("pxi", 1152, I32), ("lsr", 128, I32), ("fpr", 8, I32),
-    ("omi", 48, I32), ("omf", 48, F32), ("omu", 48, U16),
-    ("OMS", 1536, F32), ("KT", 1024, F32), ("PY", 1024, F32),
-    ("ones", 1024, BF), ("onef", 128, F32), ("Ib", 128, BF), ("nI", 128, BF), ("I25", 128, BF),
-    ("If", 128, F32), ("I21", 128, F32), ("PRa", 128, F32), ("PRb", 128, F32), ("PL", 128, F32),
-    ("c14", 256, BF), ("Mm", 512, BF), ("Cst", 512, BF),
-    ("blk", 8, F32), ("blkK", 8, F32), ("blk4", 8, F32), ("RS", 16, BF),
-    ("E16", 512, BF), ("rst", 256, BF), ("r16", 128, BF), ("d0c", 256, F32), ("cG", 256, F32), ("cGy", 128, F32),
-    ("ck", 128, F32), ("mk2", 256, BF), ("sio", 256, F32), ("pj", 8, I32), ("col", 8, F32), ("hI", 128, BF),
-    ("nh", 128, BF), ("rs4", 512, BF),
-    ("NO", 96, U16), ("NL", 96, U16), ("LS", 640, F32), ("LL", 768, F32),
-    ("g0", 128, I32), ("k0i", 128, I32), ("k0f", 128, F32), ("LG", 128, F32),
-    ("OF", 1024, U16), ("lm", 512, F32), ("X", 8192, BF), ("S", 4096, BF), ("L", 6144, F32),
-    ("C0", 8208, BF), ("C1", 8208, BF),
-    ("tr0", 2056, F32), ("tr1", 2056, F32), ("tr2", 2056, F32), ("tr3", 2056, F32), ("Eo", 2056, F32),
-    ("YC", 256, F32), ("YT", 256, F32), ("c3k", 256, BF), ("I25f", 128, F32),
-    ("bk16", 16, BF), ("ckp", 128, F32), ("c3m", 128, BF), ("III", 384, F32),
-    ("PG", 256, F32), ("Lo0", 128, F32), ("Lo1", 128, F32), ("Ks", 256, I32), ("fi", 256, I32), ("dA", 256, BF),
-    ("qq", 256, BF), ("AB", 512, BF), ("SL", 256, BF), ("zs", 272, F32), ("ln", 256, F32), ("w", 256, F32),
-    ("gt", 256, F32), ("mm", 256, BF), ("lk", 256, F32), ("dF", 256, F32), ("e", 256, I32), ("e2", 256, I32),
-    ("nn", 256, F32), ("G", 256, F32), ("li", 32, I32), ("NI", 256, F16), ("AN", 256, F16), ("YG0", 128, F32),
-    ("YG1", 128, F32), ("M0", 256, F32),
-    ("LI", 128, F32), ("LB", 128, F32), ("nl", 128, F32), ("lt", 128, F32), ("Gy", 128, F32), ("PN", 384, F32),
-    ("DM", 384, I32), ("E0", 192, F32), ("E1", 192, F32),
-    ("XF", 128, F32), ("xr", 128, F32), ("Sel", 1024, BF), ("HL", 512, BF), ("LT", 512, BF), ("cm", 128, BF),
+    ("SG", 2 * TW, BF), ("CO", 2 * TW, BF), ("pxi", 1152, I32), ("fpr", 8, I32),
+    ("omi", 48, I32), ("omf", 48, F32), ("omu", 48, U16), ("OMS", 1536, F32), ("KT", 1024, F32), ("PY", 1024, F32),
+    ("ones", 1024, BF), ("onef", 128, F32), ("Ib", 128, BF), ("nI", 128, BF), ("I25", 128, BF), ("nh", 128, BF),
+    ("hI", 128, BF), ("If", 128, F32), ("I21", 128, F32), ("I25f", 128, F32), ("III", 384, F32),
+    ("PRa", 128, F32), ("PRb", 128, F32), ("PL", 128, F32), ("Mm", 512, BF), ("Sel", 1024, BF),
+    ("c14", 128, BF), ("c3k", 128, BF), ("c3m", 64, BF), ("ckb", 256, BF), ("cm", 128, BF), ("Cst", 256, BF),
+    ("blk", 8, F32), ("blkK", 8, F32), ("blk4", 8, F32), ("bk16", 16, BF), ("RS", 16, BF),
+    ("rst", 128, BF), ("r16", 64, BF), ("d16", 64, BF), ("c22", 128, BF), ("rs4", 512, BF), ("d0c", 128, F32), ("cG", 128, F32), ("cGy", 64, F32),
+    ("mk2", 128, BF), ("sio", 128, F32), ("pj", 8, I32), ("col", 8, F32),
+    ("NO", 48, U16), ("NL", 48, U16), ("LS", 640, F32), ("LL", 768, F32), ("OF", 1024, U16), ("PG", 128, F32),
+    ("YG0", 128, F32), ("YG1", 128, F32), ("lm", 512, F32), ("HL", 512, BF), ("LT", 512, BF),
+    ("X", 8192, BF), ("S", 4096, BF), ("L", 6144, F32), ("C0", 8208, BF), ("C1", 8208, BF),
+    ("tr0", 2056, F32), ("tr1", 2056, F32), ("tr2", 2056, F32), ("tr3", 2056, F32),
+    ("Eo", 4098, F32), ("YC", 256, F32), ("YT", 256, F32),
+    ("M0", 256, F32), ("M1", 128, F32), ("Ks", 256, I32), ("fi", 256, I32), ("dA", 256, BF), ("qq", 256, BF),
+    ("AB", 512, BF), ("SL", 256, BF), ("zs", 272, F32), ("ln", 256, F32), ("w", 256, F32), ("gt", 256, F32),
+    ("mm", 256, BF), ("lk", 256, F32), ("dF", 256, F32), ("e", 256, I32), ("e2", 256, I32), ("nn", 256, F32),
+    ("G", 256, F32), ("li", 32, I32), ("NI", 256, F16), ("AN", 256, F16), ("LB", 128, F32),
+    ("nl", 128, F32), ("lt", 128, F32), ("Gy", 128, F32), ("PN", 384, F32), ("DM", 384, I32), ("E0", 192, F32),
+    ("E1", 192, F32), ("XF", 128, F32), ("xr", 128, F32),
 ]:
     SCRATCH[_n] = ("sbuf", [128, _c], _d)
-TWO = True
-SCRATCH["Z2" if TWO else "Z"] = ("sbuf", [128, 32, 12] if TWO else [128, 16, 24], F32)
+SCRATCH["Z"] = ("sbuf", [128, 32, 12], F32)
 SCRATCH["Ld"] = ("dram", [2, 8, 128, 32], F32)
 for _k in range(8):
     SCRATCH["b%d" % _k] = ("psum", [128, 512], F32)
 
 SEMAPHORES = (["sV", "sA", "sP", "sG", "sent"] + ["d%d" % _k for _k in range(90)]
-              + [_n % _k for _n in ("nm%d", "li%d") for _k in (range(2, 2 * V) if TWO else range(1, V))])
+              + ["nm%d" % _k for _k in range(1, V)] + ["li%d" % _k for _k in range(2, 2 * V)])
 
 ALU = AluOpType
 ACT = ActivationFunctionType
-CYC = 0.83
-GAP1, GAP2, SLACK = 100.0, 200.0, 300.0
+HALF = ((0, 64), (64, 128))
 
 
 def R(name, a=0, b=None, s=1, p=None):
     if b is None:
         b = SCRATCH[name][1][1]
     cols = range(a, b, s)
-    exact = 0
+    x = 0
     if abs(s) == 1:
-        exact = ((1 << len(cols)) - 1) << min(cols)
+        x = ((1 << len(cols)) - 1) << min(cols)
     else:
         for c in cols:
-            exact |= 1 << c
+            x |= 1 << c
     lo, hi = min(cols), max(cols)
-    return {"n": name, "a": a, "b": b, "s": s, "p": p, "len": len(cols), "x": exact,
+    return {"n": name, "a": a, "b": b, "s": s, "p": p, "len": len(cols), "x": x,
             "box": ((1 << (hi - lo + 1)) - 1) << lo, "ps": SCRATCH[name][0] == "psum", "dt": SCRATCH[name][2]}
 
 
@@ -132,18 +125,19 @@ def build(T, rank, core, topo):
                     deps.update(turn[2][-2:])
                 if me not in turn[2]:
                     turn[2].append(me)
-            for (o, oe, ox, obox, ow) in h:
-                if oe == eng and sem is None and (o == me or ops[o]["sem"] is None):
+            for (o, ox, obox, ow) in h:
+                if sem is None and (o == me or ops[o]["sem"] is None):
                     if (wr or ow) and (ox & r["x"]):
                         deps.add(o)
                 elif (wr or ow) and (obox & r["box"]):
                     deps.add(o)
             if wr and r["p"] is None:
-                h[:] = [z for z in h if z[2] & ~r["x"]]
-            h.append((me, eng, r["x"], r["box"], wr))
+                h[:] = [z for z in h if z[1] & ~r["x"]]
+            h.append((me, r["x"], r["box"], wr))
         deps.discard(me)
         ops.append({"e": eng, "fn": fn, "deps": deps, "cost": cost, "lat": lat, "sem": sem, "ext": ext, "ord": set(),
-                    "nm": outs[0]["n"] if outs else "-", "tag": tag[0], "dm": dm})
+                    "nm": outs[0]["n"] if outs else "-", "tag": tag[0], "dm": dm,
+                    "gn": sum(r["len"] for r in ins if isinstance(r, dict) and "win" in r)})
         return me
 
     def chain(lst):
@@ -167,7 +161,7 @@ def build(T, rank, core, topo):
         return add("V", f, [out], [in0, s1, s2], vcost(out["len"], gk(in0, half(out, in0))))
 
     def tt(out, a, b, op):
-        k = gk(a, 1.0 if (a["ps"] or b["ps"]) else 2.0)
+        k = 1.0 if (a["ps"] or b["ps"]) else 2.0
         return add("V", lambda g: g.vector.tensor_tensor(ap(out), ap(a), ap(b), op), [out], [a, b], vcost(out["len"], k))
 
     def cp(out, a):
@@ -233,138 +227,113 @@ def build(T, rank, core, topo):
         f = lambda g: g.dma_start(ap(out), ap(src), accum_op=ALU.add, max_dma_last_dim=4096)
         return add("G", f, [out], [src, out], GDC, lat=2000 + ADDK * nbytes / GBW, sem=(s, 16), dm=ADDK * nbytes / GBW)
 
-    HALF = ((0, 64), (64, 128))
+    def load(name, src):
+        for h in range(2):
+            dmas([(R(name, TW * h, TW * h + 4096, p=HALF[x]), src[64 * h:64 * h + 64, :]) for x in range(2)],
+                 1048576 / GBW, [R(name, TW * h, TW * h + 4096)], [])
 
-    def load4(name, src):
-        for gh in range(2):
-            r = R(name, 4096 * gh, 4096 * gh + 4096)
-            dmas([(R(name, 4096 * gh, 4096 * gh + 4096, p=HALF[x]), src[64 * gh:64 * gh + 64, :]) for x in range(2)],
-                 1048576 / GBW, [r], [])
-
-    dma(R("lsr"), T.ls[:], 65536, [R("lsr")], [])
+    dma(R("DM", 0, 128), T.ls[:], 65536, [R("DM", 0, 128)], [])
     dma(R("fpr"), T.fp[:], 20000, [R("fpr")], [])
     dma(R("pxi", 0, 1024), T.px[:], 524288, [R("pxi", 0, 1024)], [])
-    load4("SG", T.sg)
+    load("SG", T.sg)
     dma(R("omi"), T.om[:], 30000, [R("omi")], [])
-    load4("CO", T.co)
+    load("CO", T.co)
     chain(list(range(len(ops))))
 
-    eq = ALU.is_equal
+    eq, mn, mx = ALU.is_equal, ALU.min, ALU.max
     iota(R("pj", 0, 1), [[0, 1]], 0, 1)
     iota(R("onef"), [[0, 128]], 1, 0)
-    NG = 4 if TWO else 8
-    gp = lambda j: [[-64, 2], [j, 16], [-16, 4]] if TWO else [[j, 16], [-16, 8]]
-    sel(R("PL"), R("onef"), gp(-1), eq, 0, 1)
-    sel(R("PRb"), R("onef"), gp(1), eq, -15, 1)
+    sel(R("PL"), R("onef"), [[-64, 2], [-1, 16], [-16, 4]], eq, 0, 1)
+    sel(R("PRb"), R("onef"), [[-64, 2], [1, 16], [-16, 4]], eq, -15, 1)
+    sel(R("PRa"), R("onef"), [[-64, 2], [1, 16], [-16, 4]], eq, 1, 1)
+    sel(R("PRa", 0, 64, 4), R("onef", 0, 16), [[1, 16]], eq, -127, 1)
     sel(R("If"), R("onef"), [[-1, 128]], eq, 0, 1)
     sel(R("blk"), R("onef", 0, 8), [[-16, 8]], ALU.is_ge, 0, 1)
     sel(R("blk"), R("blk"), [[16, 8]], ALU.is_ge, 15, -1)
     ms(R("ones"), 1.0)
-    for q in range(2):
-        iota(R("Cst", 256 * q, 256 * q + 256), [[4096, 2], [4096, 2], [0, 64]], -128, 0)
-    iota(R("Cst", 0, 256, 16), [[4096, 2], [4096, 2], [0, 4]], 16384 - 128, 0)
+    iota(R("Cst"), [[0, 2], [4096, 2], [0, 64]], -128, 0)
+    iota(R("Cst", 0, 128, 16), [[4096, 2], [0, 4]], 16384 - 128, 0)
     iota(R("e2", 0, 48), [[1, 48]], 0, 0)
-    sel(R("E16", p=(0, 16)), R("ones", 0, 512, p=(0, 16)), [[0, 32], [-1, 16]], eq, 0, 1)
-    sel(R("rst"), R("ones", 0, 256), [[0, 8], [1, 32]], ALU.is_gt, 0, 0)
-    iota(R("sio"), [[0, 8], [1, 32]], 0, 0)
-    sel(R("r16"), R("ones", 0, 128), [[0, 8], [1, 16]], ALU.is_gt, 0, 0)
-    iota(R("cGy"), [[0, 8], [-1, 16]], 16, 0)
-    iota(R("ck", 0, 16 * NG), [[512, 16], [0, NG]], 512 - 2 ** 24, 0)
-    sel(R("PRa"), R("onef"), gp(1), eq, 1, 1)
-    sel(R("PRa", 0, 16 * NG, NG), R("onef", 0, 16), [[1, 16]], eq, -127, 1)
-    if TWO:
-        sel(R("Lo1"), R("PRa"), [[0, 128]], ALU.is_ge, -64, 1)
-        sel(R("PRa"), R("PRa"), [[0, 128]], ALU.is_ge, 63, -1)
+    sel(R("HL", p=(0, 16)), R("ones", 0, 512, p=(0, 16)), [[0, 32], [-1, 16]], eq, 0, 1)
+    sel(R("rst"), R("ones", 0, 128), [[0, 4], [1, 32]], ALU.is_gt, 0, 0)
+    sel(R("r16"), R("ones", 0, 64), [[0, 4], [1, 16]], ALU.is_gt, 0, 0)
+    sel(R("rs4"), R("ones", 0, 512), [[0, 16], [1, 32]], ALU.is_gt, 0, 0)
+    iota(R("sio"), [[0, 4], [1, 32]], 0, 0)
+    iota(R("cGy"), [[0, 4], [-1, 16]], 16, 0)
     for x in range(2):
         sel(R("Mm", 0, 256, p=HALF[x]), R("ones", 0, 256, p=HALF[x]), [[64, 2], [-1, 128]], eq, 0, 1)
-    if QUICK:
-        for x in range(2):
-            for u in range(0, 1024, 512):
-                sel(R("Sel", u, u + 512, p=HALF[x]), R("ones", 0, 512, p=HALF[x]), [[-1, 4], [-8, 8], [0, 16]], eq, -u // 128, 1)
-        act(R("cm"), R("onef"), scale=2.0 ** 18)
-    act(R("tr1", 0, 512), R("ones", 0, 512), scale=2.0 ** 25)
-    held = [[dma(T.Ld[:], R("tr1", 0, 512), 262144, [], [R("tr1", 0, 512)])]] * 2
+        for u in range(0, 1024, 512):
+            sel(R("Sel", u, u + 512, p=HALF[x]), R("ones", 0, 512, p=HALF[x]), [[-1, 4], [-8, 8], [0, 16]], eq, -u // 128, 1)
+    for u in range(8):
+        iota(R("ckb", u, 64, 8), [[-1, 2], [-2, 2], [-4, 2]], 8 - 8 * (u // 4), 0)
+    iota(R("ckb", 64, 128), [[0, 64]], -3072, 0)
+    iota(R("ckb", 128, 192), [[512, 16], [0, 4]], 512, 0)
     ts(R("pj", 1, 2), R("pj", 0, 1), 15, ALU.bitwise_and)
     jj = R("pj", 1, 2)
     ts(R("col", 0, 1), jj, 512.0, ALU.mult, -2.0 ** 24, ALU.add)
     ts(R("col", 1, 2), jj, 512.0, ALU.mult, 256.0 - 2.0 ** 24, ALU.add)
     ts(R("col", 4, 5), jj, 2.0, ALU.mult)
-    act(R("Ib"), R("If"))
-    act(R("I25"), R("If"), scale=2.0 ** 25)
-    act(R("hI"), R("If"), scale=0.5)
-    act(R("nh"), R("If"), scale=-0.5)
-    act(R("c14"), R("ones", 0, 256), scale=-128 * S21)
-    act(R("nI"), R("If"), scale=-1.0)
+    for (n, c) in (("Ib", 1.0), ("I25", 2.0 ** 25), ("hI", 0.5), ("nh", -0.5), ("nI", -1.0), ("I25f", 2.0 ** -25), ("I21", S21)):
+        act(R(n), R("If"), scale=c)
+    for (u, c) in enumerate((2.0 ** 25, 2.0 ** 21, -2.0 ** 21)):
+        act(R("III", 128 * u, 128 * u + 128), R("If"), scale=c)
+    for (n, c) in (("c14", -128 * S21), ("c3k", ZC * 2.0 ** -25), ("cm", 2.0 ** 18)):
+        act(R(n), R("onef"), scale=c)
+    act(R("c3m"), R("onef", 0, 64), scale=3072.0 * 2 ** 21)
+    act(R("ckb", 192, 256), R("onef", 0, 64), scale=-2.0 ** 24)
     act(R("bk16", 0, 8), R("blk"))
     act(R("bk16", 8, 16), R("blk"), scale=-1.0)
     act(R("blkK"), R("blk"), scale=2.0 ** 25)
-    act(R("c3k"), R("ones", 0, 256), scale=ZC * 2.0 ** -25)
-    act(R("I25f"), R("If"), scale=2.0 ** -25)
-    if FKP:
-        for (u, c) in enumerate((2.0 ** 25, 2.0 ** 21, -2.0 ** 21)):
-            act(R("III", 128 * u, 128 * u + 128), R("If"), scale=c)
-        act(R("c3m"), R("onef"), scale=3072.0 * 2 ** 21)
-        x0, x1 = R("DM", 0, 16 * NG), R("DM", 128, 128 + 16 * NG)
-        iota(x0, [[1, 16], [0, NG]], 0, 0)
-        ts(x1, x0, float(MM), ALU.mult)
-        ts(x0, x1, 0x8888, ALU.bitwise_and)
-        ts(x1, x0, float(0x249), ALU.mult)
-        ts(x0, x1, 12, ALU.arith_shift_right, 15, ALU.bitwise_and)
-        ts(R("ckp", 0, 16 * NG), x0, 3064.0, ALU.add, -2.0 ** 25, ALU.mult)
     tt(R("blk4", 0, 4), R("blk", 0, 4), R("blk", 4, 8), ALU.add)
     tt(R("blk4", 4, 8), R("blk", 4, 8), R("blk", 0, 4), ALU.subtract)
-    act(R("RS", 4, 8), R("blk4", 4, 8), scale=-2.0 ** 30)
     act(R("RS", 0, 4), R("blk4", 0, 4), scale=2.0 ** 42)
+    act(R("RS", 4, 8), R("blk4", 4, 8), scale=-2.0 ** 30)
     act(R("RS", 8, 12), R("blk4", 0, 4), scale=-2.0 ** 45)
     act(R("RS", 12, 16), R("blk4", 0, 4), scale=0.0)
-    act(R("I21"), R("If"), scale=S21)
     act(R("d0c"), R("rst"), scale=2.0 ** 30, bias=-float(MM))
     act(R("cG"), R("sio"), scale=-MM / HOLE, bias=32.0 * MM / HOLE)
-    if TWO:
-        act(R("b0", 384, 448), R("cGy", 0, 64), scale=float(MM))
-        act(R("b0", 448, 512), R("ck", 0, 64))
-        ms(R("NO"), 0)
-    else:
-        act(R("b3", 128, 256), R("cGy"), scale=float(MM))
-        act(R("b2", 384, 512), R("ck"))
+    act(R("b0", 384, 448), R("cGy"), scale=float(MM))
     act(R("Mm", 256, 512), R("Mm", 0, 256), scale=-1.0)
-    ms(R("SG", 8192, 8208), 16.0)
-    ms(R("CO", 8192, 8208), 0.0)
-    for n in ("C0", "C1"):
-        ms(R(n, 8192, 8200), 0.0)
-    for n in ("tr0", "tr1", "tr2", "tr3"):
-        ms(R(n, 2048, 2056), 0.0)
+    for h in range(2):
+        iota(R("SG", TW * h + 4096, TW * h + TW), [[0, 16]], 16, 0)
+        iota(R("CO", TW * h + 4096, TW * h + TW), [[0, 16]], 0, 0)
+        iota(R("C%d" % h, 8192, 8200), [[0, 8]], 0, 0)
+    for u in range(4):
+        iota(R("tr%d" % u, 2048, 2056), [[0, 8]], 0, 0)
+    ms(R("NO"), 0)
     ms(R("lm", 0, 512, 128), -2.0 ** 25)
     ms(R("NI"), 0.0)
-    ms(R("LI"), 0.0)
+    act(R("c22", 0, 64), R("onef", 0, 64), scale=-256 * S21)
+    act(R("c22", 64, 128), R("onef", 0, 64), scale=-0.5 * S21)
+    sel(R("d16"), R("ones", 0, 64), [[0, 4], [-1, 16]], ALU.is_gt, 15, 0)
     ts(R("mk2"), R("sio"), R("col", 4, 5), ALU.is_le)
-    sel(R("mk2"), R("mk2"), [[0, 8], [1, 32]], ALU.is_gt, 0, 0)
-    if "V" in TAU:
-        sel(R("rs4"), R("ones", 0, 512), [[0, 16], [1, 32]], ALU.is_gt, 0, 0)
+    sel(R("mk2"), R("mk2"), [[0, 4], [1, 32]], ALU.is_gt, 0, 0)
+    act(R("tr1", 0, 512), R("ones", 0, 512), scale=2.0 ** 25)
+    held = [[dma(T.Ld[:], R("tr1", 0, 512), 262144, [], [R("tr1", 0, 512)])]] * 2
     iota(R("OMS", 0, 256), [[0, 256]], 0, 0)
     iota(R("OMS", 256, 1536), [[0, 1280]], 0, 0)
     cp(R("omu"), R("e2", 0, 48))
     cp(R("omf"), R("omi"))
     act(R("Eo", 1024, 1792), IND(R("omf"), R("omu")))
-    mm([(R("b5"), R("E16", 0, 128, p=(0, 16)), R("E16", p=(0, 16)), True, True)])
+    mm([(R("b5"), R("HL", 0, 128, p=(0, 16)), R("HL", p=(0, 16)), True, True)])
     tt(R("Eo", 0, 256), R("b5", 0, 256), R("Eo", 1024, 1280), ALU.mult)
     tt(R("Eo", 256, 768), R("b5"), R("Eo", 1280, 1792), ALU.mult)
     for (k0, k1, bk) in ((0, 1, "b6"), (1, V, "b7")):
         mm([(R(bk, 8 * k, 8 * k + 8), R("Eo", 128 * k, 128 * k + 128), R("blkK"), True, True) for k in range(k0, k1)])
         act(R("OMS", 256 * k0, 256 * k1, 32), R(bk, 8 * k0, 8 * k1))
 
-    def keys(out, src, n, ti, tf, c):
-        ts(R(ti, 0, n), src, 0xFFF00, ALU.bitwise_and)
-        ts(R(tf, 0, n), R(ti, 0, n), 31.0, ALU.mult, c, ALU.add)
-        tt(out, R(tf, 0, n), src, ALU.add)
+    def keys(out, src, ti, tf, c):
+        ts(R(ti, 0, 128), src, 0xFFF00, ALU.bitwise_and)
+        ts(R(tf, 0, 128), R(ti, 0, 128), 31.0, ALU.mult, c, ALU.add)
+        tt(out, R(tf, 0, 128), src, ALU.add)
 
-    keys(R("LG"), R("lsr"), 128, "e", "dF", R("col", 1, 2))
+    keys(R("lk", 0, 128), R("DM", 0, 128), "e", "dF", R("col", 1, 2))
     ms(R("dF", 0, 256, 128), -1.0)
-    mm([(R("b4", 0, 128), R("LG"), R("PL"), True, True)])
+    mm([(R("b4", 0, 128), R("lk", 0, 128), R("PL"), True, True)])
     cp(R("LL", 0, 128), R("b4", 0, 128))
     cp(R("NL", 0, 8), R("fpr"))
-    cp(R("g0"), IND(R("pxi", 0, 1024), R("NL", 0, 8)))
-    keys(R("PG", 0, 128), R("g0"), 128, "k0i", "k0f", R("col", 0, 1))
+    cp(R("DM", 128, 256), IND(R("pxi", 0, 1024), R("NL", 0, 8)))
+    keys(R("PG"), R("DM", 128, 256), "fi", "w", R("col", 0, 1))
     for a in range(0, 1024, 512):
         px, hi = R("pxi", a, a + 512), R("tr3", 1024 + a, 1536 + a)
         ts(hi, px, 127.5, ALU.subtract, 1.5 * 2.0 ** 31, ALU.add)
@@ -386,183 +355,30 @@ def build(T, rank, core, topo):
         f = lambda g: g.remote_dma(ap(dst), ap(src), T.sem[sem], T.sem.sent, pid, rid, msk)
         nsent[0] += neng
         o = add("G", f, [], [src], 600, sem=("", 0))
-        return add("X", None, [dst], [], 0, lat=LAT + (8 * src["len"] + 200 if src["dt"] == F32 else 0), after=[o], ext=(sem, neng), sem=("", 0))
+        return add("X", None, [dst], [], 0, lat=LAT + (8 * src["len"] + 200 if src["dt"] == F32 else 0), after=[o],
+                   ext=(sem, neng), sem=("", 0))
 
-    mn, mx = ALU.min, ALU.max
-    rot = {"s": [0, ("b4", "b4")], "d": [0, ("b5", "b6")]}
-
-    def bank(k):
-        rot[k][0] += 1
-        return rot[k][1][rot[k][0] % 2]
-
-    def gathers(dst, win, o0, gh, l0, l1, nv, step, last):
+    def gathers(dst, win, o0, h, l0, l1, nv, step, last):
         for (e, p0, p1) in (("A", l0, l1 - nv), ("V", l1 - nv, l1)):
             n = -(-(p1 - p0) // step)
             cuts = [p0 + (p1 - p0) * k // max(n, 1) for k in range(n + 1)]
-            cuts = [128 * gh + a + a % 2 for a in cuts]
-            for (a, b) in zip(cuts, cuts[1:]):
-                for q in range(2):
-                    out = R(dst, 32 * a + q, 32 * b, 2)
-                    c = o0 + 128 * (gh + q)
-                    src = IND(R(win), R("OF", c + a, c + b))
-                    if dst != "X":
-                        o = (act if e == "A" else cp)(out, src)
-                    elif e == "A":
-                        o = act(out, src, scale=-2.0 ** -30)
-                    else:
-                        o = ts(out, src, -2.0 ** -30, ALU.mult)
-                    chain(last.get(e, []) + [o])
-                    last[e] = [o]
-
-    def whole(v):
-        tag[0] = ("w", v, 0)
-        o0, l0 = 512 * (v % 2), 256 * (v % 2)
-        lm = lambda a, b: R("lm", l0 + a, l0 + b)
-        if v > 0:
-            act(R("PG", 0, 128), IND(R("KT"), R("NL", 8 * v, 8 * v + 8)))
-        mm([(R("b3", 0, 128), R("PG", 0, 128), R("PRa" if v > 0 else "PRb"), True, True)])
-        lo, hi = ("LL", 128 * v), ("b3", 0)
-        for st in range(4):
-            nlo, nhi = ("Lo%d" % (st % 2), 0), ("b0", 128 * (st % 2))
-            for (h0, dst) in ((0, nlo), (64, nhi)):
-                for (u, op) in ((0, mn), (1, mx)):
-                    tt(R(dst[0], dst[1] + u, dst[1] + 128, 2), R(lo[0], lo[1] + h0, lo[1] + h0 + 64),
-                       R(hi[0], hi[1] + h0, hi[1] + h0 + 64), op)
-            lo, hi = nlo, nhi
-        for (u, op) in ((0, mn), (1, mx)):
-            tt(R("Ks", u, 256, 2), R(lo[0], lo[1], lo[1] + 128), R(hi[0], hi[1], hi[1] + 128), op)
-        ts(R("fi"), R("Ks"), 511, ALU.bitwise_and)
-        ts(R("SL"), R("Ks"), S21, ALU.mult, 135.5 - 2.0 ** -14, ALU.add)
-        ts(R("dA"), R("fi"), 256.0, ALU.subtract, S21, ALU.mult)
-        if QQF:
-            ts(R("qq"), R("fi"), 256.0, ALU.is_lt)
-        else:
-            ts(R("qq"), R("dA"), 0.0, ALU.is_lt)
-        ts(R("zs", 0, 256), R("Ks"), 4096.0, ALU.subtract, ZC + 2.0 ** 24, ALU.add)
-        act(R("zs", 0, 257, 32), R("onef", 0, 9), scale=ZC + 2.0 ** 25)
-        A = [R("AB", 256 * gh, 256 * gh + 128) for gh in range(2)]
-        Bm = [R("AB", 256 * gh + 128, 256 * gh + 256) for gh in range(2)]
-        for gh in range(2):
-            c = 128 * gh
-            scan(A[gh], R("qq", c, c + 128), R("dA", c, c + 128), 0.0, mn, mx)
-            scan(Bm[gh], R("qq", c, c + 128), R("dA", c, c + 128), 0.0, ALU.add, mn)
-        qg = [(q, gh, 256 * q + 128 * gh) for gh in range(2) for q in range(2)]
-        mm([(R("b1", c, c + 128), R("Cst", c, c + 128), R("Ib"), c == 0, False) for (q, gh, c) in qg])
-        mm([(R("b1", c, c + 128, p=HALF[x]), R("SL", 128 * gh + q, 128 * gh + 128, 2), R("Ib"), False, False)
-            for (q, gh, c) in qg for x in range(2)])
-        mm([(R("b1", c, c + 128), R("AB", 256 * gh + q, 256 * gh + 256, 2), R("I25"), False, c == 384) for (q, gh, c) in qg])
-        for (q, gh, c) in qg:
-            d = o0 + 256 * gh + 128 * q
-            ts(R("OF", d, d + 128), R("b1", c, c + 128), 8192.0, mn)
-        scan(R("ln"), R("zs", 1, 257), R("zs", 0, 256), 0.0, mx, ALU.subtract)
-        P2, P3 = R("b2", 0, 256), R("b3", 256, 512)
-        if v < V - 1:
-            hv = [(gh, 128 * gh) for gh in range(2)]
-            mm([(P2, R("nI"), R("c3k"), True, False), (P2, R("I25f"), R("zs", 0, 256), False, False)])
-            mm([(P2, R("nI"), R("c14"), False, False)]
-               + [(R("b2", c, c + 128), R("nh"), z[gh], False, z is Bm and gh == 1 and not P1P) for z in (A, Bm) for (gh, c) in hv])
-            mm([(P3, R("Ib"), R("c14"), u == 0, False) for u in range(2 if GTV else 1)]
-               + [(R("b3", 256 + c, 384 + c), R("Ib" if GTV else "hI"), A[gh], False, False) for (gh, c) in hv]
-               + [(R("b3", 256 + c, 384 + c), R("nI" if GTV else "nh"), Bm[gh], False, gh == 1) for (gh, c) in hv])
-        n = 8 if v < V - 1 else 4
-        last = {}
-        for gh in range(2):
-            gathers("X", "SG", o0, gh, 0, 128, SGV[v], GCH, last)
-            c, d = 256 * gh, 128 * gh
-            mm([(R("b1", c + s, c + 32 * n, 32), R("X", 4096 * gh + s, 4096 * gh + 4096, 32),
-                 R("RS", 8 * (s == 0), 8 * (s == 0) + n), s == 0, s == 31) for s in range(32)])
-            tt(R("w", d, d + 128), R("b1", c, c + 128), R("ln", d, d + 128), ALU.mult)
-            if v < V - 1:
-                if GTV:
-                    ts(R("gt", d, d + 128), R("b1", c + 128, c + 256), 0.5, ALU.is_gt, 0.5, ALU.subtract)
+            cuts = [128 * h + a + a % 2 for a in cuts]
+            todo = [(a, b, q) for (a, b) in zip(cuts, cuts[1:]) for q in range(2)]
+            if dst == "X":
+                todo.sort(key=lambda z: z[2])
+            for (a, b, q) in todo:
+                out, c = R(dst, 32 * a + q, 32 * b, 2), o0 + 128 * (h + q)
+                src = IND(R(win, TW * h, TW * h + TW), R("OF", c + a, c + b))
+                if dst != "X":
+                    o = (act if e == "A" else cp)(out, src)
+                elif e == "A":
+                    o = act(out, src, scale=-2.0 ** -30)
                 else:
-                    act(R("gt", d, d + 128), R("b1", c + 128, c + 256), ACT.Sign, bias=-0.5)
-        scan(R("b0", 0, 256), R("w"), R("OMS", 256 * v, 256 * v + 256), 0.0, ALU.add, mx)
-        tt(lm(1, 256), R("b0", 0, 255), R("ln", 1, 256), mn)
-        if v == V - 1:
-            return
-        tt(R("mm"), P3, R("gt"), ALU.mult)
-        if P1P:
-            mm([(P2, R("Ib"), R("mm"), False, True)])
-        else:
-            tt(P2, P2, R("mm"), ALU.add)
-        tt(R("lk"), P2, lm(0, 256), mn)
-        scan(R("b0", 256, 512), R("rst"), R("lk"), 0.0, ALU.mult, mx)
-        last = R("b0", 256 + 31, 512, 32)
-        li, a1, a2 = R("li", 0, 8), R("li", 8, 16), R("li", 16, 24)
-        ts(li, last, 2.0 ** 23, ALU.mult)
-        ts(a1, li, 0x7FC, ALU.bitwise_and)
-        ts(a2, li, 21, ALU.arith_shift_right)
-        tt(R("NI", 0, 256, 32), a2, a1, ALU.subtract)
-        scan(R("AN"), R("mk2"), R("NI"), 0.0, ALU.mult, ALU.add)
-        mm([(R("b3", 0, 8), R("AN", 0, 256, 2), R("bk16", 0, 8), True, False),
-            (R("b3", 0, 8), R("AN", 1, 256, 2), R("bk16", 8, 16), False, True)])
-        no = R("NO", 8 * v, 8 * v + 8)
-        ts(no, R("b3", 0, 8), 1024.0, ALU.add)
-        send(R("NL", 8 * v + 8, 8 * v + 16), no, "nm%d" % (v + 1))
-        act(R("YG0"), IND(R("PY"), no))
-        yps = R("b3", 256, 384)
-        mm([(yps, R("YG0"), R("I21"), True, True)])
-        tt(R("dF", 1, 256), R("lk", 1, 256), R("b0", 256, 511), ALU.subtract)
-        ts(R("LI", 0, 128, 16), last, 256.5 * S21, ALU.add)
-        ts(R("e"), R("dF"), 0.0, mx, 2.0 ** 21, ALU.mult)
-        ts(R("e2"), R("e"), 511, ALU.bitwise_and)
-        ts(R("nn"), R("e2"), 1.0, mn, float(MM), ALU.mult)
-        hole = R("b2", 0, 256)
-        if HOV:
-            ts(hole, R("e2"), 0.0, eq, HOLE, ALU.mult)
-        else:
-            act(hole, R("nn"), ACT.Relu, scale=-2.0 / MM, bias=HOLE)
-        scan(R("b0", 0, 256), R("d0c"), R("nn"), -float(MM), mn, ALU.add)
-        tt(R("G"), hole, R("cG"), ALU.mult)
-        tt(R("PN", 0, 256), hole, R("lk"), mx)
-        tt(R("DM", 0, 256), R("b0", 0, 256), R("G"), ALU.add)
-        scan(R("LB"), R("r16"), R("LI"), 0.0, ALU.mult, ALU.add)
-        tt(R("nl"), yps, R("LB"), ALU.is_le)
-        if LTA:
-            act(R("lt"), R("nl"), scale=-float(MM), bias=float(MM))
-        else:
-            ts(R("lt"), R("nl"), -float(MM), ALU.mult, float(MM), ALU.add)
-        ts(R("lt", 0, 128, 16), R("b0", 31, 256, 32), 15.0 * MM, mn)
-        scan(R("b0", 256, 384), R("r16"), R("lt"), 0.0, ALU.mult, ALU.add)
-        tt(R("Gy"), R("b3", 128, 256), R("nl"), ALU.mult)
-        tt(R("PN", 256, 384), yps, R("nl"), mx)
-        tt(R("DM", 256, 384), R("b0", 256, 384), R("Gy"), ALU.add)
-        act(R("b2", 0, 384), R("PN"), bias=-8.0)
-        for (a, b) in YSP:
-            ts(R("y2", a, b), R("DM", a, b), 0x8888, ALU.bitwise_and)
-            ts(R("y3", a, b), R("y2", a, b), float(0x249), ALU.mult)
-            ts(R("y4", a, b), R("y3", a, b), 12, ALU.arith_shift_right, 15, ALU.bitwise_and)
-        tt(R("E0"), R("b2", 0, 384, 2), R("y4", 0, 384, 2), ALU.add)
-        tt(R("b0", 0, 192), R("b2", 1, 384, 2), R("y4", 1, 384, 2), ALU.add)
-        for st in range(3):
-            e0, e1, q0, q1 = "E%d" % (st % 2), "E%d" % (1 - st % 2), 256 * (st % 2), 256 * (1 - st % 2)
-            for (u, dn, d0) in ((0, e1, 0), (1, "b0", q1)):
-                for (d, op) in ((0, mn), (96, mx)):
-                    tt(R(dn, d0 + d, d0 + d + 96), R(e0, u, 192, 2), R("b0", q0 + u, q0 + 192, 2), op)
-        tt(R3("Z", 0, 8, 0, 24), R("E1"), R("b0", 256, 448), mn)
-        tt(R3("Z", 8, 16, 0, 24), R("E1"), R("b0", 256, 448), mx)
-        tt(R("b0", 0, 128), R3("Z", 0, 16, 0, 16, 2), R3("Z", 0, 16, 1, 16, 2), mn)
-        tt(R("XF"), R("b0", 0, 128), R3("Z", 0, 16, 16, 24), mn)
-        ls = R("LS", 128 * v, 128 * v + 128)
-        if FKP:
-            ts(R("xr"), R("XF"), 128 * S21, ALU.subtract, 3072.0, ALU.add)
-            o = R("b1", 0, 128)
-            mm([(o, R("If"), R("ckp"), True, False)])
-            mm([(o, R("III", 0, 128), R("xr"), False, False),
-                (o, R("If"), R("ck"), False, False), (o, R("III", 128, 256), R("xr"), False, False),
-                (o, R("nI"), R("c3m"), False, False), (o, R("III", 256, 384), R("XF"), False, True)])
-            act(ls, o)
-        else:
-            xi, xl, xh = R("y2", 0, 128), R("y2", 128, 256), R("y2", 256, 384)
-            ts(xi, R("XF"), 2.0 ** 25, ALU.mult)
-            ts(xl, xi, 4, ALU.arith_shift_right, 511, ALU.bitwise_and)
-            ts(xh, xi, 0x1FFE000, ALU.bitwise_and)
-            tt(R("b0", 128, 256), R("b2", 384, 512), xl, ALU.subtract)
-            tt(ls, R("b0", 128, 256), xh, ALU.add)
-        send(R("LL", 128 * v + 128, 128 * v + 256), ls, "li%d" % (v + 1))
+                    o = ts(out, src, -2.0 ** -30, ALU.mult)
+                chain(last.get(e, []) + [o])
+                last[e] = [o]
 
-    def whole2(v, h):
+    def whole(v, h, last):
         k = 2 * v + h
         tag[0] = ("w", v, h)
 
@@ -576,27 +392,19 @@ def build(T, rank, core, topo):
         def B(a, b, s=1, p=None):
             return R("b%d" % (1 + h), a, b, s, p)
 
-        def first(name, n):
-            return R(name, 0, n)
-
         o0, l0 = 512 * (v % 2), 256 * (v % 2) + 128 * h
         lm = lambda a, b: R("lm", l0 + a, l0 + b)
         if v > 0 and h == 0:
-            for u in range(2):
-                act(R("PG", 128 * u, 128 * u + 128), IND(R("KT"), R("NL", 16 * v + 8 * u, 16 * v + 8 * u + 8)))
-        if v > 0:
-            mm([(B(0, 64), R("PG", 128 * u, 128 * u + 128), R(("PRa", "Lo1")[u], 64 * h, 64 * h + 64), u == 0, u == 1)
-                for u in range(2)])
-        else:
-            mm([(B(0, 64), R("PG", 0, 128), R("PRb", 64 * h, 64 * h + 64), True, True)])
+            act(R("PG"), IND(R("KT"), R("NL", 8 * v, 8 * v + 8)))
+        mm([(B(0, 64), R("PG"), R("PRa" if v > 0 else "PRb", 64 * h, 64 * h + 64), True, True)])
         lo, hi = R("LL", 64 * k, 64 * k + 64), B(0, 64)
         for st in range(2):
             for (u, op) in ((0, mn), (1, mx)):
                 tt(W("M0", u, 128, 2), lo, hi, op)
             for (u, op) in ((0, mn), (1, mx)):
-                tt(W("Lo0", u, 64, 2), W("M0", 0, 32), W("M0", 64, 96), op)
+                tt(W("M1", u, 64, 2), W("M0", 0, 32), W("M0", 64, 96), op)
                 tt(Q(u, 64, 2), W("M0", 32, 64), W("M0", 96, 128), op)
-            lo, hi = W("Lo0"), Q(0, 64)
+            lo, hi = W("M1"), Q(0, 64)
         for (u, op) in ((0, mn), (1, mx)):
             tt(W("Ks", u, 128, 2), lo, hi, op)
         ts(W("fi"), W("Ks"), 511, ALU.bitwise_and)
@@ -604,93 +412,88 @@ def build(T, rank, core, topo):
         ts(W("SL"), W("Ks"), S21, ALU.mult, 135.5 - 2.0 ** -14, ALU.add)
         ts(W("zs", 0, 128), W("Ks"), 4096.0, ALU.subtract, ZC + 2.0 ** 24, ALU.add)
         act(W("zs", 0, 129, 32), R("onef", 0, 5), scale=ZC + 2.0 ** 25)
-        if QQF:
-            ts(W("qq"), W("fi"), 256.0, ALU.is_lt)
+        if QQA[h]:
+            act(W("qq"), W("dA"), ACT.Relu, scale=-256.0)
         else:
             ts(W("qq"), W("dA"), 0.0, ALU.is_lt)
         A, Bm = W("AB", 0, 128), W("AB", 128, 256)
         scan(A, W("qq"), W("dA"), 0.0, mn, mx)
         scan(Bm, W("qq"), W("dA"), 0.0, ALU.add, mn)
-        mm([(B(128 * q, 128 * q + 128), R("Cst", 256 * q + 128 * h, 256 * q + 128 * h + 128), R("Ib"), q == 0, False)
-            for q in range(2)])
+        mm([(B(128 * q, 128 * q + 128), R("Cst", 128 * q, 128 * q + 128), R("Ib"), q == 0, False) for q in range(2)])
         mm([(B(128 * q, 128 * q + 128, p=HALF[x]), W("SL", q, 128, 2), R("Ib"), False, False)
             for q in range(2) for x in range(2)])
         mm([(B(128 * q, 128 * q + 128), W("AB", q, 256, 2), R("I25"), False, q == 1) for q in range(2)])
-        ts(R("OF", o0 + 256 * h, o0 + 256 * h + 256), B(0, 256), 8192.0, mn)
+        ts(R("OF", o0 + 256 * h, o0 + 256 * h + 256), B(0, 256), 4096.0, mn)
         scan(W("ln"), W("zs", 1, 129), W("zs", 0, 128), 0.0, mx, ALU.subtract)
         P2, P3 = R("b%d" % (3 + h), 0, 128), B(384, 512)
         if v < V - 1:
-            mm([(P2, R("nI"), first("c3k", 128), True, False), (P2, R("I25f"), W("zs", 0, 128), False, False),
-                (P2, R("nI"), first("c14", 128), False, False), (P2, R("nh"), A, False, False),
-                (P2, R("nh"), Bm, False, not P1P)])
-            mm([(P3, R("Ib" if GTV else "hI"), A, True, False), (P3, R("nI" if GTV else "nh"), Bm, False, False)]
-               + [(P3, R("Ib"), first("c14", 128), False, u == 0) for u in range(1 if GTV else 0, -1, -1)])
-        gathers("X", "SG", o0, h, 0, 128, SGV[v], GCH, {})
+            mm([(P2, R("nI"), R("c3k"), True, False), (P2, R("I25f"), W("zs", 0, 128), False, False),
+                (P2, R("nI"), R("c14"), False, False), (P2, R("nh"), A, False, False), (P2, R("nh"), Bm, False, False)])
+            mm([(P3, R("Ib" if GTV[h] else "hI"), A, True, False), (P3, R("nI" if GTV[h] else "nh"), Bm, False, False)]
+               + [(P3, R("Ib"), R("c14"), False, u == 0) for u in range(GTV[h], -1, -1)])
+        gathers("X", "SG", o0, h, 0, 128, SGV[v][h], GCH, last)
         n = 8 if v < V - 1 else 4
-        mm([(B(s, 32 * n, 32), R("X", 4096 * h + s, 4096 * h + 4096, 32), R("RS", 8 * (s == 0), 8 * (s == 0) + n),
-             s == 0, s == 31) for s in range(32)])
+        for q in range(2):
+            mm([(B(s, 32 * n, 32), R("X", 4096 * h + s, 4096 * h + 4096, 32), R("RS", 8 * (s == 0), 8 * (s == 0) + n),
+                 s == 0, s == 31) for s in range(q, 32, 2)])
         tt(W("w"), B(0, 128), W("ln"), ALU.mult)
-        if v < V - 1:
-            if GTV:
-                ts(W("gt"), B(128, 256), 0.5, ALU.is_gt, 0.5, ALU.subtract)
-            else:
-                act(W("gt"), B(128, 256), ACT.Sign, bias=-0.5)
+        if v < V - 1 and GTV[h]:
+            ts(W("gt"), B(128, 256), 0.5, ALU.is_gt, 0.5, ALU.subtract)
+        elif v < V - 1:
+            act(W("gt"), B(128, 256), ACT.Sign, bias=-0.5)
         scan(Q(0, 128), W("w"), R("OMS", 128 * k, 128 * k + 128), 0.0, ALU.add, mx)
         tt(lm(1, 128), Q(0, 127), W("ln", 1, 128), mn)
         if v == V - 1:
             return
         tt(W("mm"), P3, W("gt"), ALU.mult)
-        if P1P:
-            mm([(P2, R("Ib"), W("mm"), False, True)])
-        else:
-            tt(P2, P2, W("mm"), ALU.add)
+        mm([(P2, R("Ib"), W("mm"), False, True)])
         tt(W("lk"), P2, lm(0, 128), mn)
-        scan(Q(0, 128), first("rst", 128), W("lk"), 0.0, ALU.mult, mx)
-        last = Q(31, 128, 32)
+        scan(Q(0, 128), R("rst"), W("lk"), 0.0, ALU.mult, mx)
+        end = Q(31, 128, 32)
         li, a1, a2 = W("li", 0, 4), W("li", 4, 8), W("li", 8, 12)
-        ts(li, last, 2.0 ** 23, ALU.mult)
+        ts(li, end, 2.0 ** 23, ALU.mult)
         ts(a1, li, 0x7FC, ALU.bitwise_and)
         ts(a2, li, 21, ALU.arith_shift_right)
         tt(W("NI", 0, 128, 32), a2, a1, ALU.subtract)
-        scan(W("AN"), first("mk2", 128), W("NI"), 0.0, ALU.mult, ALU.add)
+        scan(W("AN"), R("mk2"), W("NI"), 0.0, ALU.mult, ALU.add)
+        o = B(0, 8, p=HALF[h])
+        mm([(o, W("AN", 0, 128, 2), R("bk16", 0, 8), True, False), (o, W("AN", 1, 128, 2), R("bk16", 8, 16), False, True)])
+        no = R("NO", 8 * v, 8 * v + 8)
+        ts(R("NO", 8 * v, 8 * v + 8, p=HALF[h]), o, 1024.0, ALU.add)
+        if h == 1:
+            send(R("NL", 8 * v + 8, 8 * v + 16), no, "nm%d" % (v + 1))
+        act(R("YG%d" % h), IND(R("PY"), no))
         tt(W("dF", 1, 128), W("lk", 1, 128), Q(0, 127), ALU.subtract)
-        ts(W("LI", 0, 64, 16), last, 256.5 * S21, ALU.add)
+        scan(W("LB", 63, -1, -1), R("d16", 63, -1, -1), Q(127, -1, -2), 0.0, mn, mx)
         ts(W("e"), W("dF"), 0.0, mx, 2.0 ** 21, ALU.mult)
         ts(W("e2"), W("e"), 511, ALU.bitwise_and)
         ts(W("nn"), W("e2"), 1.0, mn, float(MM), ALU.mult)
-        o = B(0, 8, p=HALF[h])
-        mm([(o, W("AN", 0, 128, 2), R("bk16", 0, 8), True, False), (o, W("AN", 1, 128, 2), R("bk16", 8, 16), False, True)])
-        no = R("NO", 8 * k, 8 * k + 8)
-        ts(R("NO", 8 * k, 8 * k + 8, p=HALF[h]), o, 1024.0, ALU.add)
-        send(R("NL", 8 * k + 16, 8 * k + 24), no, "nm%d" % (k + 2))
-        act(R("YG%d" % h), IND(R("PY"), no))
         hole = R("b%d" % (3 + h), 128, 256)
-        if HOV:
-            ts(hole, W("e2"), 0.0, eq, HOLE, ALU.mult)
-        else:
-            act(hole, W("nn"), ACT.Relu, scale=-2.0 / MM, bias=HOLE)
-        scan(Q(0, 128), first("d0c", 128), W("nn"), -float(MM), mn, ALU.add)
-        tt(W("G"), hole, first("cG", 128), ALU.mult)
+        act(hole, W("nn"), ACT.Relu, scale=-2.0 / MM, bias=HOLE)
+        scan(Q(0, 128), R("d0c"), W("nn"), -float(MM), mn, ALU.add)
+        tt(W("G"), hole, R("cG"), ALU.mult)
         tt(W("PN", 0, 128), hole, W("lk"), mx)
         tt(W("DM", 0, 128), Q(0, 128), W("G"), ALU.add)
         yps = B(0, 64)
-        mm([(yps, R("YG%d" % h), R("I21", 64 * h, 64 * h + 64), True, True)])
-        scan(W("LB"), first("r16", 64), W("LI"), 0.0, ALU.mult, ALU.add)
-        tt(W("nl"), yps, W("LB"), ALU.is_le)
+        mm([(yps, R("YG%d" % h), R("I21", 64 * h, 64 * h + 64), True, True),
+            (B(64, 128), R("YG%d" % h), R("I21", 64 * h, 64 * h + 64), True, False),
+            (B(64, 128), R("Ib"), R("c22", 0, 64), False, False), (B(64, 128), R("Ib"), R("c22", 64, 128), False, True)])
+        tt(W("nl"), B(64, 128), W("LB"), ALU.is_le)
         if LTA:
             act(W("lt"), W("nl"), scale=-float(MM), bias=float(MM))
         else:
             ts(W("lt"), W("nl"), -float(MM), ALU.mult, float(MM), ALU.add)
         ts(W("lt", 0, 64, 16), Q(31, 128, 32), 15.0 * MM, mn)
-        scan(Q(128, 192), first("r16", 64), W("lt"), 0.0, ALU.mult, ALU.add)
+        scan(Q(128, 192), R("r16"), W("lt"), 0.0, ALU.mult, ALU.add)
         tt(W("Gy"), R("b0", 384, 448), W("nl"), ALU.mult)
         tt(W("PN", 128, 192), yps, W("nl"), mx)
         tt(W("DM", 128, 192), Q(128, 192), W("Gy"), ALU.add)
         act(B(0, 192), W("PN"), bias=-8.0)
         Y = lambda n, a=0, b=192, s=1: R("pxi", 384 * n + 192 * h + a, 384 * n + 192 * h + b, s)
-        ts(Y(0), W("DM"), 0x8888, ALU.bitwise_and)
-        ts(Y(1), Y(0), float(0x249), ALU.mult)
-        ts(Y(2), Y(1), 12, ALU.arith_shift_right, 15, ALU.bitwise_and)
+        for (a, b) in ((0, 128), (128, 192)) if YSP[h] else ((0, 192),):
+            ts(Y(0, a, b), W("DM", a, b), 0x8888, ALU.bitwise_and)
+            ts(Y(1, a, b), Y(0, a, b), float(0x249), ALU.mult)
+            ts(Y(2, a, b), Y(1, a, b), 12, ALU.arith_shift_right, 15, ALU.bitwise_and)
         tt(W("E0"), B(0, 192, 2), Y(2, 0, 192, 2), ALU.add)
         tt(Q(0, 96), B(1, 192, 2), Y(2, 1, 192, 2), ALU.add)
         for st in range(3):
@@ -700,50 +503,40 @@ def build(T, rank, core, topo):
                     dst = W(e1, d, d + 48) if u == 0 else Q(q1 + d, q1 + d + 48)
                     tt(dst, W(e0, u, 96, 2), Q(q0 + u, q0 + 96, 2), op)
         z0 = 16 * h
-        tt(R3("Z2", z0, z0 + 8, 0, 12), W("E1"), Q(96, 192), mn)
-        tt(R3("Z2", z0 + 8, z0 + 16, 0, 12), W("E1"), Q(96, 192), mx)
-        tt(Q(0, 64), R3("Z2", z0, z0 + 16, 0, 8, 2), R3("Z2", z0, z0 + 16, 1, 8, 2), mn)
-        tt(W("XF"), Q(0, 64), R3("Z2", z0, z0 + 16, 8, 12), mn)
-        ls = R("LS", 64 * k, 64 * k + 64)
-        if FKP:
-            ts(W("xr"), W("XF"), 128 * S21, ALU.subtract, 3072.0, ALU.add)
-            o = B(256, 320)
-            mm([(o, R("If"), first("ckp", 64), True, False)])
-            mm([(o, R("III", 0, 128), W("xr"), False, False),
-                (o, R("If"), first("ck", 64), False, False), (o, R("III", 128, 256), W("xr"), False, False),
-                (o, R("nI"), first("c3m", 64), False, False), (o, R("III", 256, 384), W("XF"), False, True)])
-            act(ls, o)
-        else:
-            xi, xl, xh = Y(0, 0, 64), Y(0, 64, 128), Y(0, 128, 192)
-            ts(xi, W("XF"), 2.0 ** 25, ALU.mult)
-            ts(xl, xi, 4, ALU.arith_shift_right, 511, ALU.bitwise_and)
-            ts(xh, xi, 0x1FFE000, ALU.bitwise_and)
-            tt(Q(64, 128), R("b0", 448, 512), xl, ALU.subtract)
-            tt(ls, Q(64, 128), xh, ALU.add)
+        tt(R3("Z", z0, z0 + 8, 0, 12), W("E1"), Q(96, 192), mn)
+        tt(R3("Z", z0 + 8, z0 + 16, 0, 12), W("E1"), Q(96, 192), mx)
+        tt(Q(0, 64), R3("Z", z0, z0 + 16, 0, 8, 2), R3("Z", z0, z0 + 16, 1, 8, 2), mn)
+        tt(W("XF"), Q(0, 64), R3("Z", z0, z0 + 16, 8, 12), mn)
+        ts(W("xr"), W("XF"), 128 * S21, ALU.subtract, 3072.0, ALU.add)
+        o, ls = B(256, 320), R("LS", 64 * k, 64 * k + 64)
+        mm([(o, R("I25"), R("ckb", 64 * u, 64 * u + 64), u == 0, False) for u in range(2)])
+        mm([(o, R("III", 0, 128), W("xr"), False, False), (o, R("Ib"), R("ckb", 128, 192), False, False),
+            (o, R("Ib"), R("ckb", 192, 256), False, False), (o, R("III", 128, 256), W("xr"), False, False),
+            (o, R("nI"), R("c3m"), False, False), (o, R("III", 256, 384), W("XF"), False, True)])
+        act(ls, o)
         send(R("LL", 64 * k + 128, 64 * k + 192), ls, "li%d" % (k + 2))
 
     def spread(v):
         tag[0] = ("f", v, 0)
         l0 = 256 * (v % 2)
-        if SUM[v] == "D":
-            old, new = list(hist.get("S", [])), []
-            for gh in range(2):
-                hist["S"] = list(old)
-                c, d = 4096 * gh, R("S", p=HALF[gh])
-                dma(d, R("X", c, c + 4096, p=HALF[0]), 524288, [d], [R("X", c, c + 4096)])
-                gadd(d, R("X", c, c + 4096, p=HALF[1]), 524288)
-                new += hist["S"][len(old):]
-            hist["S"] = new
-        if v in QUICK:
-            lm, hi, lo = R("lm", l0, l0 + 256), R("HL", 0, 256), R("HL", 256, 512)
-            act(hi, lm)
+        old, new = list(hist.get("S", [])), []
+        for h in range(2):
+            hist["S"] = list(old)
+            c, d = 4096 * h, R("S", p=HALF[h])
+            dma(d, R("X", c, c + 4096, p=HALF[0]), 524288, [d], [R("X", c, c + 4096)])
+            gadd(d, R("X", c, c + 4096, p=HALF[1]), 524288)
+            new += hist["S"][len(old):]
+        hist["S"] = new
+        if v == V - 1:
+            lm, hi, lo, f = R("lm", l0, l0 + 256), R("HL", 0, 256), R("HL", 256, 512), act if QA else cp
+            f(hi, lm)
             mm([(R("b2", 0, 256), R("If"), lm, True, False), (R("b2", 0, 256), R("nI"), hi, False, True)])
-            act(lo, R("b2", 0, 256))
+            f(lo, R("b2", 0, 256))
             mm([(R("b1", 128 * u, 128 * u + 128), R("HL", u, 512, 4), R("Ib"), True, True) for u in range(4)])
-            act(R("LT"), R("b1"))
+            f(R("LT"), R("b1"))
             return
-        w = [dmas([(T.Ld[v % 2, u, :, 1:32], R("lm", l0 + 32 * u + 1, l0 + 32 * u + 32)) for u in range(4 * gh, 4 * gh + 4)],
-                  WLAT / 2, [], [R("lm", l0 + 128 * gh, l0 + 128 * gh + 128)], after=held[v % 2]) for gh in range(2)]
+        w = [dmas([(T.Ld[v % 2, u, :, 1:32], R("lm", l0 + 32 * u + 1, l0 + 32 * u + 32)) for u in range(4 * h, 4 * h + 4)],
+                  WLAT / 2, [], [R("lm", l0 + 128 * h, l0 + 128 * h + 128)], after=held[v % 2]) for h in range(2)]
         held[v % 2] = []
         for h in range(2):
             a = 2048 * ((2 * v + h) % 3)
@@ -755,67 +548,57 @@ def build(T, rank, core, topo):
         tag[0] = ("f", v, h)
         s0, l0, tr = 2048 * h, 2048 * (k % 3), "tr%d" % (k % 4)
         last = {}
-        for gh in range(2):
-            gathers("C%d" % (v % 2), "CO", 512 * (v % 2), gh, 64 * h, 64 * h + 64, COV[v] // 2, CCH, last)
-        to = "tr%d" % ((k + 2) % 4) if ONE[k] == "B" else tr
-        if v in QUICK:
+        for u in range(2):
+            gathers("C%d" % (v % 2), "CO", 512 * (v % 2), u, 64 * h, 64 * h + 64, COV[v] // 2, CCH, last)
+        if v == V - 1:
             for q in range(4):
                 bk = ("b3", "b4")[q % 2]
                 mm([(R(bk, t, 512, 8), R("Sel", 128 * t, 128 * t + 128), R("LT", 128 * q + 64 * h, 128 * q + 64 * h + 64), True, True)
                     if q + t else (R(bk, 0, 512, 8), R("cm"), R("ones", 0, 64), True, True) for t in range(8)])
                 tt(R(tr, q, 2048, 4), R(bk), R("S", s0 + q, s0 + 2048, 4), ALU.mult)
+        to = "tr%d" % ((k + 2) % 4) if ONE[k] == "B" else tr
         for a in range(1536, -1, -512):
-            if v in QUICK:
-                pass
-            elif SUM[v] == "D":
-                if a % PCH == 0:
-                    scan(R(tr, a, a + PCH), R("L", l0 + a, l0 + a + PCH), R("S", s0 + a, s0 + a + PCH), 0.0, mx, ALU.mult)
-            else:
-                bk = bank("s")
-                mm([(R(bk), R("Mm", 128 * gh, 128 * gh + 128), R("X", 4096 * gh + s0 + a, 4096 * gh + s0 + a + 512),
-                     gh == 0, gh == 1) for gh in range(2)])
-                tt(R(tr, a, a + 512), R(bk), R("L", l0 + a, l0 + a + 512), ALU.mult)
-            if ONE[k] == "D":
-                if a % 1024 == 0:
-                    gadd(R(tr, a, a + 1024), R("ones", 0, 1024), 524288)
-            elif ONE[k] in "AB":
-                n = 512 if v == V - 1 else PCH
-                if a % n == 0:
-                    act(R(to, a, a + n), R(tr, a, a + n), bias=1.0)
-            else:
-                ts(R(tr, a, a + 512), R(tr, a, a + 512), 1.0, ALU.add)
+            if v < V - 1:
+                scan(R(tr, a, a + 512), R("L", l0 + a, l0 + a + 512), R("S", s0 + a, s0 + a + 512), 0.0, mx, ALU.mult)
+            if ONE[k] != "D":
+                act(R(to, a, a + 512), R(tr, a, a + 512), bias=1.0)
+            elif a % 1024 == 0:
+                gadd(R(tr, a, a + 1024), R("ones"), 524288)
+
+    nb = [0]
 
     def colour(v, h):
         k = 2 * v + h
         tag[0] = ("f", v, h)
-        tr, C, c0 = "tr%d" % (k % 4), "C%d" % (v % 2), 2048 * h
+        tr, C = "tr%d" % (k % 4), "C%d" % (v % 2)
         t1 = "tr%d" % ((k + 2) % 4) if ONE[k] == "B" else tr
         for a in range(1536, -1, -512):
-            bk = bank("d")
-            c = c0 + a
+            nb[0] += 1
+            bk, c = ("b5", "b6")[nb[0] % 2], 2048 * h + a
             for (u, (m, d)) in enumerate(((0, c + 1), (128, 4096 + c + 1), (256, c), (384, 4096 + c))):
                 mm([(R(bk), R("Mm", m, m + 128), R(C, d, d + 512), u == 0, u == 3)])
-            for c in range(0, 512, FCH):
-                scan(R("Eo", a + c + FCH, a + c, -1), R(t1, a + c + FCH, a + c, -1), R(bk, c + FCH - 1, c - 1, -1),
-                     0.0, ALU.mult, ALU.add)
-        o = 64 * k
-        base = 248.0
+            scan(R("Eo", c + 512, c, -1), R(t1, a + 512, a, -1), R(bk, 511, -1, -1), 0.0, ALU.mult, ALU.add)
         if TAU[k] == "P":
             for s0 in range(1, 32, 2):
                 mm([(R("b7", 0, 64), R("If"), R(tr, s, 2048, 32), s == 1, s == 31) for s in range(s0, min(s0 + 2, 32))])
-            if ONE[k] == "B":
-                base = 0.0
-            src = R("b7", 0, 64)
+            src, base = R("b7", 0, 64), 0.0 if ONE[k] == "B" else 248.0
+        elif TAU[k] == "H":
+            e0 = 2048 * (k % 3)
+            for s0 in range(1, 32, 4):
+                mm([(R("b7", 0, 64), R("If"), R(tr, s, 2048, 32), s == 1, False) for s in (s0, s0 + 2)])
+            for a in range(0, 1024, 256):
+                scan(R("L", e0 + a, e0 + a + 256), R("rs4", 0, 512, 2), R(tr, 2 * a, 2 * a + 512, 2), 0.0, ALU.mult, ALU.add)
+            mm([(R("b7", 0, 64), R("If"), R("L", e0 + 15, e0 + 1024, 16), False, True)])
+            src, base = R("b7", 0, 64), -8.0 if ONE[k] == "B" else 248.0
         else:
             e0 = 2048 * (k % 3)
-            for a in range(e0, e0 + 2048, 512):
-                scan(R("L", a, a + 512), R("rs4"), R(tr, a - e0, a - e0 + 512), 0.0, ALU.mult, ALU.add)
-            src = R("L", e0 + 31, e0 + 2048, 32)
-            if ONE[k] == "B":
-                base = -8.0
+            for a in range(0, 2048, 512):
+                scan(R("L", e0 + a, e0 + a + 512), R("rs4"), R(tr, a, a + 512), 0.0, ALU.mult, ALU.add)
+            src, base = R("L", e0 + 31, e0 + 2048, 32), -8.0 if ONE[k] == "B" else 248.0
+        o = 64 * k
         y = o % 256
         act(R("YT", y, y + 64), src, scale=-8.0, bias=base)
-        (act if YCA else cp)(R("YC", y, y + 64), R("Eo", 1, 2048, 32))
+        (act if YCA and v < V - 1 else cp)(R("YC", y, y + 64), R("Eo", 2048 * h + 1, 2048 * h + 2048, 32))
         if v == V - 1:
             dma(T.yt[:, o:o + 64], R("YT", y, y + 64), 32768, [], [R("YT", y, y + 64)])
             dma(T.yc[:, o:o + 64], R("YC", y, y + 64), 32768, [], [R("YC", y, y + 64)])
@@ -825,21 +608,15 @@ def build(T, rank, core, topo):
                  [], [R("YC", y, y + 128), R("YT", y, y + 128)])
 
     for v in range(V):
-        if TWO:
-            whole2(v, 0)
-            whole2(v, 1)
-        else:
-            whole(v)
+        last = {}
+        for h in range(2):
+            whole(v, h, last)
         spread(v)
         for h in range(2):
             opacity(v, h)
         for h in range(2):
             colour(v, h)
     return ops, nsent[0]
-
-
-YSP = [(0, 384)]
-LSP = [2] * 6
 
 
 def schedule(ops):
@@ -863,7 +640,7 @@ def schedule(ops):
             due = (V - 1 - v) * STAG + (WOFF - h * LAG if kind == "w" else FOFF - h * STAG / 4)
         tail[i] = ops[i]["cost"] + max([gap(i, k) + tail[k] for k in kids[i]] + [ops[i]["lat"], due])
     par = [sorted(o["deps"] | o["ord"]) for o in ops]
-    key = [-tail[i] + JIT * (((i + SEED) * 2654435761 >> 7) % 1000) / 1000.0 for i in range(n)]
+    key = [-x for x in tail]
     best = None
     for it in range(NIT):
         order, st, end = one_pass(ops, par, kids, gap, key)
@@ -873,7 +650,7 @@ def schedule(ops):
         key = [-(back[i] + ops[i]["cost"]) for i in range(n)]
     for i in range(n):
         ops[i]["st"] = best[2][i]
-    return best[0], best[1]
+    return polish(ops, best[0]), best[1]
 
 
 def one_pass(ops, par, kids, gap, key, fwd=True):
@@ -896,21 +673,12 @@ def one_pass(ops, par, kids, gap, key, fwd=True):
         t, e = min((max(free[e], min(rdy[i] for i in pool[e])), e) for e in pool if pool[e])
         i = None
         soon = 1e18
-        when = {k: rdy[k] for k in pool[e]}
-        for f in pool:
-            if f != e and AHEAD:
-                for p in pool[f]:
-                    s = max(free[f], rdy[p], t)
-                    if s < t + AHEAD:
-                        for k in kids[p]:
-                            if left[k] == 1 and ops[k]["e"] == e:
-                                when[k] = max(rdy[k], s + ops[p]["cost"] + gap(p, k), t + 2.0)
-        for k in sorted(when, key=lambda k: (key[k], k)):
-            if when[k] <= t + 1.0 and t + ops[k]["cost"] <= soon + SLACK:
+        for k in sorted(pool[e], key=lambda k: (key[k], k)):
+            if rdy[k] <= t + 1.0 and t + ops[k]["cost"] <= soon + SLACK:
                 i = k
                 break
-            if when[k] > t + 1.0:
-                soon = min(soon, when[k])
+            if rdy[k] > t + 1.0:
+                soon = min(soon, rdy[k])
         if i is None:
             free[e] = min(soon, t + 100.0)
             continue
@@ -931,6 +699,83 @@ def one_pass(ops, par, kids, gap, key, fwd=True):
             if left[k] == 0:
                 pool[ops[k]["e"]].append(k)
     return order, start, end
+
+
+def replay(ops, order, cost):
+    n = len(ops)
+    fin, lat, why = [None] * n, [o["lat"] for o in ops], [None] * n
+    pos, free, cand = dict.fromkeys(order, 0), dict.fromkeys(order, 0.0), dict.fromkeys(order)
+    pipe, end, last = 0.0, 0.0, 0
+    for _ in range(n):
+        bs, be = 1e30, None
+        for e in order:
+            if cand[e] is None and pos[e] < len(order[e]):
+                i, s = order[e][pos[e]], free[e]
+                why[i] = order[e][pos[e] - 1] if pos[e] and e != "X" else None
+                for (d, gp) in ops[i]["in"]:
+                    if fin[d] is None:
+                        s = None
+                        break
+                    if fin[d] + gp + lat[d] > s:
+                        s, why[i] = fin[d] + gp + lat[d], d
+                cand[e] = s
+            if cand[e] is not None and cand[e] < bs:
+                bs, be = cand[e], e
+        if be is None:
+            return 1e30, None, None
+        i = order[be][pos[be]]
+        fin[i] = bs + cost[i]
+        pos[be] += 1
+        cand[be] = None
+        if be != "X":
+            free[be] = fin[i]
+        if ops[i]["dm"]:
+            pipe = max(bs + 1500, pipe) + ops[i]["dm"]
+            lat[i] = max(pipe, fin[i] + 1500) + 500 - fin[i]
+        if fin[i] + lat[i] > end:
+            end, last = fin[i] + lat[i], i
+    return end, why, last
+
+
+def polish(ops, order):
+    for o in ops:
+        o["in"] = [(d, 0.0 if ops[d]["e"] == o["e"] == "P" else GAP1 if ops[d]["e"] == o["e"] and ops[d]["sem"] is None else GAP2)
+                   for d in o["deps"]]
+    costs = [[f * (o["cost"] + CYC * o["gn"] * (gk - GK)) if o["e"] in "VA" else
+              30 + (o["cost"] - 30) * pe / PEC if o["e"] == "P" else o["cost"] for o in ops] for (f, gk, pe) in SPEEDS]
+    runs = [replay(ops, order, c) for c in costs]
+    base = [r[0] for r in runs]
+    now, tried = float(len(runs)), set()
+    for it in range(SWAPS):
+        end, why, i = runs[it % len(runs)]
+        pairs = []
+        while why[i] is not None:
+            a = why[i]
+            if ops[a]["e"] == ops[i]["e"] and a not in ops[i]["deps"] and a not in ops[i]["ord"] and (a, i) not in tried:
+                pairs.append((a, i))
+            i = a
+        if not pairs:
+            tried.clear()
+            continue
+        a, b = pairs[(it * 7919) % len(pairs)]
+        tried.add((a, b))
+        q = order[ops[a]["e"]]
+        p, old = q.index(a), list(q)
+        d = (1, 2, 3, 5, 8)[it // 3 % 5]
+        if it % 2:
+            q.insert(max(p + 1 - d, 0), q.pop(p + 1))
+        else:
+            q.insert(p + d, q.pop(p))
+        m = it % len(runs)
+        new = [replay(ops, order, costs[m])]
+        if new[0][0] < runs[m][0]:
+            new = [new[0] if u == m else replay(ops, order, costs[u]) for u in range(len(runs))]
+        score = sum(r[0] / z for r, z in zip(new, base))
+        if len(new) == len(runs) and score < now:
+            now, runs = score, new
+        else:
+            q[:] = old
+    return order
 
 
 ORDER = []

from concourse.bass import DstId, RemoteDMATransfer
from concourse.mybir import dt, AluOpType, AxisListType, ActivationFunctionType

V = 6
MM = 0x8421
S21 = 2.0 ** -21
HOLE = 1.0 - 2.0 ** -13
ZC = 1.5 * 2.0 ** 36
TW = 4112
SGV = [(40, 72)] + [(0, 12)] * 4 + [(16, 48)]
COV = [0] * 5 + [16]
ONE = "DDDDDDDDAAAB"
TAU = "PPHPPPPVHVVV"
GCH, CCH = 64, 32
LTA, QA, YCA, QQA, GTV, YSP = False, True, True, (0, 0), (0, 0), (0, 1)
CYC, FF, OVH, MINC, GK, PEC = 0.83, 1.0, 62, 16, 1.75, 0.63
GDC, SDC, GBW, WLAT, ADDK, LAT = 1000, 100, 300.0, 1000, 1.4, 3000
SPEEDS, SWAPS = [(1.0, 1.1, 0.42), (1.0, 1.56, 0.42), (1.2, 2.05, 0.5), (1.35, 1.4, 0.58), (1.05, 1.5, 0.7)], 8000
GAP1, GAP2, SLACK = 100.0, 200.0, 250.0
STAG, WOFF, FOFF, LAG, NIT = 33000.0, 30000.0, 4000.0, 3000.0, 8
F32, BF, I32, U16, F16 = "float32", "bfloat16", "int32", "uint16", "float16"

SCRATCH = {}
for _n, _c, _d in [
    ("SG", 2 * TW, BF), ("CO", 2 * TW, BF), ("pxi", 1152, I32), ("fpr", 8, I32),
    ("omi", 48, I32), ("omf", 48, F32), ("omu", 48, U16), ("OMS", 1536, F32), ("KT", 1024, F32), ("PY", 1024, F32),
    ("ones", 1024, BF), ("onef", 128, F32), ("Ib", 128, BF), ("nI", 128, BF), ("I25", 128, BF), ("nh", 128, BF),
    ("hI", 128, BF), ("If", 128, F32), ("I21", 128, F32), ("I25f", 128, F32), ("III", 384, F32),
    ("PRa", 128, F32), ("PRb", 128, F32), ("PL", 128, F32), ("Mm", 512, BF), ("Sel", 1024, BF),
    ("c14", 128, BF), ("c3k", 128, BF), ("c3m", 64, BF), ("ckb", 256, BF), ("cm", 128, BF), ("Cst", 256, BF),
    ("blk", 8, F32), ("blkK", 8, F32), ("blk4", 8, F32), ("bk16", 16, BF), ("RS", 16, BF),
    ("rst", 128, BF), ("r16", 64, BF), ("d16", 64, BF), ("c22", 128, BF), ("rs4", 512, BF), ("d0c", 128, F32), ("cG", 128, F32), ("cGy", 64, F32),
    ("mk2", 128, BF), ("sio", 128, F32), ("pj", 8, I32), ("col", 8, F32),
    ("NO", 48, U16), ("NL", 48, U16), ("LS", 640, F32), ("LL", 768, F32), ("OF", 1024, U16), ("PG", 128, F32),
    ("YG0", 128, F32), ("YG1", 128, F32), ("lm", 512, F32), ("HL", 512, BF), ("LT", 512, BF),
    ("X", 8192, BF), ("S", 4096, BF), ("L", 6144, F32), ("C0", 8208, BF), ("C1", 8208, BF),
    ("tr0", 2056, F32), ("tr1", 2056, F32), ("tr2", 2056, F32), ("tr3", 2056, F32),
    ("Eo", 4098, F32), ("YC", 256, F32), ("YT", 256, F32),
    ("M0", 256, F32), ("M1", 128, F32), ("Ks", 256, I32), ("fi", 256, I32), ("dA", 256, BF), ("qq", 256, BF),
    ("AB", 512, BF), ("SL", 256, BF), ("zs", 272, F32), ("ln", 256, F32), ("w", 256, F32), ("gt", 256, F32),
    ("mm", 256, BF), ("lk", 256, F32), ("dF", 256, F32), ("e", 256, I32), ("e2", 256, I32), ("nn", 256, F32),
    ("G", 256, F32), ("li", 32, I32), ("NI", 256, F16), ("AN", 256, F16), ("LB", 128, F32),
    ("nl", 128, F32), ("lt", 128, F32), ("Gy", 128, F32), ("PN", 384, F32), ("DM", 384, I32), ("E0", 192, F32),
    ("E1", 192, F32), ("XF", 128, F32), ("xr", 128, F32),
]:
    SCRATCH[_n] = ("sbuf", [128, _c], _d)
SCRATCH["Z"] = ("sbuf", [128, 32, 12], F32)
SCRATCH["Ld"] = ("dram", [2, 8, 128, 32], F32)
for _k in range(8):
    SCRATCH["b%d" % _k] = ("psum", [128, 512], F32)

SEMAPHORES = (["sV", "sA", "sP", "sG", "sent"] + ["d%d" % _k for _k in range(90)]
              + ["nm%d" % _k for _k in range(1, V)] + ["li%d" % _k for _k in range(2, 2 * V)])

ALU = AluOpType
ACT = ActivationFunctionType
HALF = ((0, 64), (64, 128))


def R(name, a=0, b=None, s=1, p=None):
    if b is None:
        b = SCRATCH[name][1][1]
    cols = range(a, b, s)
    x = 0
    if abs(s) == 1:
        x = ((1 << len(cols)) - 1) << min(cols)
    else:
        for c in cols:
            x |= 1 << c
    lo, hi = min(cols), max(cols)
    return {"n": name, "a": a, "b": b, "s": s, "p": p, "len": len(cols), "x": x,
            "box": ((1 << (hi - lo + 1)) - 1) << lo, "ps": SCRATCH[name][0] == "psum", "dt": SCRATCH[name][2]}


def R3(name, o0, o1, a, b, s=1):
    w = SCRATCH[name][1][2]
    x = 0
    for k in range(o0, o1):
        for c in range(a, b, s):
            x |= 1 << (w * k + c)
    return {"n": name, "in": (o0, o1, a, b, s), "p": None, "len": (o1 - o0) * len(range(a, b, s)), "x": x,
            "box": ((1 << (w * (o1 - o0))) - 1) << (w * o0), "ps": False, "dt": SCRATCH[name][2]}


def IND(win, off):
    return {"win": win, "off": off, "len": 16 * off["len"], "ps": False, "dt": win["dt"]}


def build(T, rank, core, topo):
    ops = []
    hist = {}
    turns = {}
    tag = [None]

    def ap(r):
        if not isinstance(r, dict):
            return r
        if "win" in r:
            return ap(r["win"]).indirect(ap(r["off"]))
        t = T[r["n"]]
        if "in" in r:
            o0, o1, a, b, s = r["in"]
            return t[:, o0:o1, a:b] if s == 1 else t[:, o0:o1, a:b:s]
        b = None if r["b"] < 0 else r["b"]
        cs = slice(r["a"], b) if r["s"] == 1 else slice(r["a"], b, r["s"])
        ps = slice(None) if r["p"] is None else slice(*r["p"])
        return t[ps, cs]

    def add(eng, fn, outs, ins, cost, lat=0.0, after=(), sem=None, ext=None, dm=0.0):
        me = len(ops)
        reads = []
        for r in ins:
            if isinstance(r, dict):
                reads += [r["win"], r["off"]] if "win" in r else [r]
        deps = set(after)
        for r, wr in [(r, False) for r in reads] + [(r, True) for r in outs]:
            h = hist.setdefault(r["n"], [])
            if r["ps"]:
                turn = turns.setdefault(r["n"], [eng, [], []])
                if turn[0] != eng:
                    turn[:] = [eng, turn[2], []]
                    h[:] = []
                deps.update(turn[1])
                if eng == "P":
                    deps.update(turn[2][-2:])
                if me not in turn[2]:
                    turn[2].append(me)
            for (o, ox, obox, ow) in h:
                if sem is None and (o == me or ops[o]["sem"] is None):
                    if (wr or ow) and (ox & r["x"]):
                        deps.add(o)
                elif (wr or ow) and (obox & r["box"]):
                    deps.add(o)
            if wr and r["p"] is None:
                h[:] = [z for z in h if z[1] & ~r["x"]]
            h.append((me, r["x"], r["box"], wr))
        deps.discard(me)
        ops.append({"e": eng, "fn": fn, "deps": deps, "cost": cost, "lat": lat, "sem": sem, "ext": ext, "ord": set(),
                    "nm": outs[0]["n"] if outs else "-", "tag": tag[0], "dm": dm,
                    "gn": sum(r["len"] for r in ins if isinstance(r, dict) and "win" in r)})
        return me

    def chain(lst):
        for a, b in zip(lst, lst[1:]):
            ops[b]["ord"].add(a)

    def vcost(n, k=1.0):
        return CYC * FF * (OVH + max(n * k, MINC))

    def half(*rs):
        return 0.5 if all(r["dt"] in (BF, U16, F16) for r in rs if isinstance(r, dict)) else 1.0

    def gk(r, k):
        return GK if "win" in r else k

    def ts(out, in0, s1, op0, s2=None, op1=None):
        if op1 is None:
            f = lambda g: g.vector.tensor_scalar(ap(out), ap(in0), ap(s1), None, op0)
        else:
            f = lambda g: g.vector.tensor_scalar(ap(out), ap(in0), ap(s1), ap(s2), op0, op1)
        return add("V", f, [out], [in0, s1, s2], vcost(out["len"], gk(in0, half(out, in0))))

    def tt(out, a, b, op):
        k = 1.0 if (a["ps"] or b["ps"]) else 2.0
        return add("V", lambda g: g.vector.tensor_tensor(ap(out), ap(a), ap(b), op), [out], [a, b], vcost(out["len"], k))

    def cp(out, a):
        return add("V", lambda g: g.vector.tensor_copy(ap(out), ap(a)), [out], [a], vcost(out["len"], gk(a, half(out, a))))

    def ms(out, c):
        return add("V", lambda g: g.vector.memset(ap(out), c), [out], [], vcost(out["len"], half(out)))

    def scan(out, d0, d1, init, op0, op1):
        return add("V", lambda g: g.vector.tensor_tensor_scan(ap(out), ap(d0), ap(d1), init, op0, op1),
                   [out], [d0, d1], vcost(out["len"], half(out, d0, d1)))

    def act(out, a, func=None, bias=None, scale=None):
        kw = {}
        if bias is not None:
            kw["bias"] = bias
        if scale is not None:
            kw["scale"] = scale
        fu = ACT.Identity if func is None else func
        return add("A", lambda g: g.scalar.activation(ap(out), ap(a), fu, **{u: ap(kw[u]) for u in kw}), [out], [a, bias],
                   vcost(out["len"] + 20, gk(a, 1.0)))

    def mm(lst):
        def f(g):
            r = None
            for (o, l, h, st, sp) in lst:
                r = g.tensor.matmul(ap(o), ap(l), ap(h), st, sp)
            return r
        c = sum(max(min(64, l["len"]), h["len"]) * (4 if l["dt"] == F32 else 1) for (o, l, h, st, sp) in lst)
        return add("P", f, [x[0] for x in lst], [x[1] for x in lst] + [x[2] for x in lst], 30 + PEC * c)

    def iota(out, pat, base, ch):
        if out["dt"] == I32:
            f = lambda g: g.iota(ap(out), pat, base, ch)
        else:
            f = lambda g: g.iota(ap(out), pat, base, ch, allow_small_or_imprecise_dtypes=True)
        return add("G", f, [out], [], 150 + 2 * out["len"])

    def sel(out, a, pat, op, base, ch):
        return add("G", lambda g: g.affine_select(ap(out), ap(a), pat, op, 0.0, base, ch), [out], [a], 200 + 2 * out["len"])

    nd = [0]

    def dmas(lst, busy, outs, ins, after=()):
        s = "d%d" % nd[0]
        nd[0] += 1

        def f(g):
            r = None
            for (u, (o, a)) in enumerate(lst):
                r = g.sync.dma_start(ap(o), ap(a))
                if u < len(lst) - 1 and r is not None:
                    r.then_inc(T.sem[s], 16)
            return r
        return add("S", f, outs, ins, SDC * len(lst), lat=2000 + busy, sem=(s, 16 * len(lst)), after=after, dm=busy)

    def dma(out, src, nbytes, outs, ins):
        return dmas([(out, src)], nbytes / GBW, outs, ins)

    def gadd(out, src, nbytes):
        s = "d%d" % nd[0]
        nd[0] += 1
        f = lambda g: g.dma_start(ap(out), ap(src), accum_op=ALU.add, max_dma_last_dim=4096)
        return add("G", f, [out], [src, out], GDC, lat=2000 + ADDK * nbytes / GBW, sem=(s, 16), dm=ADDK * nbytes / GBW)

    def load(name, src):
        for h in range(2):
            dmas([(R(name, TW * h, TW * h + 4096, p=HALF[x]), src[64 * h:64 * h + 64, :]) for x in range(2)],
                 1048576 / GBW, [R(name, TW * h, TW * h + 4096)], [])

    dma(R("DM", 0, 128), T.ls[:], 65536, [R("DM", 0, 128)], [])
    dma(R("fpr"), T.fp[:], 20000, [R("fpr")], [])
    dma(R("pxi", 0, 1024), T.px[:], 524288, [R("pxi", 0, 1024)], [])
    load("SG", T.sg)
    dma(R("omi"), T.om[:], 30000, [R("omi")], [])
    load("CO", T.co)
    chain(list(range(len(ops))))

    eq, mn, mx = ALU.is_equal, ALU.min, ALU.max
    iota(R("pj", 0, 1), [[0, 1]], 0, 1)
    iota(R("onef"), [[0, 128]], 1, 0)
    sel(R("PL"), R("onef"), [[-64, 2], [-1, 16], [-16, 4]], eq, 0, 1)
    sel(R("PRb"), R("onef"), [[-64, 2], [1, 16], [-16, 4]], eq, -15, 1)
    sel(R("PRa"), R("onef"), [[-64, 2], [1, 16], [-16, 4]], eq, 1, 1)
    sel(R("PRa", 0, 64, 4), R("onef", 0, 16), [[1, 16]], eq, -127, 1)
    sel(R("If"), R("onef"), [[-1, 128]], eq, 0, 1)
    sel(R("blk"), R("onef", 0, 8), [[-16, 8]], ALU.is_ge, 0, 1)
    sel(R("blk"), R("blk"), [[16, 8]], ALU.is_ge, 15, -1)
    ms(R("ones"), 1.0)
    iota(R("Cst"), [[0, 2], [4096, 2], [0, 64]], -128, 0)
    iota(R("Cst", 0, 128, 16), [[4096, 2], [0, 4]], 16384 - 128, 0)
    iota(R("e2", 0, 48), [[1, 48]], 0, 0)
    sel(R("HL", p=(0, 16)), R("ones", 0, 512, p=(0, 16)), [[0, 32], [-1, 16]], eq, 0, 1)
    sel(R("rst"), R("ones", 0, 128), [[0, 4], [1, 32]], ALU.is_gt, 0, 0)
    sel(R("r16"), R("ones", 0, 64), [[0, 4], [1, 16]], ALU.is_gt, 0, 0)
    sel(R("rs4"), R("ones", 0, 512), [[0, 16], [1, 32]], ALU.is_gt, 0, 0)
    iota(R("sio"), [[0, 4], [1, 32]], 0, 0)
    iota(R("cGy"), [[0, 4], [-1, 16]], 16, 0)
    for x in range(2):
        sel(R("Mm", 0, 256, p=HALF[x]), R("ones", 0, 256, p=HALF[x]), [[64, 2], [-1, 128]], eq, 0, 1)
        for u in range(0, 1024, 512):
            sel(R("Sel", u, u + 512, p=HALF[x]), R("ones", 0, 512, p=HALF[x]), [[-1, 4], [-8, 8], [0, 16]], eq, -u // 128, 1)
    for u in range(8):
        iota(R("ckb", u, 64, 8), [[-1, 2], [-2, 2], [-4, 2]], 8 - 8 * (u // 4), 0)
    iota(R("ckb", 64, 128), [[0, 64]], -3072, 0)
    iota(R("ckb", 128, 192), [[512, 16], [0, 4]], 512, 0)
    ts(R("pj", 1, 2), R("pj", 0, 1), 15, ALU.bitwise_and)
    jj = R("pj", 1, 2)
    ts(R("col", 0, 1), jj, 512.0, ALU.mult, -2.0 ** 24, ALU.add)
    ts(R("col", 1, 2), jj, 512.0, ALU.mult, 256.0 - 2.0 ** 24, ALU.add)
    ts(R("col", 4, 5), jj, 2.0, ALU.mult)
    for (n, c) in (("Ib", 1.0), ("I25", 2.0 ** 25), ("hI", 0.5), ("nh", -0.5), ("nI", -1.0), ("I25f", 2.0 ** -25), ("I21", S21)):
        act(R(n), R("If"), scale=c)
    for (u, c) in enumerate((2.0 ** 25, 2.0 ** 21, -2.0 ** 21)):
        act(R("III", 128 * u, 128 * u + 128), R("If"), scale=c)
    for (n, c) in (("c14", -128 * S21), ("c3k", ZC * 2.0 ** -25), ("cm", 2.0 ** 18)):
        act(R(n), R("onef"), scale=c)
    act(R("c3m"), R("onef", 0, 64), scale=3072.0 * 2 ** 21)
    act(R("ckb", 192, 256), R("onef", 0, 64), scale=-2.0 ** 24)
    act(R("bk16", 0, 8), R("blk"))
    act(R("bk16", 8, 16), R("blk"), scale=-1.0)
    act(R("blkK"), R("blk"), scale=2.0 ** 25)
    tt(R("blk4", 0, 4), R("blk", 0, 4), R("blk", 4, 8), ALU.add)
    tt(R("blk4", 4, 8), R("blk", 4, 8), R("blk", 0, 4), ALU.subtract)
    act(R("RS", 0, 4), R("blk4", 0, 4), scale=2.0 ** 42)
    act(R("RS", 4, 8), R("blk4", 4, 8), scale=-2.0 ** 30)
    act(R("RS", 8, 12), R("blk4", 0, 4), scale=-2.0 ** 45)
    act(R("RS", 12, 16), R("blk4", 0, 4), scale=0.0)
    act(R("d0c"), R("rst"), scale=2.0 ** 30, bias=-float(MM))
    act(R("cG"), R("sio"), scale=-MM / HOLE, bias=32.0 * MM / HOLE)
    act(R("b0", 384, 448), R("cGy"), scale=float(MM))
    act(R("Mm", 256, 512), R("Mm", 0, 256), scale=-1.0)
    for h in range(2):
        iota(R("SG", TW * h + 4096, TW * h + TW), [[0, 16]], 16, 0)
        iota(R("CO", TW * h + 4096, TW * h + TW), [[0, 16]], 0, 0)
        iota(R("C%d" % h, 8192, 8200), [[0, 8]], 0, 0)
    for u in range(4):
        iota(R("tr%d" % u, 2048, 2056), [[0, 8]], 0, 0)
    ms(R("NO"), 0)
    ms(R("lm", 0, 512, 128), -2.0 ** 25)
    ms(R("NI"), 0.0)
    act(R("c22", 0, 64), R("onef", 0, 64), scale=-256 * S21)
    act(R("c22", 64, 128), R("onef", 0, 64), scale=-0.5 * S21)
    sel(R("d16"), R("ones", 0, 64), [[0, 4], [-1, 16]], ALU.is_gt, 15, 0)
    ts(R("mk2"), R("sio"), R("col", 4, 5), ALU.is_le)
    sel(R("mk2"), R("mk2"), [[0, 4], [1, 32]], ALU.is_gt, 0, 0)
    act(R("tr1", 0, 512), R("ones", 0, 512), scale=2.0 ** 25)
    held = [[dma(T.Ld[:], R("tr1", 0, 512), 262144, [], [R("tr1", 0, 512)])]] * 2
    iota(R("OMS", 0, 256), [[0, 256]], 0, 0)
    iota(R("OMS", 256, 1536), [[0, 1280]], 0, 0)
    cp(R("omu"), R("e2", 0, 48))
    cp(R("omf"), R("omi"))
    act(R("Eo", 1024, 1792), IND(R("omf"), R("omu")))
    mm([(R("b5"), R("HL", 0, 128, p=(0, 16)), R("HL", p=(0, 16)), True, True)])
    tt(R("Eo", 0, 256), R("b5", 0, 256), R("Eo", 1024, 1280), ALU.mult)
    tt(R("Eo", 256, 768), R("b5"), R("Eo", 1280, 1792), ALU.mult)
    for (k0, k1, bk) in ((0, 1, "b6"), (1, V, "b7")):
        mm([(R(bk, 8 * k, 8 * k + 8), R("Eo", 128 * k, 128 * k + 128), R("blkK"), True, True) for k in range(k0, k1)])
        act(R("OMS", 256 * k0, 256 * k1, 32), R(bk, 8 * k0, 8 * k1))

    def keys(out, src, ti, tf, c):
        ts(R(ti, 0, 128), src, 0xFFF00, ALU.bitwise_and)
        ts(R(tf, 0, 128), R(ti, 0, 128), 31.0, ALU.mult, c, ALU.add)
        tt(out, R(tf, 0, 128), src, ALU.add)

    keys(R("lk", 0, 128), R("DM", 0, 128), "e", "dF", R("col", 1, 2))
    ms(R("dF", 0, 256, 128), -1.0)
    mm([(R("b4", 0, 128), R("lk", 0, 128), R("PL"), True, True)])
    cp(R("LL", 0, 128), R("b4", 0, 128))
    cp(R("NL", 0, 8), R("fpr"))
    cp(R("DM", 128, 256), IND(R("pxi", 0, 1024), R("NL", 0, 8)))
    keys(R("PG"), R("DM", 128, 256), "fi", "w", R("col", 0, 1))
    for a in range(0, 1024, 512):
        px, hi = R("pxi", a, a + 512), R("tr3", 1024 + a, 1536 + a)
        ts(hi, px, 127.5, ALU.subtract, 1.5 * 2.0 ** 31, ALU.add)
        act(hi, hi, bias=-1.5 * 2.0 ** 31)
        act(R("b5"), hi, scale=3.0, bias=256.0)
        tt(R("PY", a, a + 512), R("b5"), px, ALU.subtract)
        act(R("b6"), hi, scale=31.0, bias=R("col", 0, 1))
        tt(R("tr3", a, a + 512), R("b6"), px, ALU.add)
    dmas([(R("KT", p=(0, 112)), R("tr3", 0, 1024, p=(16, 128))), (R("KT", p=(112, 128)), R("tr3", 0, 1024, p=(0, 16)))],
         524288 / GBW, [R("KT")], [R("tr3", 0, 1024)])

    nxt = T.cores[(rank + 1) % len(T.cores)]
    rid, pid = topo.addr(nxt)[0], topo.addr(nxt)[1]
    msk = topo.mask(core, nxt)
    neng = len(topo.engines(core, nxt))
    nsent = [0]

    def send(dst, src, sem):
        f = lambda g: g.remote_dma(ap(dst), ap(src), T.sem[sem], T.sem.sent, pid, rid, msk)
        nsent[0] += neng
        o = add("G", f, [], [src], 600, sem=("", 0))
        return add("X", None, [dst], [], 0, lat=LAT + (8 * src["len"] + 200 if src["dt"] == F32 else 0), after=[o],
                   ext=(sem, neng), sem=("", 0))

    def gathers(dst, win, o0, h, l0, l1, nv, step, last):
        for (e, p0, p1) in (("A", l0, l1 - nv), ("V", l1 - nv, l1)):
            n = -(-(p1 - p0) // step)
            cuts = [p0 + (p1 - p0) * k // max(n, 1) for k in range(n + 1)]
            cuts = [128 * h + a + a % 2 for a in cuts]
            todo = [(a, b, q) for (a, b) in zip(cuts, cuts[1:]) for q in range(2)]
            if dst == "X":
                todo.sort(key=lambda z: z[2])
            for (a, b, q) in todo:
                out, c = R(dst, 32 * a + q, 32 * b, 2), o0 + 128 * (h + q)
                src = IND(R(win, TW * h, TW * h + TW), R("OF", c + a, c + b))
                if dst != "X":
                    o = (act if e == "A" else cp)(out, src)
                elif e == "A":
                    o = act(out, src, scale=-2.0 ** -30)
                else:
                    o = ts(out, src, -2.0 ** -30, ALU.mult)
                chain(last.get(e, []) + [o])
                last[e] = [o]

    def whole(v, h, last):
        k = 2 * v + h
        tag[0] = ("w", v, h)

        def W(name, a=0, b=None, s=1):
            n = SCRATCH[name][1][1] // 2
            return R(name, n * h + a, n * h + (n if b is None else b), s)

        def Q(a, b, s=1):
            return R("b0", 192 * h + a, 192 * h + b, s)

        def B(a, b, s=1, p=None):
            return R("b%d" % (1 + h), a, b, s, p)

        o0, l0 = 512 * (v % 2), 256 * (v % 2) + 128 * h
        lm = lambda a, b: R("lm", l0 + a, l0 + b)
        if v > 0 and h == 0:
            act(R("PG"), IND(R("KT"), R("NL", 8 * v, 8 * v + 8)))
        mm([(B(0, 64), R("PG"), R("PRa" if v > 0 else "PRb", 64 * h, 64 * h + 64), True, True)])
        lo, hi = R("LL", 64 * k, 64 * k + 64), B(0, 64)
        for st in range(2):
            for (u, op) in ((0, mn), (1, mx)):
                tt(W("M0", u, 128, 2), lo, hi, op)
            for (u, op) in ((0, mn), (1, mx)):
                tt(W("M1", u, 64, 2), W("M0", 0, 32), W("M0", 64, 96), op)
                tt(Q(u, 64, 2), W("M0", 32, 64), W("M0", 96, 128), op)
            lo, hi = W("M1"), Q(0, 64)
        for (u, op) in ((0, mn), (1, mx)):
            tt(W("Ks", u, 128, 2), lo, hi, op)
        ts(W("fi"), W("Ks"), 511, ALU.bitwise_and)
        ts(W("dA"), W("fi"), 256.0, ALU.subtract, S21, ALU.mult)
        ts(W("SL"), W("Ks"), S21, ALU.mult, 135.5 - 2.0 ** -14, ALU.add)
        ts(W("zs", 0, 128), W("Ks"), 4096.0, ALU.subtract, ZC + 2.0 ** 24, ALU.add)
        act(W("zs", 0, 129, 32), R("onef", 0, 5), scale=ZC + 2.0 ** 25)
        if QQA[h]:
            act(W("qq"), W("dA"), ACT.Relu, scale=-256.0)
        else:
            ts(W("qq"), W("dA"), 0.0, ALU.is_lt)
        A, Bm = W("AB", 0, 128), W("AB", 128, 256)
        scan(A, W("qq"), W("dA"), 0.0, mn, mx)
        scan(Bm, W("qq"), W("dA"), 0.0, ALU.add, mn)
        mm([(B(128 * q, 128 * q + 128), R("Cst", 128 * q, 128 * q + 128), R("Ib"), q == 0, False) for q in range(2)])
        mm([(B(128 * q, 128 * q + 128, p=HALF[x]), W("SL", q, 128, 2), R("Ib"), False, False)
            for q in range(2) for x in range(2)])
        mm([(B(128 * q, 128 * q + 128), W("AB", q, 256, 2), R("I25"), False, q == 1) for q in range(2)])
        ts(R("OF", o0 + 256 * h, o0 + 256 * h + 256), B(0, 256), 4096.0, mn)
        scan(W("ln"), W("zs", 1, 129), W("zs", 0, 128), 0.0, mx, ALU.subtract)
        P2, P3 = R("b%d" % (3 + h), 0, 128), B(384, 512)
        if v < V - 1:
            mm([(P2, R("nI"), R("c3k"), True, False), (P2, R("I25f"), W("zs", 0, 128), False, False),
                (P2, R("nI"), R("c14"), False, False), (P2, R("nh"), A, False, False), (P2, R("nh"), Bm, False, False)])
            mm([(P3, R("Ib" if GTV[h] else "hI"), A, True, False), (P3, R("nI" if GTV[h] else "nh"), Bm, False, False)]
               + [(P3, R("Ib"), R("c14"), False, u == 0) for u in range(GTV[h], -1, -1)])
        gathers("X", "SG", o0, h, 0, 128, SGV[v][h], GCH, last)
        n = 8 if v < V - 1 else 4
        for q in range(2):
            mm([(B(s, 32 * n, 32), R("X", 4096 * h + s, 4096 * h + 4096, 32), R("RS", 8 * (s == 0), 8 * (s == 0) + n),
                 s == 0, s == 31) for s in range(q, 32, 2)])
        tt(W("w"), B(0, 128), W("ln"), ALU.mult)
        if v < V - 1 and GTV[h]:
            ts(W("gt"), B(128, 256), 0.5, ALU.is_gt, 0.5, ALU.subtract)
        elif v < V - 1:
            act(W("gt"), B(128, 256), ACT.Sign, bias=-0.5)
        scan(Q(0, 128), W("w"), R("OMS", 128 * k, 128 * k + 128), 0.0, ALU.add, mx)
        tt(lm(1, 128), Q(0, 127), W("ln", 1, 128), mn)
        if v == V - 1:
            return
        tt(W("mm"), P3, W("gt"), ALU.mult)
        mm([(P2, R("Ib"), W("mm"), False, True)])
        tt(W("lk"), P2, lm(0, 128), mn)
        scan(Q(0, 128), R("rst"), W("lk"), 0.0, ALU.mult, mx)
        end = Q(31, 128, 32)
        li, a1, a2 = W("li", 0, 4), W("li", 4, 8), W("li", 8, 12)
        ts(li, end, 2.0 ** 23, ALU.mult)
        ts(a1, li, 0x7FC, ALU.bitwise_and)
        ts(a2, li, 21, ALU.arith_shift_right)
        tt(W("NI", 0, 128, 32), a2, a1, ALU.subtract)
        scan(W("AN"), R("mk2"), W("NI"), 0.0, ALU.mult, ALU.add)
        o = B(0, 8, p=HALF[h])
        mm([(o, W("AN", 0, 128, 2), R("bk16", 0, 8), True, False), (o, W("AN", 1, 128, 2), R("bk16", 8, 16), False, True)])
        no = R("NO", 8 * v, 8 * v + 8)
        ts(R("NO", 8 * v, 8 * v + 8, p=HALF[h]), o, 1024.0, ALU.add)
        if h == 1:
            send(R("NL", 8 * v + 8, 8 * v + 16), no, "nm%d" % (v + 1))
        act(R("YG%d" % h), IND(R("PY"), no))
        tt(W("dF", 1, 128), W("lk", 1, 128), Q(0, 127), ALU.subtract)
        scan(W("LB", 63, -1, -1), R("d16", 63, -1, -1), Q(127, -1, -2), 0.0, mn, mx)
        ts(W("e"), W("dF"), 0.0, mx, 2.0 ** 21, ALU.mult)
        ts(W("e2"), W("e"), 511, ALU.bitwise_and)
        ts(W("nn"), W("e2"), 1.0, mn, float(MM), ALU.mult)
        hole = R("b%d" % (3 + h), 128, 256)
        act(hole, W("nn"), ACT.Relu, scale=-2.0 / MM, bias=HOLE)
        scan(Q(0, 128), R("d0c"), W("nn"), -float(MM), mn, ALU.add)
        tt(W("G"), hole, R("cG"), ALU.mult)
        tt(W("PN", 0, 128), hole, W("lk"), mx)
        tt(W("DM", 0, 128), Q(0, 128), W("G"), ALU.add)
        yps = B(0, 64)
        mm([(yps, R("YG%d" % h), R("I21", 64 * h, 64 * h + 64), True, True),
            (B(64, 128), R("YG%d" % h), R("I21", 64 * h, 64 * h + 64), True, False),
            (B(64, 128), R("Ib"), R("c22", 0, 64), False, False), (B(64, 128), R("Ib"), R("c22", 64, 128), False, True)])
        tt(W("nl"), B(64, 128), W("LB"), ALU.is_le)
        if LTA:
            act(W("lt"), W("nl"), scale=-float(MM), bias=float(MM))
        else:
            ts(W("lt"), W("nl"), -float(MM), ALU.mult, float(MM), ALU.add)
        ts(W("lt", 0, 64, 16), Q(31, 128, 32), 15.0 * MM, mn)
        scan(Q(128, 192), R("r16"), W("lt"), 0.0, ALU.mult, ALU.add)
        tt(W("Gy"), R("b0", 384, 448), W("nl"), ALU.mult)
        tt(W("PN", 128, 192), yps, W("nl"), mx)
        tt(W("DM", 128, 192), Q(128, 192), W("Gy"), ALU.add)
        act(B(0, 192), W("PN"), bias=-8.0)
        Y = lambda n, a=0, b=192, s=1: R("pxi", 384 * n + 192 * h + a, 384 * n + 192 * h + b, s)
        for (a, b) in ((0, 128), (128, 192)) if YSP[h] else ((0, 192),):
            ts(Y(0, a, b), W("DM", a, b), 0x8888, ALU.bitwise_and)
            ts(Y(1, a, b), Y(0, a, b), float(0x249), ALU.mult)
            ts(Y(2, a, b), Y(1, a, b), 12, ALU.arith_shift_right, 15, ALU.bitwise_and)
        tt(W("E0"), B(0, 192, 2), Y(2, 0, 192, 2), ALU.add)
        tt(Q(0, 96), B(1, 192, 2), Y(2, 1, 192, 2), ALU.add)
        for st in range(3):
            e0, e1, q0, q1 = "E%d" % (st % 2), "E%d" % (1 - st % 2), 96 * (st % 2), 96 * (1 - st % 2)
            for u in range(2):
                for (d, op) in ((0, mn), (48, mx)):
                    dst = W(e1, d, d + 48) if u == 0 else Q(q1 + d, q1 + d + 48)
                    tt(dst, W(e0, u, 96, 2), Q(q0 + u, q0 + 96, 2), op)
        z0 = 16 * h
        tt(R3("Z", z0, z0 + 8, 0, 12), W("E1"), Q(96, 192), mn)
        tt(R3("Z", z0 + 8, z0 + 16, 0, 12), W("E1"), Q(96, 192), mx)
        tt(Q(0, 64), R3("Z", z0, z0 + 16, 0, 8, 2), R3("Z", z0, z0 + 16, 1, 8, 2), mn)
        tt(W("XF"), Q(0, 64), R3("Z", z0, z0 + 16, 8, 12), mn)
        ts(W("xr"), W("XF"), 128 * S21, ALU.subtract, 3072.0, ALU.add)
        o, ls = B(256, 320), R("LS", 64 * k, 64 * k + 64)
        mm([(o, R("I25"), R("ckb", 64 * u, 64 * u + 64), u == 0, False) for u in range(2)])
        mm([(o, R("III", 0, 128), W("xr"), False, False), (o, R("Ib"), R("ckb", 128, 192), False, False),
            (o, R("Ib"), R("ckb", 192, 256), False, False), (o, R("III", 128, 256), W("xr"), False, False),
            (o, R("nI"), R("c3m"), False, False), (o, R("III", 256, 384), W("XF"), False, True)])
        act(ls, o)
        send(R("LL", 64 * k + 128, 64 * k + 192), ls, "li%d" % (k + 2))

    def spread(v):
        tag[0] = ("f", v, 0)
        l0 = 256 * (v % 2)
        old, new = list(hist.get("S", [])), []
        for h in range(2):
            hist["S"] = list(old)
            c, d = 4096 * h, R("S", p=HALF[h])
            dma(d, R("X", c, c + 4096, p=HALF[0]), 524288, [d], [R("X", c, c + 4096)])
            gadd(d, R("X", c, c + 4096, p=HALF[1]), 524288)
            new += hist["S"][len(old):]
        hist["S"] = new
        if v == V - 1:
            lm, hi, lo, f = R("lm", l0, l0 + 256), R("HL", 0, 256), R("HL", 256, 512), act if QA else cp
            f(hi, lm)
            mm([(R("b2", 0, 256), R("If"), lm, True, False), (R("b2", 0, 256), R("nI"), hi, False, True)])
            f(lo, R("b2", 0, 256))
            mm([(R("b1", 128 * u, 128 * u + 128), R("HL", u, 512, 4), R("Ib"), True, True) for u in range(4)])
            f(R("LT"), R("b1"))
            return
        w = [dmas([(T.Ld[v % 2, u, :, 1:32], R("lm", l0 + 32 * u + 1, l0 + 32 * u + 32)) for u in range(4 * h, 4 * h + 4)],
                  WLAT / 2, [], [R("lm", l0 + 128 * h, l0 + 128 * h + 128)], after=held[v % 2]) for h in range(2)]
        held[v % 2] = []
        for h in range(2):
            a = 2048 * ((2 * v + h) % 3)
            held[v % 2].append(dmas([(R("L", a, a + 2048, p=(i, 128, 16)), T.Ld[v % 2, :, 64 * h:64 * h + 64, :])
                                     for i in range(16)], 1048576 / GBW, [R("L", a, a + 2048)], [], after=w))

    def opacity(v, h):
        k = 2 * v + h
        tag[0] = ("f", v, h)
        s0, l0, tr = 2048 * h, 2048 * (k % 3), "tr%d" % (k % 4)
        last = {}
        for u in range(2):
            gathers("C%d" % (v % 2), "CO", 512 * (v % 2), u, 64 * h, 64 * h + 64, COV[v] // 2, CCH, last)
        if v == V - 1:
            for q in range(4):
                bk = ("b3", "b4")[q % 2]
                mm([(R(bk, t, 512, 8), R("Sel", 128 * t, 128 * t + 128), R("LT", 128 * q + 64 * h, 128 * q + 64 * h + 64), True, True)
                    if q + t else (R(bk, 0, 512, 8), R("cm"), R("ones", 0, 64), True, True) for t in range(8)])
                tt(R(tr, q, 2048, 4), R(bk), R("S", s0 + q, s0 + 2048, 4), ALU.mult)
        to = "tr%d" % ((k + 2) % 4) if ONE[k] == "B" else tr
        for a in range(1536, -1, -512):
            if v < V - 1:
                scan(R(tr, a, a + 512), R("L", l0 + a, l0 + a + 512), R("S", s0 + a, s0 + a + 512), 0.0, mx, ALU.mult)
            if ONE[k] != "D":
                act(R(to, a, a + 512), R(tr, a, a + 512), bias=1.0)
            elif a % 1024 == 0:
                gadd(R(tr, a, a + 1024), R("ones"), 524288)

    nb = [0]

    def colour(v, h):
        k = 2 * v + h
        tag[0] = ("f", v, h)
        tr, C = "tr%d" % (k % 4), "C%d" % (v % 2)
        t1 = "tr%d" % ((k + 2) % 4) if ONE[k] == "B" else tr
        for a in range(1536, -1, -512):
            nb[0] += 1
            bk, c = ("b5", "b6")[nb[0] % 2], 2048 * h + a
            for (u, (m, d)) in enumerate(((0, c + 1), (128, 4096 + c + 1), (256, c), (384, 4096 + c))):
                mm([(R(bk), R("Mm", m, m + 128), R(C, d, d + 512), u == 0, u == 3)])
            scan(R("Eo", c + 512, c, -1), R(t1, a + 512, a, -1), R(bk, 511, -1, -1), 0.0, ALU.mult, ALU.add)
        if TAU[k] == "P":
            for s0 in range(1, 32, 2):
                mm([(R("b7", 0, 64), R("If"), R(tr, s, 2048, 32), s == 1, s == 31) for s in range(s0, min(s0 + 2, 32))])
            src, base = R("b7", 0, 64), 0.0 if ONE[k] == "B" else 248.0
        elif TAU[k] == "H":
            e0 = 2048 * (k % 3)
            for s0 in range(1, 32, 4):
                mm([(R("b7", 0, 64), R("If"), R(tr, s, 2048, 32), s == 1, False) for s in (s0, s0 + 2)])
            for a in range(0, 1024, 256):
                scan(R("L", e0 + a, e0 + a + 256), R("rs4", 0, 512, 2), R(tr, 2 * a, 2 * a + 512, 2), 0.0, ALU.mult, ALU.add)
            mm([(R("b7", 0, 64), R("If"), R("L", e0 + 15, e0 + 1024, 16), False, True)])
            src, base = R("b7", 0, 64), -8.0 if ONE[k] == "B" else 248.0
        else:
            e0 = 2048 * (k % 3)
            for a in range(0, 2048, 512):
                scan(R("L", e0 + a, e0 + a + 512), R("rs4"), R(tr, a, a + 512), 0.0, ALU.mult, ALU.add)
            src, base = R("L", e0 + 31, e0 + 2048, 32), -8.0 if ONE[k] == "B" else 248.0
        o = 64 * k
        y = o % 256
        act(R("YT", y, y + 64), src, scale=-8.0, bias=base)
        (act if YCA and v < V - 1 else cp)(R("YC", y, y + 64), R("Eo", 2048 * h + 1, 2048 * h + 2048, 32))
        if v == V - 1:
            dma(T.yt[:, o:o + 64], R("YT", y, y + 64), 32768, [], [R("YT", y, y + 64)])
            dma(T.yc[:, o:o + 64], R("YC", y, y + 64), 32768, [], [R("YC", y, y + 64)])
        elif h == 1:
            o, y = o - 64, y - 64
            dmas([(T.yc[:, o:o + 128], R("YC", y, y + 128)), (T.yt[:, o:o + 128], R("YT", y, y + 128))], 131072 / GBW,
                 [], [R("YC", y, y + 128), R("YT", y, y + 128)])

    for v in range(V):
        last = {}
        for h in range(2):
            whole(v, h, last)
        spread(v)
        for h in range(2):
            opacity(v, h)
        for h in range(2):
            colour(v, h)
    return ops, nsent[0]


def schedule(ops):
    n = len(ops)
    kids = [[] for _ in range(n)]
    for i, o in enumerate(ops):
        for d in o["deps"] | o["ord"]:
            kids[d].append(i)

    def gap(a, b):
        if a not in ops[b]["deps"] or (ops[a]["e"] == "P" and ops[b]["e"] == "P"):
            return 0.0
        if ops[a]["e"] == ops[b]["e"] and ops[a]["sem"] is None:
            return GAP1
        return GAP2 + ops[a]["lat"]
    tail = [0.0] * n
    for i in range(n - 1, -1, -1):
        due = 0.0
        if ops[i]["tag"] is not None:
            kind, v, h = ops[i]["tag"]
            due = (V - 1 - v) * STAG + (WOFF - h * LAG if kind == "w" else FOFF - h * STAG / 4)
        tail[i] = ops[i]["cost"] + max([gap(i, k) + tail[k] for k in kids[i]] + [ops[i]["lat"], due])
    par = [sorted(o["deps"] | o["ord"]) for o in ops]
    key = [-x for x in tail]
    best = None
    for it in range(NIT):
        order, st, end = one_pass(ops, par, kids, gap, key)
        if best is None or end < best[1]:
            best = (order, end, st)
        back = one_pass(ops, kids, par, lambda a, b: gap(b, a), [-(st[i] + ops[i]["cost"]) for i in range(n)], False)[1]
        key = [-(back[i] + ops[i]["cost"]) for i in range(n)]
    for i in range(n):
        ops[i]["st"] = best[2][i]
    return polish(ops, best[0]), best[1]


def one_pass(ops, par, kids, gap, key, fwd=True):
    n = len(ops)
    pipe = 0.0
    left = [len(b) for b in par]
    rdy = [0.0] * n
    start = [0.0] * n
    pool = {}
    free = {}
    order = {}
    for e in "VAPGSX":
        pool[e], free[e], order[e] = [], 0.0, []
    for i in range(n):
        if left[i] == 0:
            pool[ops[i]["e"]].append(i)
    done = 0
    end = 0.0
    while done < n:
        t, e = min((max(free[e], min(rdy[i] for i in pool[e])), e) for e in pool if pool[e])
        i = None
        soon = 1e18
        for k in sorted(pool[e], key=lambda k: (key[k], k)):
            if rdy[k] <= t + 1.0 and t + ops[k]["cost"] <= soon + SLACK:
                i = k
                break
            if rdy[k] > t + 1.0:
                soon = min(soon, rdy[k])
        if i is None:
            free[e] = min(soon, t + 100.0)
            continue
        pool[e].remove(i)
        st = max(t, rdy[i])
        start[i] = st
        fin = st + ops[i]["cost"]
        if ops[i]["dm"] and fwd:
            pipe = max(st + 1500, pipe) + ops[i]["dm"]
            ops[i]["lat"] = max(pipe, fin + 1500) + 500 - fin
        free[e] = fin if e != "X" else 0.0
        order[e].append(i)
        end = max(end, fin + ops[i]["lat"])
        done += 1
        for k in kids[i]:
            rdy[k] = max(rdy[k], fin + gap(i, k))
            left[k] -= 1
            if left[k] == 0:
                pool[ops[k]["e"]].append(k)
    return order, start, end


def replay(ops, order, cost):
    n = len(ops)
    fin, lat, why = [None] * n, [o["lat"] for o in ops], [None] * n
    pos, free, cand = dict.fromkeys(order, 0), dict.fromkeys(order, 0.0), dict.fromkeys(order)
    pipe, end, last = 0.0, 0.0, 0
    for _ in range(n):
        bs, be = 1e30, None
        for e in order:
            if cand[e] is None and pos[e] < len(order[e]):
                i, s = order[e][pos[e]], free[e]
                why[i] = order[e][pos[e] - 1] if pos[e] and e != "X" else None
                for (d, gp) in ops[i]["in"]:
                    if fin[d] is None:
                        s = None
                        break
                    if fin[d] + gp + lat[d] > s:
                        s, why[i] = fin[d] + gp + lat[d], d
                cand[e] = s
            if cand[e] is not None and cand[e] < bs:
                bs, be = cand[e], e
        if be is None:
            return 1e30, None, None
        i = order[be][pos[be]]
        fin[i] = bs + cost[i]
        pos[be] += 1
        cand[be] = None
        if be != "X":
            free[be] = fin[i]
        if ops[i]["dm"]:
            pipe = max(bs + 1500, pipe) + ops[i]["dm"]
            lat[i] = max(pipe, fin[i] + 1500) + 500 - fin[i]
        if fin[i] + lat[i] > end:
            end, last = fin[i] + lat[i], i
    return end, why, last


def polish(ops, order):
    for o in ops:
        o["in"] = [(d, 0.0 if ops[d]["e"] == o["e"] == "P" else GAP1 if ops[d]["e"] == o["e"] and ops[d]["sem"] is None else GAP2)
                   for d in o["deps"]]
    costs = [[f * (o["cost"] + CYC * o["gn"] * (gk - GK)) if o["e"] in "VA" else
              30 + (o["cost"] - 30) * pe / PEC if o["e"] == "P" else o["cost"] for o in ops] for (f, gk, pe) in SPEEDS]
    runs = [replay(ops, order, c) for c in costs]
    base = [r[0] for r in runs]
    now, tried = float(len(runs)), set()
    for it in range(SWAPS):
        end, why, i = runs[it % len(runs)]
        pairs = []
        while why[i] is not None:
            a = why[i]
            if ops[a]["e"] == ops[i]["e"] and a not in ops[i]["deps"] and a not in ops[i]["ord"] and (a, i) not in tried:
                pairs.append((a, i))
            i = a
        if not pairs:
            tried.clear()
            continue
        a, b = pairs[(it * 7919) % len(pairs)]
        tried.add((a, b))
        q = order[ops[a]["e"]]
        p, old = q.index(a), list(q)
        d = (1, 2, 3, 5, 8)[it // 3 % 5]
        if it % 2:
            q.insert(max(p + 1 - d, 0), q.pop(p + 1))
        else:
            q.insert(p + d, q.pop(p))
        m = it % len(runs)
        new = [replay(ops, order, costs[m])]
        if new[0][0] < runs[m][0]:
            new = [new[0] if u == m else replay(ops, order, costs[u]) for u in range(len(runs))]
        score = sum(r[0] / z for r, z in zip(new, base))
        if len(new) == len(runs) and score < now:
            now, runs = score, new
        else:
            q[:] = old
    return order


ORDER = []


def rank_program(g, core, T, topo):
    rank = T.rank_of(core)
    if rank is None:
        return
    ops, nsent = build(T, rank, core, topo)
    if not ORDER:
        ORDER.append(schedule(ops)[0])
    order = ORDER[0]
    queue = {"V": g.vector, "A": g.scalar, "P": g.tensor, "G": g, "S": g.sync}
    mark = {}
    total = {}
    for e in "VAPG":
        c = 0
        for i in order[e]:
            if ops[i]["sem"] is None:
                c += 1
                mark[i] = ("s" + e, c)
        total["s" + e] = c
    for i, o in enumerate(ops):
        if o["ext"] is not None:
            mark[i] = o["ext"]
            total[o["ext"][0]] = o["ext"][1]
        elif o["sem"] is not None and o["sem"][0]:
            mark[i] = o["sem"]
            total[o["sem"][0]] = o["sem"][1]
    for e in "SAGPV":
        seen = {}
        for i in order[e]:
            need = {}
            for d in ops[i]["deps"]:
                if d in mark and not (e == "P" and ops[d]["e"] == "P"):
                    s, c = mark[d]
                    need[s] = max(need.get(s, 0), c)
            if e == "G" and i in mark and ops[i]["sem"] is None and mark[i][1] > 1:
                need["sG"] = mark[i][1] - 1
            for s in sorted(need):
                if seen.get(s, 0) < need[s]:
                    queue[e].wait_ge(T.sem[s], need[s])
                    seen[s] = need[s]
            r = ops[i]["fn"](g)
            if i in mark:
                r.then_inc(T.sem[mark[i][0]], 16 if ops[i]["sem"] is not None else 1)
    total["sent"] = nsent
    for s in sorted(total):
        g.wait_ge(T.sem[s], total[s])
